import numpy as np
import ml_dtypes


def mxq(x, axis, fmt="e4m3"):
    dtype, down = {"e4m3": (ml_dtypes.float8_e4m3fn, 7), "e5m2": (ml_dtypes.float8_e5m2, 14)}[fmt]
    v = np.moveaxis(np.asarray(x, np.float32).astype(ml_dtypes.bfloat16).astype(np.float64), axis, -1)
    blocks = v.reshape(v.shape[:-1] + (-1, 32))
    amax = np.abs(blocks).max(-1, keepdims=True)
    byte = np.maximum(np.where(amax > 0, np.frexp(amax)[1] - 1 + 127, 0) - down, 1)
    scale = np.exp2(byte - 127.0)
    codes = (blocks / scale).astype(np.float32).astype(dtype).astype(np.float64)
    return np.moveaxis((codes * scale).reshape(v.shape), -1, axis)


WIDE = False


def mx_kscale(k):
    if not WIDE:
        return np.ones(k)
    levels = np.array([24, -24, 12, -12, 0])
    if k % 512:
        return np.exp2(np.random.permutation(np.resize(levels, k // 32))).repeat(32)
    a = np.empty((k // 512, 16))
    for p in range(k // 512):
        a[p, :8] = np.random.permutation(np.resize(levels, 8))
        for g in range(8):
            far = levels[np.abs(levels - a[p, g]) >= 10]
            a[p, g + 8] = far[np.random.randint(len(far))]
    return np.exp2(a.ravel()).repeat(32)


def f64(x):
    return np.asarray(x).astype(np.float64)


def striped(idx):
    return np.tile(idx.reshape(-1, 16).T, (8, 1)).astype(np.uint16)


def unstriped(offs):
    return offs[:16].T.reshape(-1).astype(np.int64)


E2M1 = np.array([0.0, 0.5, 1.0, 1.5, 2.0, 3.0, 4.0, 6.0, -0.0, -0.5, -1.0, -1.5, -2.0, -3.0, -4.0, -6.0])


def pack_weight(w, fmt):
    k, n = w.shape
    w = f64(np.asarray(w, np.float32).astype(ml_dtypes.bfloat16)).reshape(k // 32, 32, n)
    amax = np.abs(w).max(1)
    if fmt == "e4m3":
        byte = np.frexp(amax)[1] - 1 + 127 - 7
    else:
        mant, ex = np.frexp(amax / 6.0)
        byte = np.where(mant > 0.5, ex, ex - 1) + 127
    byte = np.clip(np.where(amax > 0, byte, 1), 1, 254)
    scaled = (w * np.exp2(127.0 - byte)[:, None, :]).reshape(k, n).astype(np.float32)
    by_word = np.ascontiguousarray(scaled.reshape(k // 512, 128, 4, n).transpose(0, 1, 3, 2))
    if fmt == "e4m3":
        words = by_word.astype(ml_dtypes.float8_e4m3fn).view(np.uint8)
    else:
        c = by_word.astype(ml_dtypes.float4_e2m1fn).view(np.uint8) & 0xF
        words = (c[..., 0::2] | (c[..., 1::2] << 4)).reshape(k // 512, 128, 2 * n)
    return np.ascontiguousarray(words), np.ascontiguousarray(byte.astype(np.uint8).reshape(k // 512, 16, n))


def unpack_weight(words, scales, fmt):
    g, _, n = scales.shape
    words = np.ascontiguousarray(words).reshape(g, 128, n, -1)
    if fmt == "e4m3":
        vals = words.view(ml_dtypes.float8_e4m3fn).astype(np.float64)
    else:
        nib = np.empty((g, 128, n, 4), np.uint8)
        nib[..., 0::2] = words & 0xF
        nib[..., 1::2] = words >> 4
        vals = E2M1[nib]
    vals = vals * np.repeat(np.exp2(scales.astype(np.float64) - 127.0), 8, axis=1)[..., None]
    return vals.transpose(0, 1, 3, 2).reshape(g * 512, n)


def pack_table4(v):
    words, scales = pack_weight(v, "e2m1")
    g, t = words.shape[0] // 2, v.shape[1]
    return np.ascontiguousarray(words.reshape(g, 2, 128, t, 2).transpose(0, 2, 3, 1, 4).reshape(g, 128, t, 4)), scales


def unpack_table4(words, scales):
    g, _, t, _ = words.shape
    return unpack_weight(words.reshape(g, 128, t, 2, 2).transpose(0, 3, 1, 2, 4).reshape(2 * g, 128, 2 * t), scales, "e2m1")


def planes(y):
    n, m = y.shape
    v = y.astype(np.float32).astype(ml_dtypes.bfloat16).astype(np.float64).reshape(n // 32, 32, m)
    top = np.abs(v).max(1)
    byte = np.clip(np.where(top > 0, np.frexp(top)[1] - 1 + 127 - 7, 1), 1, 254)
    codes = (v * np.exp2(127.0 - byte)[:, None, :]).reshape(n, m).astype(np.float32).astype(ml_dtypes.float8_e4m3fn).view(np.uint8)
    words = codes.reshape(n // 512, 128, 4, m).transpose(0, 1, 3, 2)
    return np.ascontiguousarray(words), np.ascontiguousarray(byte.astype(np.uint8).reshape(n // 512, 16, m))


def silu(f):
    return f / (1.0 + np.exp(-np.maximum(f, -700.0)))


def sigm(f):
    return 1.0 / (1.0 + np.exp(-np.maximum(f, -700.0)))


K, L, N, T, J = 1024, 512, 512, 2048, 1024


def setup_inputs():
    n = np.random.standard_normal
    s = mx_kscale(K)[:, None]
    s2 = mx_kscale(L)[:, None]
    p_tab = pack_table4(n((K, T)) * s)
    p_tab2 = pack_weight(n((L, T)) * s2, "e4m3")
    p_zv = pack_weight(n((K, N)) / np.sqrt(K) / s, "e2m1")
    p_zt = pack_weight(n((L, N)) / np.sqrt(L) / s2, "e2m1")
    p_wv = pack_weight(n((K, N)) / np.sqrt(K) / s, "e2m1")
    return {
        "tab_words": p_tab[0],
        "tab_scales": p_tab[1],
        "tab2_words": p_tab2[0],
        "tab2_scales": p_tab2[1],
        "zv_words": p_zv[0],
        "zv_scales": p_zv[1],
        "zt_words": p_zt[0],
        "zt_scales": p_zt[1],
        "b": (0.3 * n(N)).astype(np.float32),
        "wv_words": p_wv[0],
        "wv_scales": p_wv[1],
        "wt": (n((L, N)) / np.sqrt(L) / s2).astype(np.float32),
        "wgo": np.tile(np.random.uniform(0.5, 2.0, J), (128, 1)).astype(np.float32),
        "offs": striped(np.random.permutation(T)[:J]),
        "offs2": striped(np.random.permutation(T)[:J]),
    }


def reference(tab_words, tab_scales, tab2_words, tab2_scales, zv_words, zv_scales, zt_words, zt_scales, b, wv_words, wv_scales, wt, wgo, offs, offs2):
    idx = unstriped(offs)
    idx2 = unstriped(offs2)
    tab_ = unpack_table4(tab_words, tab_scales)[:, idx]
    tab2_ = unpack_weight(tab2_words, tab2_scales, "e4m3")[:, idx2]
    zv_ = unpack_weight(zv_words, zv_scales, "e2m1")
    zt_ = unpack_weight(zt_words, zt_scales, "e2m1")
    z = zv_.T @ tab_ + zt_.T @ tab2_
    gate = sigm(z + f64(b)[:, None])
    wv_ = unpack_weight(wv_words, wv_scales, "e2m1")
    wt_ = mxq(f64(wt), 0, "e4m3")
    hv = wv_.T @ tab_
    ht = wt_.T @ tab2_
    av = silu(hv)
    at = silu(ht)
    out = np.zeros((N, T))
    out[:, idx] = f64(wgo)[0] * (at + gate * (av - at))
    return (out,) + planes(out)

@@ -1,0 +1,204 @@
+from contextlib import ExitStack
+
+import concourse.mybir as mybir
+
+K, L, N, T, J = 1024, 512, 512, 2048, 1024
+FLOPS = 2 * J * N * (2 * K + 2 * L)
+
+F32 = mybir.dt.float32
+BF16 = mybir.dt.bfloat16
+I32 = mybir.dt.int32
+U32 = mybir.dt.uint32
+U16 = mybir.dt.uint16
+U8 = mybir.dt.uint8
+FP8X4 = mybir.dt.float8_e4m3fn_x4
+FP4X4 = mybir.dt.float4_e2m1fn_x4
+ACT = mybir.ActivationFunctionType
+ALU = mybir.AluOpType
+
+P = 128
+PACK = 4
+HALF = 512
+HALVES = J // HALF
+CHUNK = 512
+CHUNKS = T // CHUNK
+
+
+def tile_list_gmu_silu_scatP_kernel(
+    tc, tab_words, tab_scales, tab2_words, tab2_scales, zv_words, zv_scales, zt_words, zt_scales,
+    b, wv_words, wv_scales, wt, wgo, offs, offs2, out_0, out_1, out_2,
+):
+    nc = tc.nc
+    with ExitStack() as ctx:
+        keep = ctx.enter_context(tc.tile_pool(name="keep", bufs=1))
+        work = ctx.enter_context(tc.tile_pool(name="work", bufs=4))
+        acts = ctx.enter_context(tc.tile_pool(name="acts", bufs=PACK * HALVES))
+        psum = ctx.enter_context(tc.psum_pool(name="psum", bufs=2))
+
+        def held(shape, dtype, name, tag=""):
+            return keep.tile(shape, dtype, name=name, tag=tag or name, align_bytes=64)
+
+        list1 = held([P, J // 16], U16, "list1")
+        list2 = held([P, J // 16], U16, "list2")
+        tab_w = held([P, T], I32, "tab_w")
+        tab_s = held([P, T], U8, "tab_s")
+        tab2_w = held([P, T], I32, "tab2_w")
+        tab2_s = held([P, T], U8, "tab2_s")
+        w_scales_raw = held([P, 5, N], U8, "w_scales_raw")
+        shifted = [held([P, HALF], U8, "shifted%d" % h) for h in range(HALVES)]
+
+        nc.vector.memset(tab_s[:].bitcast(I32), 0)
+        nc.vector.memset(tab2_s[:].bitcast(I32), 0)
+        nc.gpsimd.memset(w_scales_raw[:].bitcast(I32), 0)
+        for h in range(HALVES):
+            nc.vector.memset(shifted[h][:].bitcast(I32), 0)
+
+        nc.sync.dma_start(list1[:], offs)
+        nc.sync.dma_start(tab_w[:], tab_words[0].rearrange("p t b -> p (t b)").bitcast(I32))
+        for q in range(4):
+            nc.sync.dma_start(tab_s[32 * q : 32 * q + 8, :].bitcast(I32), tab_scales[:, 4 * q : 4 * q + 4, :].bitcast(I32))
+        nc.sync.dma_start(list2[:], offs2)
+        nc.sync.dma_start(tab2_w[:], tab2_words[0].rearrange("p t b -> p (t b)").bitcast(I32))
+        for q in range(4):
+            nc.sync.dma_start(tab2_s[32 * q : 32 * q + 4, :].bitcast(I32), tab2_scales[0, 4 * q : 4 * q + 4, :].bitcast(I32))
+
+        wv_raw = held([P, 2, 2 * N], U8, "wv_raw")
+        zv_raw = held([P, 2, 2 * N], U8, "zv_raw")
+        zt_raw = held([P, 1, 2 * N], U8, "zt_raw")
+        nc.sync.dma_start(wv_raw[:].bitcast(I32), wv_words.rearrange("a p c -> p a c").bitcast(I32))
+        nc.sync.dma_start(zv_raw[:].bitcast(I32), zv_words.rearrange("a p c -> p a c").bitcast(I32))
+        nc.sync.dma_start(zt_raw[:].bitcast(I32), zt_words.rearrange("a p c -> p a c").bitcast(I32))
+        wt_raw = [held([P, PACK, N // 2], F32, "wt_raw%d" % u) for u in range(2)]
+        for u in range(2):
+            nc.sync.dma_start(wt_raw[u][:], wt.rearrange("(p i) n -> p i n", i=PACK)[:, :, u * N // 2 : (u + 1) * N // 2])
+        for first, scales, queue in ((0, wv_scales, nc.sync), (2, zv_scales, nc.gpsimd), (4, zt_scales, nc.sync)):
+            passes = scales.shape[0]
+            for q in range(4):
+                queue.dma_start(
+                    w_scales_raw[32 * q : 32 * q + 4, first : first + passes, :].bitcast(I32),
+                    scales[:, 4 * q : 4 * q + 4, :].rearrange("a r n -> r a n").bitcast(I32),
+                )
+        bias = held([P, PACK], F32, "bias")
+        nc.sync.dma_start(bias[:], b.rearrange("(p t) -> p t", t=PACK))
+        weight = held([P, J], F32, "weight")
+        nc.sync.dma_start(weight[:], wgo)
+
+        pages = [held([P, T], F32, "page%d" % t) for t in range(PACK)]
+        for t in range(PACK):
+            if t < 2:
+                nc.vector.memset(pages[t][:].bitcast(I32), 0)
+            else:
+                for c in range(CHUNKS):
+                    nc.gpsimd.memset(pages[t][:, c * CHUNK : (c + 1) * CHUNK], 0.0)
+
+        half_bias = held([P, PACK], F32, "half_bias")
+        nc.scalar.mul(half_bias[:], bias[:], 0.5)
+        wt_bf = held([P, PACK, P, PACK], BF16, "wt_bf")
+        for u in range(2):
+            nc.scalar.copy(wt_bf[:, :, u * P // 2 : (u + 1) * P // 2, :], wt_raw[u][:].rearrange("p i (m t) -> p t m i", t=PACK))
+        wt_codes = held([P, N], U32, "wt_codes")
+        wt_scales = held([P, N], U8, "wt_scales")
+
+        picked = []
+
+        def gather(h, tags):
+            cols = slice(h * HALF // 16, (h + 1) * HALF // 16)
+            v_scales = held([P, HALF], U8, "v_scales%d" % h, tags[0])
+            nc.vector.tensor_copy(v_scales[:], tab_s[:].indirect(list1[:, cols]))
+            nc.sync.dma_start(shifted[h][0:100, :].bitcast(I32), v_scales[4:104, :].bitcast(I32))
+            pairs = held([P, HALF], U32, "pairs%d" % h, tags[1])
+            nc.vector.tensor_copy(pairs[:], tab_w[:].bitcast(U32).indirect(list1[:, cols]))
+            v2_scales = held([P, HALF], U8, "v2_scales%d" % h, tags[2])
+            nc.vector.tensor_copy(v2_scales[:], tab2_s[:].indirect(list2[:, cols]))
+            v_codes = held([P, 2, 2 * HALF], U8, "v_codes%d" % h)
+            nc.vector.tensor_copy(v_codes[:].bitcast(U16), pairs[:].bitcast(U16).rearrange("p (j a) -> p a j", a=2))
+            v2_codes = held([P, HALF], U32, "v2_codes%d" % h, tags[3])
+            nc.vector.tensor_copy(v2_codes[:], tab2_w[:].bitcast(U32).indirect(list2[:, cols]))
+            picked.append((v_codes, (v_scales, shifted[h]), v2_codes, v2_scales))
+
+        gather(0, ("", "", "", ""))
+
+        dealt = []
+        for name, raw, passes in (("wv_codes", wv_raw, 2), ("zv_codes", zv_raw, 2), ("zt_codes", zt_raw, 1)):
+            codes = held([P, passes, PACK, 2 * P], U8, name)
+            nc.vector.tensor_copy(codes[:].bitcast(U16), raw[:].bitcast(U16).rearrange("p a (m t) -> p a t m", t=PACK))
+            dealt.append(codes)
+        wv_codes, zv_codes, zt_codes = dealt
+        w_scales = held([P, 5, PACK, P], U8, "w_scales")
+        nc.vector.tensor_copy(w_scales[:], w_scales_raw[:].rearrange("p a (m t) -> p a t m", t=PACK))
+        nc.vector.quantize_mx(out=wt_codes[:].bitcast(FP8X4), scales=wt_scales[:], in_=wt_bf[:].rearrange("p t m i -> p (t m i)"))
+
+        gather(1, ("w_scales_raw", "wv_raw", "zt_raw", "zv_raw"))
+
+        woven = [held([P, CHUNK, PACK], BF16, "woven%d" % c) for c in range(CHUNKS)]
+        y_codes = [held([P, CHUNK], U32, "y_codes%d" % c) for c in range(CHUNKS)]
+        y_scales = held([P, T], U8, "y_scales")
+        out_rows = out_0.rearrange("(p t) c -> p t c", t=PACK)
+        out_words = out_1[0].rearrange("p t b -> p (t b)").bitcast(I32)
+
+        made = {}
+        for t in range(PACK):
+            for h in range(HALVES):
+                v_codes, v_scales, v2_codes, v2_scales = picked[h]
+                hv = psum.tile([P, HALF], F32, name="hv")
+                for a in range(2):
+                    nc.tensor.matmul_mx(
+                        out=hv[:], lhsT=wv_codes[:, a, t, :].bitcast(FP4X4), lhsT_scale=w_scales[:, a, t, :],
+                        rhs=v_codes[:, a, :].bitcast(FP4X4), rhs_scale=v_scales[a][:], start=(a == 0), stop=(a == 1),
+                    )
+                ht = psum.tile([P, HALF], F32, name="ht")
+                nc.tensor.matmul_mx(
+                    out=ht[:], lhsT=wt_codes[:, t * P : (t + 1) * P].bitcast(FP8X4), lhsT_scale=wt_scales[:, t * P : (t + 1) * P],
+                    rhs=v2_codes[:].bitcast(FP8X4), rhs_scale=v2_scales[:], start=True, stop=True,
+                )
+                z = psum.tile([P, HALF], F32, name="z")
+                for a in range(2):
+                    nc.tensor.matmul_mx(
+                        out=z[:], lhsT=zv_codes[:, a, t, :].bitcast(FP4X4), lhsT_scale=w_scales[:, 2 + a, t, :],
+                        rhs=v_codes[:, a, :].bitcast(FP4X4), rhs_scale=v_scales[a][:], start=(a == 0), stop=False,
+                    )
+                nc.tensor.matmul_mx(
+                    out=z[:], lhsT=zt_codes[:, 0, t, :].bitcast(FP4X4), lhsT_scale=w_scales[:, 4, t, :],
+                    rhs=v2_codes[:].bitcast(FP8X4), rhs_scale=v2_scales[:], start=False, stop=True,
+                )
+                av = acts.tile([P, HALF], F32, name="av")
+                nc.scalar.activation(av[:], hv[:], ACT.Silu)
+                at = acts.tile([P, HALF], F32, name="at")
+                nc.scalar.activation(at[:], ht[:], ACT.Silu)
+                th = acts.tile([P, HALF], F32, name="th")
+                nc.scalar.activation(th[:], z[:], ACT.Tanh, bias=half_bias[:, t : t + 1], scale=0.5)
+                made[t, h] = (av, at, th)
+
+        for t in range(PACK):
+            diff = [work.tile([P, HALF], F32, name="diff") for h in range(HALVES)]
+            twice = [work.tile([P, HALF], F32, name="twice") for h in range(HALVES)]
+            mixed = [work.tile([P, HALF], F32, name="mixed") for h in range(HALVES)]
+            for h in range(HALVES):
+                nc.vector.tensor_tensor(diff[h][:], made[t, h][0][:], made[t, h][1][:], ALU.subtract)
+            for h in range(HALVES):
+                nc.vector.scalar_tensor_tensor(twice[h][:], made[t, h][2][:], 1.0, diff[h][:], ALU.add, ALU.mult)
+            for h in range(HALVES):
+                nc.vector.scalar_tensor_tensor(mixed[h][:], twice[h][:], 0.5, made[t, h][1][:], ALU.mult, ALU.add)
+            for h in range(HALVES):
+                nc.vector.tensor_tensor(
+                    pages[t][:].indirect(list1[:, h * HALF // 16 : (h + 1) * HALF // 16]),
+                    mixed[h][:], weight[:, h * HALF : (h + 1) * HALF], ALU.mult,
+                )
+            nc.sync.dma_start(out_rows[:, t, :], pages[t][:])
+            for c in range(CHUNKS):
+                src = pages[t][:, c * CHUNK : (c + 1) * CHUNK]
+                on_vector = c % 2 == 0
+                if t == PACK - 1 and on_vector:
+                    nc.vector.tensor_copy(woven[c][:, :, t], src)
+                elif t == PACK - 2 and on_vector:
+                    nc.scalar.copy(woven[c][:, :, t : t + 2], src.unsqueeze(2).to_broadcast([P, CHUNK, 2]))
+                else:
+                    nc.scalar.copy(woven[c][:, :, t], src)
+        for c in range(CHUNKS):
+            nc.vector.quantize_mx(
+                out=y_codes[c][:].bitcast(FP8X4), scales=y_scales[:, c * CHUNK : (c + 1) * CHUNK],
+                in_=woven[c][:].rearrange("p c t -> p (c t)"),
+            )
+            nc.sync.dma_start(out_words[:, c * CHUNK : (c + 1) * CHUNK], y_codes[c][:].bitcast(I32))
+        for q in range(4):
+            nc.scalar.dma_start(out_2[0, 4 * q : 4 * q + 4, :].bitcast(I32), y_scales[32 * q : 32 * q + 4, :].bitcast(I32))

@@ -22,6 +22,7 @@ HALF = 512
 HALVES = J // HALF
 CHUNK = 512
 CHUNKS = T // CHUNK
+PAGES = 2
 
 
 def tile_list_gmu_silu_scatP_kernel(
@@ -31,7 +32,7 @@ def tile_list_gmu_silu_scatP_kernel(
     nc = tc.nc
     with ExitStack() as ctx:
         keep = ctx.enter_context(tc.tile_pool(name="keep", bufs=1))
-        work = ctx.enter_context(tc.tile_pool(name="work", bufs=4))
+        work = ctx.enter_context(tc.tile_pool(name="work", bufs=3))
         acts = ctx.enter_context(tc.tile_pool(name="acts", bufs=PACK * HALVES))
         psum = ctx.enter_context(tc.psum_pool(name="psum", bufs=2))
 
@@ -40,95 +41,96 @@ def tile_list_gmu_silu_scatP_kernel(
 
         list1 = held([P, J // 16], U16, "list1")
         list2 = held([P, J // 16], U16, "list2")
-        tab_w = held([P, T], I32, "tab_w")
         tab_s = held([P, T], U8, "tab_s")
-        tab2_w = held([P, T], I32, "tab2_w")
         tab2_s = held([P, T], U8, "tab2_s")
-        w_scales_raw = held([P, 5, N], U8, "w_scales_raw")
-        shifted = [held([P, HALF], U8, "shifted%d" % h) for h in range(HALVES)]
-
+        w_scales_raw = held([P, 5 * N], U8, "w_scales_raw")
+        shifted = held([P, J], U8, "shifted")
         nc.vector.memset(tab_s[:].bitcast(I32), 0)
         nc.vector.memset(tab2_s[:].bitcast(I32), 0)
-        nc.gpsimd.memset(w_scales_raw[:].bitcast(I32), 0)
-        for h in range(HALVES):
-            nc.vector.memset(shifted[h][:].bitcast(I32), 0)
+        nc.vector.memset(w_scales_raw[:].bitcast(I32), 0)
+        nc.vector.memset(shifted[:].bitcast(I32), 0)
+        pages = [held([P, T], F32, "page0")]
+        nc.vector.memset(pages[0][:].bitcast(I32), 0)
 
         nc.sync.dma_start(list1[:], offs)
-        nc.sync.dma_start(tab_w[:], tab_words[0].rearrange("p t b -> p (t b)").bitcast(I32))
         for q in range(4):
             nc.sync.dma_start(tab_s[32 * q : 32 * q + 8, :].bitcast(I32), tab_scales[:, 4 * q : 4 * q + 4, :].bitcast(I32))
         nc.sync.dma_start(list2[:], offs2)
-        nc.sync.dma_start(tab2_w[:], tab2_words[0].rearrange("p t b -> p (t b)").bitcast(I32))
+        tab_w = held([P, T], I32, "tab_w")
+        nc.sync.dma_start(tab_w[:], tab_words[0].rearrange("p t b -> p (t b)").bitcast(I32))
         for q in range(4):
             nc.sync.dma_start(tab2_s[32 * q : 32 * q + 4, :].bitcast(I32), tab2_scales[0, 4 * q : 4 * q + 4, :].bitcast(I32))
-
-        wv_raw = held([P, 2, 2 * N], U8, "wv_raw")
-        zv_raw = held([P, 2, 2 * N], U8, "zv_raw")
-        zt_raw = held([P, 1, 2 * N], U8, "zt_raw")
-        nc.sync.dma_start(wv_raw[:].bitcast(I32), wv_words.rearrange("a p c -> p a c").bitcast(I32))
-        nc.sync.dma_start(zv_raw[:].bitcast(I32), zv_words.rearrange("a p c -> p a c").bitcast(I32))
-        nc.sync.dma_start(zt_raw[:].bitcast(I32), zt_words.rearrange("a p c -> p a c").bitcast(I32))
-        wt_raw = [held([P, PACK, N // 2], F32, "wt_raw%d" % u) for u in range(2)]
-        for u in range(2):
-            nc.sync.dma_start(wt_raw[u][:], wt.rearrange("(p i) n -> p i n", i=PACK)[:, :, u * N // 2 : (u + 1) * N // 2])
-        for first, scales, queue in ((0, wv_scales, nc.sync), (2, zv_scales, nc.gpsimd), (4, zt_scales, nc.sync)):
+        for first, scales in ((0, wv_scales), (2, zv_scales), (4, zt_scales)):
             passes = scales.shape[0]
-            for q in range(4):
-                queue.dma_start(
-                    w_scales_raw[32 * q : 32 * q + 4, first : first + passes, :].bitcast(I32),
-                    scales[:, 4 * q : 4 * q + 4, :].rearrange("a r n -> r a n").bitcast(I32),
-                )
+            nc.sync.dma_start(
+                w_scales_raw[0:P:8, first * N : (first + passes) * N].bitcast(I32).rearrange("q (a n) -> q a n", a=passes),
+                scales.rearrange("a q n -> q a n").bitcast(I32),
+            )
+        raws = []
+        for name, words in (("wv_raw", wv_words), ("zv_raw", zv_words), ("zt_raw", zt_words)):
+            raw = held([P, words.shape[0], 2 * N], U8, name)
+            nc.sync.dma_start(raw[:].bitcast(I32), words.rearrange("a p c -> p a c").bitcast(I32))
+            raws.append(raw)
         bias = held([P, PACK], F32, "bias")
         nc.sync.dma_start(bias[:], b.rearrange("(p t) -> p t", t=PACK))
-        weight = held([P, J], F32, "weight")
-        nc.sync.dma_start(weight[:], wgo)
-
-        pages = [held([P, T], F32, "page%d" % t) for t in range(PACK)]
-        for t in range(PACK):
-            if t < 2:
-                nc.vector.memset(pages[t][:].bitcast(I32), 0)
-            else:
-                for c in range(CHUNKS):
-                    nc.gpsimd.memset(pages[t][:, c * CHUNK : (c + 1) * CHUNK], 0.0)
-
         half_bias = held([P, PACK], F32, "half_bias")
         nc.scalar.mul(half_bias[:], bias[:], 0.5)
+
+        v_scales = held([P, J], U8, "v_scales")
+        nc.vector.tensor_copy(v_scales[:], tab_s[:].indirect(list1[:]))
+        nc.sync.dma_start(shifted[0:100, :].bitcast(I32), v_scales[4:104, :].bitcast(I32))
+        wt_raw = held([P, PACK, N], F32, "wt_raw", "tab_s")
+        nc.sync.dma_start(wt_raw[:], wt.rearrange("(p i) n -> p i n", i=PACK))
+        w_scales = held([P, PACK, 5 * P], U8, "w_scales")
+        nc.vector.tensor_copy(w_scales[:], w_scales_raw[:].rearrange("p (m t) -> p t m", t=PACK))
+        flat_scales = w_scales[:].rearrange("p t m -> p (t m)").bitcast(I32)
+        for r in range(1, 4):
+            nc.sync.dma_start(flat_scales[r:P:32, :], flat_scales[8 * r : P : 32, :])
+        tab2_w = held([P, T], I32, "tab2_w", "w_scales_raw")
+        nc.sync.dma_start(tab2_w[:], tab2_words[0].rearrange("p t b -> p (t b)").bitcast(I32))
+        v2_scales = held([P, J], U8, "v2_scales")
+        nc.vector.tensor_copy(v2_scales[:], tab2_s[:].indirect(list2[:]))
+        weight = held([P, J], F32, "weight", "tab2_s")
+        nc.sync.dma_start(weight[:], wgo)
+
         wt_bf = held([P, PACK, P, PACK], BF16, "wt_bf")
-        for u in range(2):
-            nc.scalar.copy(wt_bf[:, :, u * P // 2 : (u + 1) * P // 2, :], wt_raw[u][:].rearrange("p i (m t) -> p t m i", t=PACK))
+        nc.scalar.copy(wt_bf[:].rearrange("p t m i -> p m t i"), wt_raw[:].rearrange("p i (m t) -> p m t i", t=PACK))
         wt_codes = held([P, N], U32, "wt_codes")
         wt_scales = held([P, N], U8, "wt_scales")
 
-        picked = []
+        def gather_v(h, tag):
+            pairs = held([P, HALF], U32, "pairs%d" % h, tag)
+            nc.vector.tensor_copy(pairs[:], tab_w[:].bitcast(U32).indirect(list1[:, h * HALF // 16 : (h + 1) * HALF // 16]))
+            return pairs
 
-        def gather(h, tags):
-            cols = slice(h * HALF // 16, (h + 1) * HALF // 16)
-            v_scales = held([P, HALF], U8, "v_scales%d" % h, tags[0])
-            nc.vector.tensor_copy(v_scales[:], tab_s[:].indirect(list1[:, cols]))
-            nc.sync.dma_start(shifted[h][0:100, :].bitcast(I32), v_scales[4:104, :].bitcast(I32))
-            pairs = held([P, HALF], U32, "pairs%d" % h, tags[1])
-            nc.vector.tensor_copy(pairs[:], tab_w[:].bitcast(U32).indirect(list1[:, cols]))
-            v2_scales = held([P, HALF], U8, "v2_scales%d" % h, tags[2])
-            nc.vector.tensor_copy(v2_scales[:], tab2_s[:].indirect(list2[:, cols]))
-            v_codes = held([P, 2, 2 * HALF], U8, "v_codes%d" % h)
-            nc.vector.tensor_copy(v_codes[:].bitcast(U16), pairs[:].bitcast(U16).rearrange("p (j a) -> p a j", a=2))
-            v2_codes = held([P, HALF], U32, "v2_codes%d" % h, tags[3])
-            nc.vector.tensor_copy(v2_codes[:], tab2_w[:].bitcast(U32).indirect(list2[:, cols]))
-            picked.append((v_codes, (v_scales, shifted[h]), v2_codes, v2_scales))
+        def part_v(h, pairs):
+            codes = held([P, 2, 2 * HALF], U8, "v_codes%d" % h)
+            nc.vector.tensor_copy(codes[:].bitcast(U16), pairs[:].bitcast(U16).rearrange("p (j a) -> p a j", a=2))
+            return codes
 
-        gather(0, ("", "", "", ""))
+        def gather_v2(h, tag):
+            codes = held([P, HALF], U32, "v2_codes%d" % h, tag)
+            nc.vector.tensor_copy(codes[:], tab2_w[:].bitcast(U32).indirect(list2[:, h * HALF // 16 : (h + 1) * HALF // 16]))
+            return codes
 
-        dealt = []
-        for name, raw, passes in (("wv_codes", wv_raw, 2), ("zv_codes", zv_raw, 2), ("zt_codes", zt_raw, 1)):
-            codes = held([P, passes, PACK, 2 * P], U8, name)
-            nc.vector.tensor_copy(codes[:].bitcast(U16), raw[:].bitcast(U16).rearrange("p a (m t) -> p a t m", t=PACK))
-            dealt.append(codes)
-        wv_codes, zv_codes, zt_codes = dealt
-        w_scales = held([P, 5, PACK, P], U8, "w_scales")
-        nc.vector.tensor_copy(w_scales[:], w_scales_raw[:].rearrange("p a (m t) -> p a t m", t=PACK))
+        def deal(name, raw):
+            codes = held([P, raw.shape[1], PACK, 2 * P], U8, name)
+            nc.vector.tensor_copy(codes[:].bitcast(U16).rearrange("p a t m -> p t a m"), raw[:].bitcast(U16).rearrange("p a (m t) -> p t a m", t=PACK))
+            return codes
+
+        pairs0 = gather_v(0, "")
+        wv_codes = deal("wv_codes", raws[0])
+        v_codes = [part_v(0, pairs0)]
+        zv_codes = deal("zv_codes", raws[1])
+        zt_codes = deal("zt_codes", raws[2])
+        v2_codes = [gather_v2(0, "")]
         nc.vector.quantize_mx(out=wt_codes[:].bitcast(FP8X4), scales=wt_scales[:], in_=wt_bf[:].rearrange("p t m i -> p (t m i)"))
-
-        gather(1, ("w_scales_raw", "wv_raw", "zt_raw", "zv_raw"))
+        pairs1 = gather_v(1, "wt_bf")
+        v2_codes.append(gather_v2(1, "zt_raw"))
+        v_codes.append(part_v(1, pairs1))
+        for i in range(1, PAGES):
+            pages.append(held([P, T], F32, "page%d" % i, ("tab_w", "tab_s")[i - 1]))
+            nc.vector.memset(pages[i][:].bitcast(I32), 0)
 
         woven = [held([P, CHUNK, PACK], BF16, "woven%d" % c) for c in range(CHUNKS)]
         y_codes = [held([P, CHUNK], U32, "y_codes%d" % c) for c in range(CHUNKS)]
@@ -136,30 +138,31 @@ def tile_list_gmu_silu_scatP_kernel(
         out_rows = out_0.rearrange("(p t) c -> p t c", t=PACK)
         out_words = out_1[0].rearrange("p t b -> p (t b)").bitcast(I32)
 
-        made = {}
+        made = []
         for t in range(PACK):
             for h in range(HALVES):
-                v_codes, v_scales, v2_codes, v2_scales = picked[h]
+                cols = slice(h * HALF, (h + 1) * HALF)
+                planes = (v_scales[:, cols], shifted[:, cols])
                 hv = psum.tile([P, HALF], F32, name="hv")
                 for a in range(2):
                     nc.tensor.matmul_mx(
-                        out=hv[:], lhsT=wv_codes[:, a, t, :].bitcast(FP4X4), lhsT_scale=w_scales[:, a, t, :],
-                        rhs=v_codes[:, a, :].bitcast(FP4X4), rhs_scale=v_scales[a][:], start=(a == 0), stop=(a == 1),
+                        out=hv[:], lhsT=wv_codes[:, a, t, :].bitcast(FP4X4), lhsT_scale=w_scales[:, t, a * P : (a + 1) * P],
+                        rhs=v_codes[h][:, a, :].bitcast(FP4X4), rhs_scale=planes[a], start=(a == 0), stop=(a == 1),
                     )
                 ht = psum.tile([P, HALF], F32, name="ht")
                 nc.tensor.matmul_mx(
                     out=ht[:], lhsT=wt_codes[:, t * P : (t + 1) * P].bitcast(FP8X4), lhsT_scale=wt_scales[:, t * P : (t + 1) * P],
-                    rhs=v2_codes[:].bitcast(FP8X4), rhs_scale=v2_scales[:], start=True, stop=True,
+                    rhs=v2_codes[h][:].bitcast(FP8X4), rhs_scale=v2_scales[:, cols], start=True, stop=True,
                 )
                 z = psum.tile([P, HALF], F32, name="z")
                 for a in range(2):
                     nc.tensor.matmul_mx(
-                        out=z[:], lhsT=zv_codes[:, a, t, :].bitcast(FP4X4), lhsT_scale=w_scales[:, 2 + a, t, :],
-                        rhs=v_codes[:, a, :].bitcast(FP4X4), rhs_scale=v_scales[a][:], start=(a == 0), stop=False,
+                        out=z[:], lhsT=zv_codes[:, a, t, :].bitcast(FP4X4), lhsT_scale=w_scales[:, t, (2 + a) * P : (3 + a) * P],
+                        rhs=v_codes[h][:, a, :].bitcast(FP4X4), rhs_scale=planes[a], start=(a == 0), stop=False,
                     )
                 nc.tensor.matmul_mx(
-                    out=z[:], lhsT=zt_codes[:, 0, t, :].bitcast(FP4X4), lhsT_scale=w_scales[:, 4, t, :],
-                    rhs=v2_codes[:].bitcast(FP8X4), rhs_scale=v2_scales[:], start=False, stop=True,
+                    out=z[:], lhsT=zt_codes[:, 0, t, :].bitcast(FP4X4), lhsT_scale=w_scales[:, t, 4 * P : 5 * P],
+                    rhs=v2_codes[h][:].bitcast(FP8X4), rhs_scale=v2_scales[:, cols], start=False, stop=True,
                 )
                 av = acts.tile([P, HALF], F32, name="av")
                 nc.scalar.activation(av[:], hv[:], ACT.Silu)
@@ -167,26 +170,13 @@ def tile_list_gmu_silu_scatP_kernel(
                 nc.scalar.activation(at[:], ht[:], ACT.Silu)
                 th = acts.tile([P, HALF], F32, name="th")
                 nc.scalar.activation(th[:], z[:], ACT.Tanh, bias=half_bias[:, t : t + 1], scale=0.5)
-                made[t, h] = (av, at, th)
+                made.append((av, at, th))
 
-        for t in range(PACK):
-            diff = [work.tile([P, HALF], F32, name="diff") for h in range(HALVES)]
-            twice = [work.tile([P, HALF], F32, name="twice") for h in range(HALVES)]
-            mixed = [work.tile([P, HALF], F32, name="mixed") for h in range(HALVES)]
-            for h in range(HALVES):
-                nc.vector.tensor_tensor(diff[h][:], made[t, h][0][:], made[t, h][1][:], ALU.subtract)
-            for h in range(HALVES):
-                nc.vector.scalar_tensor_tensor(twice[h][:], made[t, h][2][:], 1.0, diff[h][:], ALU.add, ALU.mult)
-            for h in range(HALVES):
-                nc.vector.scalar_tensor_tensor(mixed[h][:], twice[h][:], 0.5, made[t, h][1][:], ALU.mult, ALU.add)
-            for h in range(HALVES):
-                nc.vector.tensor_tensor(
-                    pages[t][:].indirect(list1[:, h * HALF // 16 : (h + 1) * HALF // 16]),
-                    mixed[h][:], weight[:, h * HALF : (h + 1) * HALF], ALU.mult,
-                )
-            nc.sync.dma_start(out_rows[:, t, :], pages[t][:])
+        def finish(t):
+            page = pages[t % PAGES]
+            nc.sync.dma_start(out_rows[:, t, :], page[:])
             for c in range(CHUNKS):
-                src = pages[t][:, c * CHUNK : (c + 1) * CHUNK]
+                src = page[:, c * CHUNK : (c + 1) * CHUNK]
                 on_vector = c % 2 == 0
                 if t == PACK - 1 and on_vector:
                     nc.vector.tensor_copy(woven[c][:, :, t], src)
@@ -194,6 +184,49 @@ def tile_list_gmu_silu_scatP_kernel(
                     nc.scalar.copy(woven[c][:, :, t : t + 2], src.unsqueeze(2).to_broadcast([P, CHUNK, 2]))
                 else:
                     nc.scalar.copy(woven[c][:, :, t], src)
+
+        units = PACK * HALVES
+        diff, twice, mixed = {}, {}, {}
+
+        def subtract(u):
+            if u < units:
+                diff[u] = work.tile([P, HALF], F32, name="diff")
+                nc.vector.tensor_tensor(diff[u][:], made[u][0][:], made[u][1][:], ALU.subtract)
+
+        def gate(u):
+            if u < units:
+                twice[u] = work.tile([P, HALF], F32, name="twice")
+                nc.vector.scalar_tensor_tensor(twice[u][:], made[u][2][:], 1.0, diff[u][:], ALU.add, ALU.mult)
+
+        def mix(u):
+            if u < units:
+                mixed[u] = work.tile([P, HALF], F32, name="mixed")
+                nc.vector.scalar_tensor_tensor(mixed[u][:], twice[u][:], 0.5, made[u][1][:], ALU.mult, ALU.add)
+
+        def place(u):
+            t, h = divmod(u, HALVES)
+            nc.vector.tensor_tensor(
+                pages[t % PAGES][:].indirect(list1[:, h * HALF // 16 : (h + 1) * HALF // 16]),
+                mixed[u][:], weight[:, h * HALF : (h + 1) * HALF], ALU.mult,
+            )
+            if h == HALVES - 1:
+                finish(t)
+
+        subtract(0)
+        gate(0)
+        mix(0)
+        place(0)
+        subtract(1)
+        subtract(2)
+        gate(1)
+        gate(2)
+        mix(1)
+        for u in range(1, units):
+            subtract(u + 2)
+            mix(u + 1)
+            place(u)
+            gate(u + 2)
+
         for c in range(CHUNKS):
             nc.vector.quantize_mx(
                 out=y_codes[c][:].bitcast(FP8X4), scales=y_scales[:, c * CHUNK : (c + 1) * CHUNK],

@@ -1,6 +1,7 @@
 from contextlib import ExitStack
 
 import concourse.mybir as mybir
+from concourse.masks import make_identity
 
 K, L, N, T, J = 1024, 512, 512, 2048, 1024
 FLOPS = 2 * J * N * (2 * K + 2 * L)
@@ -22,7 +23,7 @@ HALF = 512
 HALVES = J // HALF
 CHUNK = 512
 CHUNKS = T // CHUNK
-PAGES = 2
+PAGES = 3
 
 
 def tile_list_gmu_silu_scatP_kernel(
@@ -35,6 +36,7 @@ def tile_list_gmu_silu_scatP_kernel(
         work = ctx.enter_context(tc.tile_pool(name="work", bufs=3))
         acts = ctx.enter_context(tc.tile_pool(name="acts", bufs=PACK * HALVES))
         psum = ctx.enter_context(tc.psum_pool(name="psum", bufs=2))
+        temp = ctx.enter_context(tc.tile_pool(name="temp", bufs=2))
 
         def held(shape, dtype, name, tag=""):
             return keep.tile(shape, dtype, name=name, tag=tag or name, align_bytes=64)
@@ -43,58 +45,45 @@ def tile_list_gmu_silu_scatP_kernel(
         list2 = held([P, J // 16], U16, "list2")
         tab_s = held([P, T], U8, "tab_s")
         tab2_s = held([P, T], U8, "tab2_s")
-        w_scales_raw = held([P, 5 * N], U8, "w_scales_raw")
-        shifted = held([P, J], U8, "shifted")
-        nc.vector.memset(tab_s[:].bitcast(I32), 0)
-        nc.vector.memset(tab2_s[:].bitcast(I32), 0)
-        nc.vector.memset(w_scales_raw[:].bitcast(I32), 0)
-        nc.vector.memset(shifted[:].bitcast(I32), 0)
+        wv_planes = held([P, 2, N], U8, "wv_planes")
+        z_scales_raw = held([P, 3 * N], U8, "z_scales_raw")
+        shifted = [held([P, HALF], U8, "shifted%d" % h) for h in range(HALVES)]
+        for tile in [tab_s, wv_planes, tab2_s, z_scales_raw] + shifted:
+            nc.vector.memset(tile[:].bitcast(I32), 0)
         pages = [held([P, T], F32, "page0")]
         nc.vector.memset(pages[0][:].bitcast(I32), 0)
 
         nc.sync.dma_start(list1[:], offs)
-        for q in range(4):
-            nc.sync.dma_start(tab_s[32 * q : 32 * q + 8, :].bitcast(I32), tab_scales[:, 4 * q : 4 * q + 4, :].bitcast(I32))
-        nc.sync.dma_start(list2[:], offs2)
         tab_w = held([P, T], I32, "tab_w")
         nc.sync.dma_start(tab_w[:], tab_words[0].rearrange("p t b -> p (t b)").bitcast(I32))
         for q in range(4):
+            nc.sync.dma_start(tab_s[32 * q : 32 * q + 8, :].bitcast(I32), tab_scales[:, 4 * q : 4 * q + 4, :].bitcast(I32))
+        nc.sync.dma_start(list2[:], offs2)
+        wv_codes = held([P, 2, 2 * N], U8, "wv_codes")
+        nc.sync.dma_start(wv_codes[:].bitcast(I32), wv_words.rearrange("a p c -> p a c").bitcast(I32))
+        for q in range(4):
             nc.sync.dma_start(tab2_s[32 * q : 32 * q + 4, :].bitcast(I32), tab2_scales[0, 4 * q : 4 * q + 4, :].bitcast(I32))
-        for first, scales in ((0, wv_scales), (2, zv_scales), (4, zt_scales)):
+        for q in range(4):
+            nc.sync.dma_start(
+                wv_planes[32 * q : 32 * q + 4, :, :].bitcast(I32),
+                wv_scales[:, 4 * q : 4 * q + 4, :].rearrange("a r n -> r a n").bitcast(I32),
+            )
+        wt_raw = held([P, PACK, N], F32, "wt_raw")
+        nc.sync.dma_start(wt_raw[:], wt.rearrange("(p i) n -> p i n", i=PACK))
+        for first, scales in ((0, zv_scales), (2, zt_scales)):
             passes = scales.shape[0]
             nc.sync.dma_start(
-                w_scales_raw[0:P:8, first * N : (first + passes) * N].bitcast(I32).rearrange("q (a n) -> q a n", a=passes),
+                z_scales_raw[0:P:8, first * N : (first + passes) * N].bitcast(I32).rearrange("q (a n) -> q a n", a=passes),
                 scales.rearrange("a q n -> q a n").bitcast(I32),
             )
-        raws = []
-        for name, words in (("wv_raw", wv_words), ("zv_raw", zv_words), ("zt_raw", zt_words)):
-            raw = held([P, words.shape[0], 2 * N], U8, name)
-            nc.sync.dma_start(raw[:].bitcast(I32), words.rearrange("a p c -> p a c").bitcast(I32))
-            raws.append(raw)
         bias = held([P, PACK], F32, "bias")
         nc.sync.dma_start(bias[:], b.rearrange("(p t) -> p t", t=PACK))
         half_bias = held([P, PACK], F32, "half_bias")
         nc.scalar.mul(half_bias[:], bias[:], 0.5)
-
-        v_scales = held([P, J], U8, "v_scales")
-        nc.vector.tensor_copy(v_scales[:], tab_s[:].indirect(list1[:]))
-        nc.sync.dma_start(shifted[0:100, :].bitcast(I32), v_scales[4:104, :].bitcast(I32))
-        wt_raw = held([P, PACK, N], F32, "wt_raw", "tab_s")
-        nc.sync.dma_start(wt_raw[:], wt.rearrange("(p i) n -> p i n", i=PACK))
-        w_scales = held([P, PACK, 5 * P], U8, "w_scales")
-        nc.vector.tensor_copy(w_scales[:], w_scales_raw[:].rearrange("p (m t) -> p t m", t=PACK))
-        flat_scales = w_scales[:].rearrange("p t m -> p (t m)").bitcast(I32)
-        for r in range(1, 4):
-            nc.sync.dma_start(flat_scales[r:P:32, :], flat_scales[8 * r : P : 32, :])
-        tab2_w = held([P, T], I32, "tab2_w", "w_scales_raw")
-        nc.sync.dma_start(tab2_w[:], tab2_words[0].rearrange("p t b -> p (t b)").bitcast(I32))
-        v2_scales = held([P, J], U8, "v2_scales")
-        nc.vector.tensor_copy(v2_scales[:], tab2_s[:].indirect(list2[:]))
-        weight = held([P, J], F32, "weight", "tab2_s")
-        nc.sync.dma_start(weight[:], wgo)
-
-        wt_bf = held([P, PACK, P, PACK], BF16, "wt_bf")
-        nc.scalar.copy(wt_bf[:].rearrange("p t m i -> p m t i"), wt_raw[:].rearrange("p i (m t) -> p m t i", t=PACK))
+        wt_bf = held([P, N, PACK], BF16, "wt_bf")
+        nc.scalar.copy(wt_bf[:], wt_raw[:].rearrange("p i n -> p n i"))
+        ident = held([P, P], F32, "ident")
+        make_identity(nc, ident[:])
         wt_codes = held([P, N], U32, "wt_codes")
         wt_scales = held([P, N], U8, "wt_scales")
 
@@ -113,23 +102,48 @@ def tile_list_gmu_silu_scatP_kernel(
             nc.vector.tensor_copy(codes[:], tab2_w[:].bitcast(U32).indirect(list2[:, h * HALF // 16 : (h + 1) * HALF // 16]))
             return codes
 
-        def deal(name, raw):
-            codes = held([P, raw.shape[1], PACK, 2 * P], U8, name)
-            nc.vector.tensor_copy(codes[:].bitcast(U16).rearrange("p a t m -> p t a m"), raw[:].bitcast(U16).rearrange("p a (m t) -> p t a m", t=PACK))
-            return codes
+        v_scales, v2_scales = [], []
+
+        def gather_scales(h, tag):
+            picked = held([P, HALF], U8, "v_scales%d" % h, tag)
+            nc.vector.tensor_copy(picked[:], tab_s[:].indirect(list1[:, h * HALF // 16 : (h + 1) * HALF // 16]))
+            nc.sync.dma_start(shifted[h][0:100, :].bitcast(I32), picked[4:104, :].bitcast(I32))
+            v_scales.append(picked)
+
+        def gather_scales2(h, tag):
+            picked = held([P, HALF], U8, "v2_scales%d" % h, tag)
+            nc.vector.tensor_copy(picked[:], tab2_s[:].indirect(list2[:, h * HALF // 16 : (h + 1) * HALF // 16]))
+            v2_scales.append(picked)
 
         pairs0 = gather_v(0, "")
-        wv_codes = deal("wv_codes", raws[0])
+        gather_scales(0, "")
         v_codes = [part_v(0, pairs0)]
-        zv_codes = deal("zv_codes", raws[1])
-        zt_codes = deal("zt_codes", raws[2])
+        tab2_w = held([P, T], I32, "tab2_w", "pairs0")
+        nc.sync.dma_start(tab2_w[:], tab2_words[0].rearrange("p t b -> p (t b)").bitcast(I32))
+        gather_scales2(0, "")
+        z_planes = held([P, PACK, 3 * P], U8, "z_planes")
+        nc.vector.tensor_copy(z_planes[:], z_scales_raw[:].rearrange("p (m t) -> p t m", t=PACK))
+        flat_scales = z_planes[:].rearrange("p t m -> p (t m)").bitcast(I32)
+        for r in range(1, 4):
+            nc.sync.dma_start(flat_scales[r:P:32, :], flat_scales[8 * r : P : 32, :])
+        zv_raw = held([P, 2, 2 * N], U8, "zv_raw", "z_scales_raw")
+        nc.sync.dma_start(zv_raw[:].bitcast(I32), zv_words.rearrange("a p c -> p a c").bitcast(I32))
+        zt_raw = held([P, 1, 2 * N], U8, "zt_raw", "wt_bf")
+        nc.vector.quantize_mx(out=wt_codes[:].bitcast(FP8X4), scales=wt_scales[:], in_=wt_bf[:].rearrange("p n i -> p (n i)"))
+        nc.sync.dma_start(zt_raw[:].bitcast(I32), zt_words.rearrange("a p c -> p a c").bitcast(I32))
+        weight = held([P, J], F32, "weight", "wt_raw")
+        nc.sync.dma_start(weight[:], wgo)
         v2_codes = [gather_v2(0, "")]
-        nc.vector.quantize_mx(out=wt_codes[:].bitcast(FP8X4), scales=wt_scales[:], in_=wt_bf[:].rearrange("p t m i -> p (t m i)"))
-        pairs1 = gather_v(1, "wt_bf")
-        v2_codes.append(gather_v2(1, "zt_raw"))
+        z_codes = held([P, PACK, 3, 2 * P], U8, "z_codes")
+        nc.vector.tensor_copy(z_codes[:, :, 0:2, :].bitcast(U16), zv_raw[:].bitcast(U16).rearrange("p a (m t) -> p t a m", t=PACK))
+        nc.vector.tensor_copy(z_codes[:, :, 2:3, :].bitcast(U16), zt_raw[:].bitcast(U16).rearrange("p a (m t) -> p t a m", t=PACK))
+        gather_scales(1, "wt_bf")
+        pairs1 = gather_v(1, "z_scales_raw")
+        gather_scales2(1, "tab_s")
         v_codes.append(part_v(1, pairs1))
+        v2_codes.append(gather_v2(1, "z_scales_raw"))
         for i in range(1, PAGES):
-            pages.append(held([P, T], F32, "page%d" % i, ("tab_w", "tab_s")[i - 1]))
+            pages.append(held([P, T], F32, "page%d" % i, ("tab_w", "pairs0")[i - 1]))
             nc.vector.memset(pages[i][:].bitcast(I32), 0)
 
         woven = [held([P, CHUNK, PACK], BF16, "woven%d" % c) for c in range(CHUNKS)]
@@ -138,39 +152,51 @@ def tile_list_gmu_silu_scatP_kernel(
         out_rows = out_0.rearrange("(p t) c -> p t c", t=PACK)
         out_words = out_1[0].rearrange("p t b -> p (t b)").bitcast(I32)
 
-        made = []
-        for t in range(PACK):
-            for h in range(HALVES):
-                cols = slice(h * HALF, (h + 1) * HALF)
-                planes = (v_scales[:, cols], shifted[:, cols])
-                hv = psum.tile([P, HALF], F32, name="hv")
+        blocks = HALF // P
+        order = [(0, 0), (1, 0), (0, 1), (1, 1), (2, 0), (2, 1), (3, 0), (3, 1)]
+        av, neg_at, th = {}, {}, {}
+
+        def picture(h):
+            for k in range(blocks):
+                cols = slice(k * P, (k + 1) * P)
+                planes = (v_scales[h][:, cols], shifted[h][:, cols])
+                hv = psum.tile([P, N], F32, name="branch")
                 for a in range(2):
                     nc.tensor.matmul_mx(
-                        out=hv[:], lhsT=wv_codes[:, a, t, :].bitcast(FP4X4), lhsT_scale=w_scales[:, t, a * P : (a + 1) * P],
-                        rhs=v_codes[h][:, a, :].bitcast(FP4X4), rhs_scale=planes[a], start=(a == 0), stop=(a == 1),
+                        out=hv[:], lhsT=v_codes[h][:, a, 2 * k * P : 2 * (k + 1) * P].bitcast(FP4X4), lhsT_scale=planes[a],
+                        rhs=wv_codes[:, a, :].bitcast(FP4X4), rhs_scale=wv_planes[:, a, :], start=(a == 0), stop=(a == 1),
                     )
-                ht = psum.tile([P, HALF], F32, name="ht")
+                av[h, k] = acts.tile([P, PACK, P], F32, name="av")
+                nc.scalar.activation(av[h, k][:], hv[:].rearrange("p (m t) -> p t m", t=PACK), ACT.Silu)
+
+        def text(h):
+            for k in range(blocks):
+                cols = slice(k * P, (k + 1) * P)
+                ht = psum.tile([P, N], F32, name="branch")
                 nc.tensor.matmul_mx(
-                    out=ht[:], lhsT=wt_codes[:, t * P : (t + 1) * P].bitcast(FP8X4), lhsT_scale=wt_scales[:, t * P : (t + 1) * P],
-                    rhs=v2_codes[h][:].bitcast(FP8X4), rhs_scale=v2_scales[:, cols], start=True, stop=True,
+                    out=ht[:], lhsT=v2_codes[h][:, k * P : (k + 1) * P].bitcast(FP8X4), lhsT_scale=v2_scales[h][:, cols],
+                    rhs=wt_codes[:].bitcast(FP8X4), rhs_scale=wt_scales[:], start=True, stop=True,
                 )
-                z = psum.tile([P, HALF], F32, name="z")
-                for a in range(2):
-                    nc.tensor.matmul_mx(
-                        out=z[:], lhsT=zv_codes[:, a, t, :].bitcast(FP4X4), lhsT_scale=w_scales[:, t, (2 + a) * P : (3 + a) * P],
-                        rhs=v_codes[h][:, a, :].bitcast(FP4X4), rhs_scale=planes[a], start=(a == 0), stop=False,
-                    )
+                at = temp.tile([P, PACK, P], F32, name="at")
+                nc.scalar.activation(at[:], ht[:].rearrange("p (m t) -> p t m", t=PACK), ACT.Silu)
+                neg_at[h, k] = acts.tile([P, PACK, P], F32, name="neg_at")
+                nc.scalar.mul(neg_at[h, k][:], at[:], -1.0)
+
+        def gate_sum(u):
+            t, h = order[u]
+            planes = (v_scales[h][:], shifted[h][:])
+            z = psum.tile([P, HALF], F32, name="z")
+            for a in range(2):
                 nc.tensor.matmul_mx(
-                    out=z[:], lhsT=zt_codes[:, 0, t, :].bitcast(FP4X4), lhsT_scale=w_scales[:, t, 4 * P : 5 * P],
-                    rhs=v2_codes[h][:].bitcast(FP8X4), rhs_scale=v2_scales[:, cols], start=False, stop=True,
+                    out=z[:], lhsT=z_codes[:, t, a, :].bitcast(FP4X4), lhsT_scale=z_planes[:, t, a * P : (a + 1) * P],
+                    rhs=v_codes[h][:, a, :].bitcast(FP4X4), rhs_scale=planes[a], start=(a == 0), stop=False,
                 )
-                av = acts.tile([P, HALF], F32, name="av")
-                nc.scalar.activation(av[:], hv[:], ACT.Silu)
-                at = acts.tile([P, HALF], F32, name="at")
-                nc.scalar.activation(at[:], ht[:], ACT.Silu)
-                th = acts.tile([P, HALF], F32, name="th")
-                nc.scalar.activation(th[:], z[:], ACT.Tanh, bias=half_bias[:, t : t + 1], scale=0.5)
-                made.append((av, at, th))
+            nc.tensor.matmul_mx(
+                out=z[:], lhsT=z_codes[:, t, 2, :].bitcast(FP4X4), lhsT_scale=z_planes[:, t, 2 * P : 3 * P],
+                rhs=v2_codes[h][:].bitcast(FP8X4), rhs_scale=v2_scales[h][:], start=False, stop=True,
+            )
+            th[u] = acts.tile([P, HALF], F32, name="th")
+            nc.scalar.activation(th[u][:], z[:], ACT.Tanh, bias=half_bias[:, t : t + 1], scale=0.5)
 
         def finish(t):
             page = pages[t % PAGES]
@@ -185,26 +211,33 @@ def tile_list_gmu_silu_scatP_kernel(
                 else:
                     nc.scalar.copy(woven[c][:, :, t], src)
 
-        units = PACK * HALVES
-        diff, twice, mixed = {}, {}, {}
+        units = len(order)
+        diff, back, twice, mixed = {}, {}, {}, {}
 
-        def subtract(u):
+        def turn(u):
             if u < units:
-                diff[u] = work.tile([P, HALF], F32, name="diff")
-                nc.vector.tensor_tensor(diff[u][:], made[u][0][:], made[u][1][:], ALU.subtract)
+                t, h = order[u]
+                diff[u] = psum.tile([P, HALF], F32, name="diff")
+                back[u] = psum.tile([P, HALF], F32, name="back")
+                for k in range(blocks):
+                    cols = slice(k * P, (k + 1) * P)
+                    nc.tensor.matmul(diff[u][:, cols], av[h, k][:, t, :], ident[:], start=True, stop=False, is_transpose=True)
+                    nc.tensor.matmul(diff[u][:, cols], neg_at[h, k][:, t, :], ident[:], start=False, stop=True, is_transpose=True)
+                for k in range(blocks):
+                    nc.tensor.transpose(back[u][:, k * P : (k + 1) * P], neg_at[h, k][:, t, :], ident[:])
 
         def gate(u):
             if u < units:
                 twice[u] = work.tile([P, HALF], F32, name="twice")
-                nc.vector.scalar_tensor_tensor(twice[u][:], made[u][2][:], 1.0, diff[u][:], ALU.add, ALU.mult)
+                nc.vector.scalar_tensor_tensor(twice[u][:], th[u][:], 1.0, diff[u][:], ALU.add, ALU.mult)
 
         def mix(u):
             if u < units:
                 mixed[u] = work.tile([P, HALF], F32, name="mixed")
-                nc.vector.scalar_tensor_tensor(mixed[u][:], twice[u][:], 0.5, made[u][1][:], ALU.mult, ALU.add)
+                nc.vector.scalar_tensor_tensor(mixed[u][:], twice[u][:], 0.5, back[u][:], ALU.mult, ALU.subtract)
 
         def place(u):
-            t, h = divmod(u, HALVES)
+            t, h = order[u]
             nc.vector.tensor_tensor(
                 pages[t % PAGES][:].indirect(list1[:, h * HALF // 16 : (h + 1) * HALF // 16]),
                 mixed[u][:], weight[:, h * HALF : (h + 1) * HALF], ALU.mult,
@@ -212,20 +245,24 @@ def tile_list_gmu_silu_scatP_kernel(
             if h == HALVES - 1:
                 finish(t)
 
-        subtract(0)
+        picture(0)
+        text(0)
+        gate_sum(0)
+        turn(0)
+        gate_sum(1)
+        turn(1)
+        picture(1)
+        text(1)
+        for u in range(2, units):
+            gate_sum(u)
         gate(0)
-        mix(0)
-        place(0)
-        subtract(1)
-        subtract(2)
         gate(1)
-        gate(2)
-        mix(1)
-        for u in range(1, units):
-            subtract(u + 2)
+        mix(0)
+        for u in range(units):
             mix(u + 1)
-            place(u)
+            turn(u + 2)
             gate(u + 2)
+            place(u)
 
         for c in range(CHUNKS):
             nc.vector.quantize_mx(

@@ -48,38 +48,40 @@ def tile_list_gmu_silu_scatP_kernel(
         wv_planes = held([P, 2, N], U8, "wv_planes")
         z_scales_raw = held([P, 3 * N], U8, "z_scales_raw")
         shifted = [held([P, HALF], U8, "shifted%d" % h) for h in range(HALVES)]
-        for tile in [tab_s, wv_planes, tab2_s, z_scales_raw] + shifted:
+        for tile in [tab2_s, tab_s, wv_planes, z_scales_raw] + shifted:
             nc.vector.memset(tile[:].bitcast(I32), 0)
         pages = [held([P, T], F32, "page0")]
         nc.vector.memset(pages[0][:].bitcast(I32), 0)
 
-        nc.sync.dma_start(list1[:], offs)
-        tab_w = held([P, T], I32, "tab_w")
-        nc.sync.dma_start(tab_w[:], tab_words[0].rearrange("p t b -> p (t b)").bitcast(I32))
-        for q in range(4):
-            nc.sync.dma_start(tab_s[32 * q : 32 * q + 8, :].bitcast(I32), tab_scales[:, 4 * q : 4 * q + 4, :].bitcast(I32))
         nc.sync.dma_start(list2[:], offs2)
-        wv_codes = held([P, 2, 2 * N], U8, "wv_codes")
-        nc.sync.dma_start(wv_codes[:].bitcast(I32), wv_words.rearrange("a p c -> p a c").bitcast(I32))
-        for q in range(4):
-            nc.sync.dma_start(tab2_s[32 * q : 32 * q + 4, :].bitcast(I32), tab2_scales[0, 4 * q : 4 * q + 4, :].bitcast(I32))
-        for q in range(4):
-            nc.sync.dma_start(
-                wv_planes[32 * q : 32 * q + 4, :, :].bitcast(I32),
-                wv_scales[:, 4 * q : 4 * q + 4, :].rearrange("a r n -> r a n").bitcast(I32),
-            )
         wt_raw = held([P, PACK, N], F32, "wt_raw")
         nc.sync.dma_start(wt_raw[:], wt.rearrange("(p i) n -> p i n", i=PACK))
+        for q in range(4):
+            nc.sync.dma_start(tab2_s[32 * q : 32 * q + 4, :].bitcast(I32), tab2_scales[0, 4 * q : 4 * q + 4, :].bitcast(I32))
+        nc.sync.dma_start(list1[:], offs)
+        tab2_w = held([P, T], I32, "tab2_w")
+        nc.sync.dma_start(tab2_w[:], tab2_words[0].rearrange("p t b -> p (t b)").bitcast(I32))
+        for q in range(4):
+            nc.sync.dma_start(tab_s[32 * q : 32 * q + 8, :].bitcast(I32), tab_scales[:, 4 * q : 4 * q + 4, :].bitcast(I32))
+        tab_w = held([P, T], I32, "tab_w")
+        nc.sync.dma_start(tab_w[:], tab_words[0].rearrange("p t b -> p (t b)").bitcast(I32))
+        wv_codes = held([P, 2, 2 * N], U8, "wv_codes")
+        nc.sync.dma_start(wv_codes[:].bitcast(I32), wv_words.rearrange("a p c -> p a c").bitcast(I32))
         for first, scales in ((0, zv_scales), (2, zt_scales)):
             passes = scales.shape[0]
             nc.sync.dma_start(
                 z_scales_raw[0:P:8, first * N : (first + passes) * N].bitcast(I32).rearrange("q (a n) -> q a n", a=passes),
                 scales.rearrange("a q n -> q a n").bitcast(I32),
             )
+        for q in range(4):
+            nc.sync.dma_start(
+                wv_planes[32 * q : 32 * q + 4, :, :].bitcast(I32),
+                wv_scales[:, 4 * q : 4 * q + 4, :].rearrange("a r n -> r a n").bitcast(I32),
+            )
         bias = held([P, PACK], F32, "bias")
         nc.sync.dma_start(bias[:], b.rearrange("(p t) -> p t", t=PACK))
         half_bias = held([P, PACK], F32, "half_bias")
-        nc.scalar.mul(half_bias[:], bias[:], 0.5)
+        nc.gpsimd.tensor_scalar(half_bias[:], bias[:], 0.5, 0.0, ALU.mult, ALU.add)
         wt_bf = held([P, N, PACK], BF16, "wt_bf")
         nc.scalar.copy(wt_bf[:], wt_raw[:].rearrange("p i n -> p n i"))
         ident = held([P, P], F32, "ident")
@@ -102,7 +104,7 @@ def tile_list_gmu_silu_scatP_kernel(
             nc.vector.tensor_copy(codes[:], tab2_w[:].bitcast(U32).indirect(list2[:, h * HALF // 16 : (h + 1) * HALF // 16]))
             return codes
 
-        v_scales, v2_scales = [], []
+        v_scales = []
 
         def gather_scales(h, tag):
             picked = held([P, HALF], U8, "v_scales%d" % h, tag)
@@ -110,40 +112,32 @@ def tile_list_gmu_silu_scatP_kernel(
             nc.sync.dma_start(shifted[h][0:100, :].bitcast(I32), picked[4:104, :].bitcast(I32))
             v_scales.append(picked)
 
-        def gather_scales2(h, tag):
-            picked = held([P, HALF], U8, "v2_scales%d" % h, tag)
-            nc.vector.tensor_copy(picked[:], tab2_s[:].indirect(list2[:, h * HALF // 16 : (h + 1) * HALF // 16]))
-            v2_scales.append(picked)
-
-        pairs0 = gather_v(0, "")
+        all_v2_scales = held([P, J], U8, "v2_scales")
+        nc.vector.tensor_copy(all_v2_scales[:], tab2_s[:].indirect(list2[:]))
+        v2_scales = [all_v2_scales[:, h * HALF : (h + 1) * HALF] for h in range(HALVES)]
+        v2_codes = [gather_v2(0, "")]
+        nc.vector.quantize_mx(out=wt_codes[:].bitcast(FP8X4), scales=wt_scales[:], in_=wt_bf[:].rearrange("p n i -> p (n i)"))
+        z_words = held([P, 3, 2 * N], U8, "z_words", "tab2_s")
+        for first, words in ((0, zv_words), (2, zt_words)):
+            nc.sync.dma_start(z_words[:, first : first + words.shape[0], :].bitcast(I32), words.rearrange("a p c -> p a c").bitcast(I32))
         gather_scales(0, "")
-        v_codes = [part_v(0, pairs0)]
-        tab2_w = held([P, T], I32, "tab2_w", "pairs0")
-        nc.sync.dma_start(tab2_w[:], tab2_words[0].rearrange("p t b -> p (t b)").bitcast(I32))
-        gather_scales2(0, "")
         z_planes = held([P, PACK, 3 * P], U8, "z_planes")
         nc.vector.tensor_copy(z_planes[:], z_scales_raw[:].rearrange("p (m t) -> p t m", t=PACK))
         flat_scales = z_planes[:].rearrange("p t m -> p (t m)").bitcast(I32)
         for r in range(1, 4):
             nc.sync.dma_start(flat_scales[r:P:32, :], flat_scales[8 * r : P : 32, :])
-        zv_raw = held([P, 2, 2 * N], U8, "zv_raw", "z_scales_raw")
-        nc.sync.dma_start(zv_raw[:].bitcast(I32), zv_words.rearrange("a p c -> p a c").bitcast(I32))
-        zt_raw = held([P, 1, 2 * N], U8, "zt_raw", "wt_bf")
-        nc.vector.quantize_mx(out=wt_codes[:].bitcast(FP8X4), scales=wt_scales[:], in_=wt_bf[:].rearrange("p n i -> p (n i)"))
-        nc.sync.dma_start(zt_raw[:].bitcast(I32), zt_words.rearrange("a p c -> p a c").bitcast(I32))
+        pairs0 = gather_v(0, "")
+        v_codes = [part_v(0, pairs0)]
         weight = held([P, J], F32, "weight", "wt_raw")
         nc.sync.dma_start(weight[:], wgo)
-        v2_codes = [gather_v2(0, "")]
         z_codes = held([P, PACK, 3, 2 * P], U8, "z_codes")
-        nc.vector.tensor_copy(z_codes[:, :, 0:2, :].bitcast(U16), zv_raw[:].bitcast(U16).rearrange("p a (m t) -> p t a m", t=PACK))
-        nc.vector.tensor_copy(z_codes[:, :, 2:3, :].bitcast(U16), zt_raw[:].bitcast(U16).rearrange("p a (m t) -> p t a m", t=PACK))
-        gather_scales(1, "wt_bf")
-        pairs1 = gather_v(1, "z_scales_raw")
-        gather_scales2(1, "tab_s")
+        nc.vector.tensor_copy(z_codes[:].bitcast(U16), z_words[:].bitcast(U16).rearrange("p a (m t) -> p t a m", t=PACK))
+        gather_scales(1, "pairs0")
+        pairs1 = gather_v(1, "tab2_s")
         v_codes.append(part_v(1, pairs1))
-        v2_codes.append(gather_v2(1, "z_scales_raw"))
+        v2_codes.append(gather_v2(1, "tab2_s"))
         for i in range(1, PAGES):
-            pages.append(held([P, T], F32, "page%d" % i, ("tab_w", "pairs0")[i - 1]))
+            pages.append(held([P, T], F32, "page%d" % i, ("tab_w", "tab2_w")[i - 1]))
             nc.vector.memset(pages[i][:].bitcast(I32), 0)
 
         woven = [held([P, CHUNK, PACK], BF16, "woven%d" % c) for c in range(CHUNKS)]
@@ -193,7 +187,7 @@ def tile_list_gmu_silu_scatP_kernel(
                 )
             nc.tensor.matmul_mx(
                 out=z[:], lhsT=z_codes[:, t, 2, :].bitcast(FP4X4), lhsT_scale=z_planes[:, t, 2 * P : 3 * P],
-                rhs=v2_codes[h][:].bitcast(FP8X4), rhs_scale=v2_scales[h][:], start=False, stop=True,
+                rhs=v2_codes[h][:].bitcast(FP8X4), rhs_scale=v2_scales[h], start=False, stop=True,
             )
             th[u] = acts.tile([P, HALF], F32, name="th")
             nc.scalar.activation(th[u][:], z[:], ACT.Tanh, bias=half_bias[:, t : t + 1], scale=0.5)
@@ -245,8 +239,8 @@ def tile_list_gmu_silu_scatP_kernel(
             if h == HALVES - 1:
                 finish(t)
 
-        picture(0)
         text(0)
+        picture(0)
         gate_sum(0)
         turn(0)
         gate_sum(1)

@@ -24,6 +24,7 @@ HALVES = J // HALF
 CHUNK = 512
 CHUNKS = T // CHUNK
 PAGES = 3
+LEAD = 3
 
 
 def tile_list_gmu_silu_scatP_kernel(
@@ -140,44 +141,39 @@ def tile_list_gmu_silu_scatP_kernel(
             pages.append(held([P, T], F32, "page%d" % i, ("tab_w", "tab2_w")[i - 1]))
             nc.vector.memset(pages[i][:].bitcast(I32), 0)
 
-        woven = [held([P, CHUNK, PACK], BF16, "woven%d" % c) for c in range(CHUNKS)]
         y_codes = [held([P, CHUNK], U32, "y_codes%d" % c) for c in range(CHUNKS)]
         y_scales = held([P, T], U8, "y_scales")
         out_rows = out_0.rearrange("(p t) c -> p t c", t=PACK)
         out_words = out_1[0].rearrange("p t b -> p (t b)").bitcast(I32)
 
         blocks = HALF // P
-        order = [(0, 0), (1, 0), (0, 1), (1, 1), (2, 0), (2, 1), (3, 0), (3, 1)]
         av, neg_at, th = {}, {}, {}
 
-        def picture(h):
-            for k in range(blocks):
-                cols = slice(k * P, (k + 1) * P)
-                planes = (v_scales[h][:, cols], shifted[h][:, cols])
-                hv = psum.tile([P, N], F32, name="branch")
-                for a in range(2):
-                    nc.tensor.matmul_mx(
-                        out=hv[:], lhsT=v_codes[h][:, a, 2 * k * P : 2 * (k + 1) * P].bitcast(FP4X4), lhsT_scale=planes[a],
-                        rhs=wv_codes[:, a, :].bitcast(FP4X4), rhs_scale=wv_planes[:, a, :], start=(a == 0), stop=(a == 1),
-                    )
-                av[h, k] = acts.tile([P, PACK, P], F32, name="av")
-                nc.scalar.activation(av[h, k][:], hv[:].rearrange("p (m t) -> p t m", t=PACK), ACT.Silu)
-
-        def text(h):
-            for k in range(blocks):
-                cols = slice(k * P, (k + 1) * P)
-                ht = psum.tile([P, N], F32, name="branch")
+        def picture(h, k):
+            cols = slice(k * P, (k + 1) * P)
+            planes = (v_scales[h][:, cols], shifted[h][:, cols])
+            hv = psum.tile([P, N], F32, name="branch")
+            for a in range(2):
                 nc.tensor.matmul_mx(
-                    out=ht[:], lhsT=v2_codes[h][:, k * P : (k + 1) * P].bitcast(FP8X4), lhsT_scale=v2_scales[h][:, cols],
-                    rhs=wt_codes[:].bitcast(FP8X4), rhs_scale=wt_scales[:], start=True, stop=True,
+                    out=hv[:], lhsT=v_codes[h][:, a, 2 * k * P : 2 * (k + 1) * P].bitcast(FP4X4), lhsT_scale=planes[a],
+                    rhs=wv_codes[:, a, :].bitcast(FP4X4), rhs_scale=wv_planes[:, a, :], start=(a == 0), stop=(a == 1),
                 )
-                at = temp.tile([P, PACK, P], F32, name="at")
-                nc.scalar.activation(at[:], ht[:].rearrange("p (m t) -> p t m", t=PACK), ACT.Silu)
-                neg_at[h, k] = acts.tile([P, PACK, P], F32, name="neg_at")
-                nc.scalar.mul(neg_at[h, k][:], at[:], -1.0)
+            av[h, k] = acts.tile([P, PACK, P], F32, name="av")
+            nc.scalar.activation(av[h, k][:], hv[:].rearrange("p (m t) -> p t m", t=PACK), ACT.Silu)
 
-        def gate_sum(u):
-            t, h = order[u]
+        def text(h, k):
+            cols = slice(k * P, (k + 1) * P)
+            ht = psum.tile([P, N], F32, name="branch")
+            nc.tensor.matmul_mx(
+                out=ht[:], lhsT=v2_codes[h][:, cols].bitcast(FP8X4), lhsT_scale=v2_scales[h][:, cols],
+                rhs=wt_codes[:].bitcast(FP8X4), rhs_scale=wt_scales[:], start=True, stop=True,
+            )
+            at = temp.tile([P, PACK, P], F32, name="at")
+            nc.scalar.activation(at[:], ht[:].rearrange("p (m t) -> p t m", t=PACK), ACT.Silu)
+            neg_at[h, k] = acts.tile([P, PACK, P], F32, name="neg_at")
+            nc.scalar.mul(neg_at[h, k][:], at[:], -1.0)
+
+        def gate_sum(t, h):
             planes = (v_scales[h][:], shifted[h][:])
             z = psum.tile([P, HALF], F32, name="z")
             for a in range(2):
@@ -189,8 +185,8 @@ def tile_list_gmu_silu_scatP_kernel(
                 out=z[:], lhsT=z_codes[:, t, 2, :].bitcast(FP4X4), lhsT_scale=z_planes[:, t, 2 * P : 3 * P],
                 rhs=v2_codes[h][:].bitcast(FP8X4), rhs_scale=v2_scales[h], start=False, stop=True,
             )
-            th[u] = acts.tile([P, HALF], F32, name="th")
-            nc.scalar.activation(th[u][:], z[:], ACT.Tanh, bias=half_bias[:, t : t + 1], scale=0.5)
+            th[t, h] = acts.tile([P, HALF], F32, name="th")
+            nc.scalar.activation(th[t, h][:], z[:], ACT.Tanh, bias=half_bias[:, t : t + 1], scale=0.5)
 
         def finish(t):
             page = pages[t % PAGES]
@@ -205,58 +201,90 @@ def tile_list_gmu_silu_scatP_kernel(
                 else:
                     nc.scalar.copy(woven[c][:, :, t], src)
 
+        order = [(0, 0), (1, 0), (0, 1), (1, 1), (2, 0), (2, 1), (3, 0), (3, 1)]
         units = len(order)
-        diff, back, twice, mixed = {}, {}, {}, {}
+        diff, back, twice, mixed, twice_at = {}, {}, {}, {}, {}
 
-        def turn(u):
+        def turn_diff(u):
             if u < units:
                 t, h = order[u]
                 diff[u] = psum.tile([P, HALF], F32, name="diff")
-                back[u] = psum.tile([P, HALF], F32, name="back")
                 for k in range(blocks):
                     cols = slice(k * P, (k + 1) * P)
                     nc.tensor.matmul(diff[u][:, cols], av[h, k][:, t, :], ident[:], start=True, stop=False, is_transpose=True)
                     nc.tensor.matmul(diff[u][:, cols], neg_at[h, k][:, t, :], ident[:], start=False, stop=True, is_transpose=True)
-                for k in range(blocks):
-                    nc.tensor.transpose(back[u][:, k * P : (k + 1) * P], neg_at[h, k][:, t, :], ident[:])
+
+        def turn_back(u):
+            t, h = order[u]
+            back[u] = psum.tile([P, HALF], F32, name="back")
+            for k in range(blocks):
+                nc.tensor.transpose(back[u][:, k * P : (k + 1) * P], neg_at[h, k][:, t, :], ident[:])
+            if u >= LEAD:
+                twice_at[u] = acts.tile([P, HALF], F32, name="twice_at")
+                nc.scalar.mul(twice_at[u][:], back[u][:], -2.0)
 
         def gate(u):
             if u < units:
+                t, h = order[u]
                 twice[u] = work.tile([P, HALF], F32, name="twice")
-                nc.vector.scalar_tensor_tensor(twice[u][:], th[u][:], 1.0, diff[u][:], ALU.add, ALU.mult)
+                nc.vector.scalar_tensor_tensor(twice[u][:], th[t, h][:], 1.0, diff[u][:], ALU.add, ALU.mult)
 
         def mix(u):
-            if u < units:
+            if u < LEAD:
                 mixed[u] = work.tile([P, HALF], F32, name="mixed")
                 nc.vector.scalar_tensor_tensor(mixed[u][:], twice[u][:], 0.5, back[u][:], ALU.mult, ALU.subtract)
+            elif u < units:
+                h = order[u][1]
+                total = temp.tile([P, HALF], F32, name="total")
+                nc.gpsimd.tensor_tensor(total[:], twice[u][:], twice_at[u][:], ALU.add)
+                mixed[u] = work.tile([P, HALF], F32, name="mixed")
+                nc.gpsimd.tensor_tensor(mixed[u][:], total[:], half_weight[:, h * HALF : (h + 1) * HALF], ALU.mult)
 
         def place(u):
             t, h = order[u]
-            nc.vector.tensor_tensor(
-                pages[t % PAGES][:].indirect(list1[:, h * HALF // 16 : (h + 1) * HALF // 16]),
-                mixed[u][:], weight[:, h * HALF : (h + 1) * HALF], ALU.mult,
-            )
+            window = pages[t % PAGES][:].indirect(list1[:, h * HALF // 16 : (h + 1) * HALF // 16])
+            if u < LEAD:
+                nc.vector.tensor_tensor(window, mixed[u][:], weight[:, h * HALF : (h + 1) * HALF], ALU.mult)
+            else:
+                nc.vector.tensor_copy(window, mixed[u][:])
             if h == HALVES - 1:
                 finish(t)
 
-        text(0)
-        picture(0)
-        gate_sum(0)
-        turn(0)
-        gate_sum(1)
-        turn(1)
-        picture(1)
-        text(1)
-        for u in range(2, units):
-            gate_sum(u)
+        half_weight = held([P, J], F32, "half_weight")
+        nc.gpsimd.tensor_scalar(half_weight[:], weight[:], 0.5, 0.0, ALU.mult, ALU.add)
+        for k in range(blocks):
+            text(0, k)
+        for k in range(blocks):
+            picture(0, k)
+        for u in range(2):
+            gate_sum(*order[u])
+            turn_diff(u)
+            turn_back(u)
+        for k in range(blocks):
+            picture(1, k)
+        for k in range(blocks):
+            text(1, k)
         gate(0)
         gate(1)
         mix(0)
-        for u in range(units):
-            mix(u + 1)
-            turn(u + 2)
-            gate(u + 2)
+        mix(1)
+        place(0)
+        place(1)
+        for u in range(2, units):
+            gate_sum(*order[u])
+            turn_back(u)
+            if u < 4:
+                turn_diff(u)
+        woven = [held([P, CHUNK, PACK], BF16, "woven%d" % c, tag) for c, tag in enumerate(("z_codes", "v_codes1", "tab2_s", "z_planes"))]
+        gate(2)
+        gate(3)
+        mix(2)
+        mix(3)
+        for u in range(2, units):
+            turn_diff(u + 2)
             place(u)
+            gate(u + 2)
+            mix(u + 2)
 
         for c in range(CHUNKS):
             nc.vector.quantize_mx(

@@ -24,7 +24,7 @@ HALVES = J // HALF
 CHUNK = 512
 CHUNKS = T // CHUNK
 PAGES = 3
-LEAD = 3
+LEAD = 4
 
 
 def tile_list_gmu_silu_scatP_kernel(
@@ -185,7 +185,7 @@ def tile_list_gmu_silu_scatP_kernel(
                 out=z[:], lhsT=z_codes[:, t, 2, :].bitcast(FP4X4), lhsT_scale=z_planes[:, t, 2 * P : 3 * P],
                 rhs=v2_codes[h][:].bitcast(FP8X4), rhs_scale=v2_scales[h], start=False, stop=True,
             )
-            th[t, h] = acts.tile([P, HALF], F32, name="th")
+            th[t, h] = held([P, HALF], F32, "th%d%d" % (t, h))
             nc.scalar.activation(th[t, h][:], z[:], ACT.Tanh, bias=half_bias[:, t : t + 1], scale=0.5)
 
         def finish(t):
@@ -216,7 +216,7 @@ def tile_list_gmu_silu_scatP_kernel(
 
         def turn_back(u):
             t, h = order[u]
-            back[u] = psum.tile([P, HALF], F32, name="back")
+            back[u] = psum.tile([P, HALF], F32, name="back" if u < LEAD else "branch")
             for k in range(blocks):
                 nc.tensor.transpose(back[u][:, k * P : (k + 1) * P], neg_at[h, k][:, t, :], ident[:])
             if u >= LEAD:
@@ -243,8 +243,12 @@ def tile_list_gmu_silu_scatP_kernel(
         def place(u):
             t, h = order[u]
             window = pages[t % PAGES][:].indirect(list1[:, h * HALF // 16 : (h + 1) * HALF // 16])
-            if u < LEAD:
+            if u < LEAD - 1:
                 nc.vector.tensor_tensor(window, mixed[u][:], weight[:, h * HALF : (h + 1) * HALF], ALU.mult)
+            elif u == LEAD - 1:
+                weighed = held([P, HALF], F32, "weighed", "th%d%d" % order[LEAD])
+                nc.vector.tensor_tensor(weighed[:], mixed[u][:], weight[:, h * HALF : (h + 1) * HALF], ALU.mult)
+                nc.vector.tensor_copy(window, weighed[:])
             else:
                 nc.vector.tensor_copy(window, mixed[u][:])
             if h == HALVES - 1:
@@ -272,18 +276,22 @@ def tile_list_gmu_silu_scatP_kernel(
         place(1)
         for u in range(2, units):
             gate_sum(*order[u])
-            turn_back(u)
-            if u < 4:
+            if u < LEAD:
                 turn_diff(u)
+            turn_back(u)
         woven = [held([P, CHUNK, PACK], BF16, "woven%d" % c, tag) for c, tag in enumerate(("z_codes", "v_codes1", "tab2_s", "z_planes"))]
         gate(2)
         gate(3)
         mix(2)
+        place(2)
+        turn_diff(4)
+        gate(4)
         mix(3)
-        for u in range(2, units):
+        mix(4)
+        for u in range(3, units):
             turn_diff(u + 2)
-            place(u)
             gate(u + 2)
+            place(u)
             mix(u + 2)
 
         for c in range(CHUNKS):

@@ -23,8 +23,8 @@ HALF = 512
 HALVES = J // HALF
 CHUNK = 512
 CHUNKS = T // CHUNK
-PAGES = 3
-LEAD = 4
+QUARTER = 256
+QUARTERS = J // QUARTER
 
 
 def tile_list_gmu_silu_scatP_kernel(
@@ -34,148 +34,154 @@ def tile_list_gmu_silu_scatP_kernel(
     nc = tc.nc
     with ExitStack() as ctx:
         keep = ctx.enter_context(tc.tile_pool(name="keep", bufs=1))
-        work = ctx.enter_context(tc.tile_pool(name="work", bufs=3))
-        acts = ctx.enter_context(tc.tile_pool(name="acts", bufs=PACK * HALVES))
-        psum = ctx.enter_context(tc.psum_pool(name="psum", bufs=2))
+        reuse = ctx.enter_context(tc.tile_pool(name="reuse", bufs=1))
+        acts = ctx.enter_context(tc.tile_pool(name="acts", bufs=4))
         temp = ctx.enter_context(tc.tile_pool(name="temp", bufs=2))
+        psum = ctx.enter_context(tc.psum_pool(name="psum", bufs=2))
 
         def held(shape, dtype, name, tag=""):
             return keep.tile(shape, dtype, name=name, tag=tag or name, align_bytes=64)
+
+        def placed(shape, dtype, name, offset):
+            return reuse.tile(shape, dtype, name=name, align_bytes=64, offset=offset)
+
+        def entries(offsets, first, count):
+            return offsets[:, first // 16 : (first + count) // 16]
 
         list1 = held([P, J // 16], U16, "list1")
         list2 = held([P, J // 16], U16, "list2")
         tab_s = held([P, T], U8, "tab_s")
         tab2_s = held([P, T], U8, "tab2_s")
-        wv_planes = held([P, 2, N], U8, "wv_planes")
         z_scales_raw = held([P, 3 * N], U8, "z_scales_raw")
-        shifted = [held([P, HALF], U8, "shifted%d" % h) for h in range(HALVES)]
-        for tile in [tab2_s, tab_s, wv_planes, z_scales_raw] + shifted:
-            nc.vector.memset(tile[:].bitcast(I32), 0)
-        pages = [held([P, T], F32, "page0")]
-        nc.vector.memset(pages[0][:].bitcast(I32), 0)
+        w_planes = held([P, 5 * N], U8, "w_planes")
+        shifted_all = held([P, J], U8, "shifted")
+        shifted = [shifted_all[:, h * HALF : (h + 1) * HALF] for h in range(HALVES)]
+        for tile in [tab_s[:], z_scales_raw[:], w_planes[:, 3 * N :], tab2_s[:], shifted_all[:]]:
+            nc.vector.memset(tile.bitcast(I32), 0)
+        pages = [held([P, T], F32, "page%d" % t) for t in range(2)]
+        w_rows = held([P, P], F32, "w_rows")
+        nc.gpsimd.memset(w_rows[:], 0.0)
+        ident = held([P, P], F32, "ident")
+        make_identity(nc, ident[:])
+        for page in pages:
+            nc.gpsimd.memset(page[:], 0.0)
 
-        nc.sync.dma_start(list2[:], offs2)
+        nc.sync.dma_start(list1[:], offs)
         wt_raw = held([P, PACK, N], F32, "wt_raw")
         nc.sync.dma_start(wt_raw[:], wt.rearrange("(p i) n -> p i n", i=PACK))
         for q in range(4):
-            nc.sync.dma_start(tab2_s[32 * q : 32 * q + 4, :].bitcast(I32), tab2_scales[0, 4 * q : 4 * q + 4, :].bitcast(I32))
-        nc.sync.dma_start(list1[:], offs)
-        tab2_w = held([P, T], I32, "tab2_w")
-        nc.sync.dma_start(tab2_w[:], tab2_words[0].rearrange("p t b -> p (t b)").bitcast(I32))
-        for q in range(4):
             nc.sync.dma_start(tab_s[32 * q : 32 * q + 8, :].bitcast(I32), tab_scales[:, 4 * q : 4 * q + 4, :].bitcast(I32))
-        tab_w = held([P, T], I32, "tab_w")
-        nc.sync.dma_start(tab_w[:], tab_words[0].rearrange("p t b -> p (t b)").bitcast(I32))
-        wv_codes = held([P, 2, 2 * N], U8, "wv_codes")
-        nc.sync.dma_start(wv_codes[:].bitcast(I32), wv_words.rearrange("a p c -> p a c").bitcast(I32))
         for first, scales in ((0, zv_scales), (2, zt_scales)):
             passes = scales.shape[0]
             nc.sync.dma_start(
                 z_scales_raw[0:P:8, first * N : (first + passes) * N].bitcast(I32).rearrange("q (a n) -> q a n", a=passes),
                 scales.rearrange("a q n -> q a n").bitcast(I32),
             )
+        nc.sync.dma_start(list2[:], offs2)
+        tab2_w = held([P, T], I32, "tab2_w")
+        nc.sync.dma_start(tab2_w[:], tab2_words[0].rearrange("p t b -> p (t b)").bitcast(I32))
+        nc.sync.dma_start(
+            w_planes[0:P:8, 3 * N :].bitcast(I32).rearrange("q (a n) -> q a n", a=2),
+            wv_scales.rearrange("a q n -> q a n").bitcast(I32),
+        )
         for q in range(4):
-            nc.sync.dma_start(
-                wv_planes[32 * q : 32 * q + 4, :, :].bitcast(I32),
-                wv_scales[:, 4 * q : 4 * q + 4, :].rearrange("a r n -> r a n").bitcast(I32),
-            )
-        bias = held([P, PACK], F32, "bias")
-        nc.sync.dma_start(bias[:], b.rearrange("(p t) -> p t", t=PACK))
-        half_bias = held([P, PACK], F32, "half_bias")
-        nc.gpsimd.tensor_scalar(half_bias[:], bias[:], 0.5, 0.0, ALU.mult, ALU.add)
+            nc.sync.dma_start(tab2_s[32 * q : 32 * q + 4, :].bitcast(I32), tab2_scales[0, 4 * q : 4 * q + 4, :].bitcast(I32))
+        tab_w = held([P, T], I32, "tab_w")
+        nc.sync.dma_start(tab_w[:], tab_words[0].rearrange("p t b -> p (t b)").bitcast(I32))
+        nc.sync.dma_start(w_rows[0 : J // P, :], wgo[0].rearrange("(k p) -> k p", p=P))
+
         wt_bf = held([P, N, PACK], BF16, "wt_bf")
         nc.scalar.copy(wt_bf[:], wt_raw[:].rearrange("p i n -> p n i"))
-        ident = held([P, P], F32, "ident")
-        make_identity(nc, ident[:])
+        w_turned = psum.tile([P, P], F32, name="sums", bufs=6)
+        nc.tensor.transpose(w_turned[:], w_rows[:], ident[:])
+        half_w = held([P, J // P], F32, "half_w")
+        nc.scalar.mul(half_w[:], w_turned[:, 0 : J // P], 0.5)
+        neg_half_w = held([P, J // P], F32, "neg_half_w")
+        nc.scalar.mul(neg_half_w[:], w_turned[:, 0 : J // P], -0.5)
         wt_codes = held([P, N], U32, "wt_codes")
         wt_scales = held([P, N], U8, "wt_scales")
 
-        def gather_v(h, tag):
-            pairs = held([P, HALF], U32, "pairs%d" % h, tag)
-            nc.vector.tensor_copy(pairs[:], tab_w[:].bitcast(U32).indirect(list1[:, h * HALF // 16 : (h + 1) * HALF // 16]))
-            return pairs
+        def gather(out, window, offsets, h):
+            nc.vector.tensor_copy(out[:], window.indirect(entries(offsets, h * HALF, HALF)))
+            return out
 
         def part_v(h, pairs):
             codes = held([P, 2, 2 * HALF], U8, "v_codes%d" % h)
             nc.vector.tensor_copy(codes[:].bitcast(U16), pairs[:].bitcast(U16).rearrange("p (j a) -> p a j", a=2))
             return codes
 
-        def gather_v2(h, tag):
-            codes = held([P, HALF], U32, "v2_codes%d" % h, tag)
-            nc.vector.tensor_copy(codes[:], tab2_w[:].bitcast(U32).indirect(list2[:, h * HALF // 16 : (h + 1) * HALF // 16]))
-            return codes
-
-        v_scales = []
-
-        def gather_scales(h, tag):
-            picked = held([P, HALF], U8, "v_scales%d" % h, tag)
-            nc.vector.tensor_copy(picked[:], tab_s[:].indirect(list1[:, h * HALF // 16 : (h + 1) * HALF // 16]))
-            nc.sync.dma_start(shifted[h][0:100, :].bitcast(I32), picked[4:104, :].bitcast(I32))
-            v_scales.append(picked)
-
-        all_v2_scales = held([P, J], U8, "v2_scales")
-        nc.vector.tensor_copy(all_v2_scales[:], tab2_s[:].indirect(list2[:]))
-        v2_scales = [all_v2_scales[:, h * HALF : (h + 1) * HALF] for h in range(HALVES)]
-        v2_codes = [gather_v2(0, "")]
-        nc.vector.quantize_mx(out=wt_codes[:].bitcast(FP8X4), scales=wt_scales[:], in_=wt_bf[:].rearrange("p n i -> p (n i)"))
-        z_words = held([P, 3, 2 * N], U8, "z_words", "tab2_s")
-        for first, words in ((0, zv_words), (2, zt_words)):
-            nc.sync.dma_start(z_words[:, first : first + words.shape[0], :].bitcast(I32), words.rearrange("a p c -> p a c").bitcast(I32))
-        gather_scales(0, "")
-        z_planes = held([P, PACK, 3 * P], U8, "z_planes")
-        nc.vector.tensor_copy(z_planes[:], z_scales_raw[:].rearrange("p (m t) -> p t m", t=PACK))
-        flat_scales = z_planes[:].rearrange("p t m -> p (t m)").bitcast(I32)
+        picked = held([P, J], U8, "v_scales")
+        nc.vector.tensor_copy(picked[:], tab_s[:].indirect(list1[:]))
+        v_scales = [picked[:, h * HALF : (h + 1) * HALF] for h in range(HALVES)]
+        nc.sync.dma_start(shifted_all[0:100, :].bitcast(I32), picked[4:104, :].bitcast(I32))
+        z_planes = w_planes[:, 0 : 3 * N].rearrange("p (t m) -> p t m", t=PACK)
+        nc.vector.tensor_copy(z_planes, z_scales_raw[:].rearrange("p (m t) -> p t m", t=PACK))
+        flat_scales = w_planes[:].bitcast(I32)
         for r in range(1, 4):
             nc.sync.dma_start(flat_scales[r:P:32, :], flat_scales[8 * r : P : 32, :])
-        pairs0 = gather_v(0, "")
+        wv_codes = held([P, 2, 2 * N], U8, "wv_codes")
+        nc.sync.dma_start(wv_codes[:].bitcast(I32), wv_words.rearrange("a p c -> p a c").bitcast(I32))
+        z_words = placed([P, 3, 2 * N], U8, "z_words", 0)
+        for first, words in ((0, zv_words), (2, zt_words)):
+            nc.sync.dma_start(z_words[:, first : first + words.shape[0], :].bitcast(I32), words.rearrange("a p c -> p a c").bitcast(I32))
+        bias = held([P, PACK], F32, "bias")
+        nc.sync.dma_start(bias[:], b.rearrange("(p t) -> p t", t=PACK))
+        half_bias = held([P, PACK], F32, "half_bias")
+        nc.scalar.mul(half_bias[:], bias[:], 0.5)
+        nc.vector.quantize_mx(out=wt_codes[:].bitcast(FP8X4), scales=wt_scales[:], in_=wt_bf[:].rearrange("p n i -> p (n i)"))
+        v2_scales = [gather(held([P, HALF], U8, "v2_scales0"), tab2_s[:], list2, 0)]
+        v2_codes = [gather(held([P, HALF], U32, "v2_codes0"), tab2_w[:].bitcast(U32), list2, 0)]
+        pairs0 = gather(held([P, HALF], U32, "pairs0"), tab_w[:].bitcast(U32), list1, 0)
         v_codes = [part_v(0, pairs0)]
-        weight = held([P, J], F32, "weight", "wt_raw")
-        nc.sync.dma_start(weight[:], wgo)
         z_codes = held([P, PACK, 3, 2 * P], U8, "z_codes")
         nc.vector.tensor_copy(z_codes[:].bitcast(U16), z_words[:].bitcast(U16).rearrange("p a (m t) -> p t a m", t=PACK))
-        gather_scales(1, "pairs0")
-        pairs1 = gather_v(1, "tab2_s")
+        pairs1 = gather(placed([P, HALF], U32, "pairs1", 2 * HALF), tab_w[:].bitcast(U32), list1, 1)
+        v2_scales.append(gather(placed([P, HALF], U8, "v2_scales1", HALF), tab2_s[:], list2, 1))
         v_codes.append(part_v(1, pairs1))
-        v2_codes.append(gather_v2(1, "tab2_s"))
-        for i in range(1, PAGES):
-            pages.append(held([P, T], F32, "page%d" % i, ("tab_w", "tab2_w")[i - 1]))
-            nc.vector.memset(pages[i][:].bitcast(I32), 0)
+        v2_codes.append(gather(placed([P, HALF], U32, "v2_codes1", 2 * HALF), tab2_w[:].bitcast(U32), list2, 1))
+        pages.append(held([P, T], F32, "page2", "tab_w"))
+        for c in range(CHUNKS):
+            nc.gpsimd.memset(pages[2][:, c * CHUNK : (c + 1) * CHUNK], 0.0)
 
-        y_codes = [held([P, CHUNK], U32, "y_codes%d" % c) for c in range(CHUNKS)]
-        y_scales = held([P, T], U8, "y_scales")
         out_rows = out_0.rearrange("(p t) c -> p t c", t=PACK)
         out_words = out_1[0].rearrange("p t b -> p (t b)").bitcast(I32)
-
         blocks = HALF // P
-        av, neg_at, th = {}, {}, {}
+        seen, said = {}, {}
+        th = {(h, pair): held([P, 2, HALF], F32, "th%d%d" % (h, pair)) for h in range(HALVES) for pair in range(2)}
+        gated = {(h, pair): held([P, 2, HALF], F32, "gated%d%d" % (h, pair)) for h in range(HALVES) for pair in range(2)}
+        base = {(h, pair): held([P, 2, HALF], F32, "base%d%d" % (h, pair)) for h in range(HALVES) for pair in range(2)}
 
-        def picture(h, k):
+        def picture(block):
+            h, k = divmod(block, blocks)
             cols = slice(k * P, (k + 1) * P)
             planes = (v_scales[h][:, cols], shifted[h][:, cols])
-            hv = psum.tile([P, N], F32, name="branch")
+            hv = psum.tile([P, N], F32, name="sums", bufs=6)
             for a in range(2):
                 nc.tensor.matmul_mx(
                     out=hv[:], lhsT=v_codes[h][:, a, 2 * k * P : 2 * (k + 1) * P].bitcast(FP4X4), lhsT_scale=planes[a],
-                    rhs=wv_codes[:, a, :].bitcast(FP4X4), rhs_scale=wv_planes[:, a, :], start=(a == 0), stop=(a == 1),
+                    rhs=wv_codes[:, a, :].bitcast(FP4X4), rhs_scale=w_planes[:, (3 + a) * N : (4 + a) * N], start=(a == 0), stop=(a == 1),
                 )
-            av[h, k] = acts.tile([P, PACK, P], F32, name="av")
-            nc.scalar.activation(av[h, k][:], hv[:].rearrange("p (m t) -> p t m", t=PACK), ACT.Silu)
+            av = temp.tile([P, PACK, P], F32, name="av")
+            nc.scalar.activation(av[:], hv[:].rearrange("p (m t) -> p t m", t=PACK), ACT.Silu)
+            seen[block] = acts.tile([P, PACK, P], F32, name="seen")
+            nc.scalar.mul(seen[block][:], av[:], half_w[:, block : block + 1])
 
-        def text(h, k):
+        def text(block):
+            h, k = divmod(block, blocks)
             cols = slice(k * P, (k + 1) * P)
-            ht = psum.tile([P, N], F32, name="branch")
+            ht = psum.tile([P, N], F32, name="sums", bufs=6)
             nc.tensor.matmul_mx(
                 out=ht[:], lhsT=v2_codes[h][:, cols].bitcast(FP8X4), lhsT_scale=v2_scales[h][:, cols],
                 rhs=wt_codes[:].bitcast(FP8X4), rhs_scale=wt_scales[:], start=True, stop=True,
             )
             at = temp.tile([P, PACK, P], F32, name="at")
             nc.scalar.activation(at[:], ht[:].rearrange("p (m t) -> p t m", t=PACK), ACT.Silu)
-            neg_at[h, k] = acts.tile([P, PACK, P], F32, name="neg_at")
-            nc.scalar.mul(neg_at[h, k][:], at[:], -1.0)
+            said[block] = acts.tile([P, PACK, P], F32, name="said")
+            nc.scalar.mul(said[block][:], at[:], neg_half_w[:, block : block + 1])
 
-        def gate_sum(t, h):
-            planes = (v_scales[h][:], shifted[h][:])
-            z = psum.tile([P, HALF], F32, name="z")
+        def gate_sum(h, t):
+            planes = (v_scales[h], shifted[h])
+            z = psum.tile([P, HALF], F32, name="sums", bufs=6)
             for a in range(2):
                 nc.tensor.matmul_mx(
                     out=z[:], lhsT=z_codes[:, t, a, :].bitcast(FP4X4), lhsT_scale=z_planes[:, t, a * P : (a + 1) * P],
@@ -183,122 +189,75 @@ def tile_list_gmu_silu_scatP_kernel(
                 )
             nc.tensor.matmul_mx(
                 out=z[:], lhsT=z_codes[:, t, 2, :].bitcast(FP4X4), lhsT_scale=z_planes[:, t, 2 * P : 3 * P],
-                rhs=v2_codes[h][:].bitcast(FP8X4), rhs_scale=v2_scales[h], start=False, stop=True,
+                rhs=v2_codes[h][:].bitcast(FP8X4), rhs_scale=v2_scales[h][:], start=False, stop=True,
             )
-            th[t, h] = held([P, HALF], F32, "th%d%d" % (t, h))
-            nc.scalar.activation(th[t, h][:], z[:], ACT.Tanh, bias=half_bias[:, t : t + 1], scale=0.5)
+            nc.scalar.activation(th[h, t // 2][:, t % 2, :], z[:], ACT.Tanh, bias=half_bias[:, t : t + 1], scale=0.5)
 
-        def finish(t):
-            page = pages[t % PAGES]
-            nc.sync.dma_start(out_rows[:, t, :], page[:])
+        def combine(q, pair):
+            h, cols = q // 2, slice(q % 2 * QUARTER, (q % 2 + 1) * QUARTER)
+            back = psum.tile([P, 2, QUARTER], F32, name="sums", bufs=6)
+            diff = psum.tile([P, 2, QUARTER], F32, name="diff")
+            spots = [(i, k, 2 * q + k, 2 * pair + i) for i in range(2) for k in range(2)]
+            for i, k, block, t in spots:
+                nc.tensor.transpose(back[:, i, k * P : (k + 1) * P], said[block][:, t, :], ident[:])
+            for i, k, block, t in spots:
+                nc.tensor.matmul(diff[:, i, k * P : (k + 1) * P], seen[block][:, t, :], ident[:], start=True, stop=False, is_transpose=True)
+                nc.tensor.matmul(diff[:, i, k * P : (k + 1) * P], said[block][:, t, :], ident[:], start=False, stop=True, is_transpose=True)
+            nc.scalar.mul(base[h, pair][:, :, cols], back[:], -2.0)
+            nc.vector.scalar_tensor_tensor(gated[h, pair][:, :, cols], th[h, pair][:, :, cols], 1.0, diff[:], ALU.add, ALU.mult)
+
+        def place(t, first, count):
+            h, cols = first // HALF, slice(first % HALF, first % HALF + count)
+            window = pages[t][:].indirect(entries(list1, first, count))
+            nc.vector.tensor_tensor(window, gated[h, t // 2][:, t % 2, cols], base[h, t // 2][:, t % 2, cols], ALU.add)
+
+        for q in range(QUARTERS):
+            for branch in (text, picture) if q < 2 else (picture, text):
+                branch(2 * q)
+                branch(2 * q + 1)
+            for pair in range(2):
+                if q % 2 == 0:
+                    gate_sum(q // 2, 2 * pair)
+                    gate_sum(q // 2, 2 * pair + 1)
+                combine(q, pair)
+            for t in range(PACK - 1):
+                place(t, q * QUARTER, QUARTER)
+        pages.append(held([P, T], F32, "page3", "th10"))
+        nc.gpsimd.memset(pages[3][:], 0.0)
+        for h in range(HALVES):
+            place(PACK - 1, h * HALF, HALF)
+
+        paired = [held([P, 2, CHUNK, 2], BF16, "paired%d" % c) for c in range(CHUNKS)]
+        woven = [held([P, CHUNK, PACK], BF16, "woven%d" % c) for c in range(CHUNKS)]
+        y_codes = [held([P, CHUNK], U32, "y_codes%d" % c) for c in range(CHUNKS)]
+        y_scales = held([P, T], U8, "y_scales")
+        for t in range(PACK):
+            nc.sync.dma_start(out_rows[:, t, :], pages[t][:])
             for c in range(CHUNKS):
-                src = page[:, c * CHUNK : (c + 1) * CHUNK]
-                on_vector = c % 2 == 0
-                if t == PACK - 1 and on_vector:
-                    nc.vector.tensor_copy(woven[c][:, :, t], src)
-                elif t == PACK - 2 and on_vector:
-                    nc.scalar.copy(woven[c][:, :, t : t + 2], src.unsqueeze(2).to_broadcast([P, CHUNK, 2]))
+                src = pages[t][:, c * CHUNK : (c + 1) * CHUNK]
+                if t == PACK - 1 and c == 0:
+                    nc.vector.tensor_copy(paired[c][:, t // 2, :, t % 2], src)
+                elif t == PACK - 2 and c == 0:
+                    nc.scalar.copy(paired[c][:, t // 2, :, :], src.unsqueeze(2).to_broadcast([P, CHUNK, 2]))
                 else:
-                    nc.scalar.copy(woven[c][:, :, t], src)
+                    nc.scalar.copy(paired[c][:, t // 2, :, t % 2], src)
 
-        order = [(0, 0), (1, 0), (0, 1), (1, 1), (2, 0), (2, 1), (3, 0), (3, 1)]
-        units = len(order)
-        diff, back, twice, mixed, twice_at = {}, {}, {}, {}, {}
+        def weave(c):
+            engine_copy, word = (nc.scalar.copy, U32) if c == CHUNKS - 1 else (nc.vector.tensor_copy, I32)
+            words = paired[c][:].rearrange("p u c e -> p u (c e)").bitcast(word)
+            engine_copy(woven[c][:].bitcast(word), words.rearrange("p u c -> p c u"))
 
-        def turn_diff(u):
-            if u < units:
-                t, h = order[u]
-                diff[u] = psum.tile([P, HALF], F32, name="diff")
-                for k in range(blocks):
-                    cols = slice(k * P, (k + 1) * P)
-                    nc.tensor.matmul(diff[u][:, cols], av[h, k][:, t, :], ident[:], start=True, stop=False, is_transpose=True)
-                    nc.tensor.matmul(diff[u][:, cols], neg_at[h, k][:, t, :], ident[:], start=False, stop=True, is_transpose=True)
-
-        def turn_back(u):
-            t, h = order[u]
-            back[u] = psum.tile([P, HALF], F32, name="back" if u < LEAD else "branch")
-            for k in range(blocks):
-                nc.tensor.transpose(back[u][:, k * P : (k + 1) * P], neg_at[h, k][:, t, :], ident[:])
-            if u >= LEAD:
-                twice_at[u] = acts.tile([P, HALF], F32, name="twice_at")
-                nc.scalar.mul(twice_at[u][:], back[u][:], -2.0)
-
-        def gate(u):
-            if u < units:
-                t, h = order[u]
-                twice[u] = work.tile([P, HALF], F32, name="twice")
-                nc.vector.scalar_tensor_tensor(twice[u][:], th[t, h][:], 1.0, diff[u][:], ALU.add, ALU.mult)
-
-        def mix(u):
-            if u < LEAD:
-                mixed[u] = work.tile([P, HALF], F32, name="mixed")
-                nc.vector.scalar_tensor_tensor(mixed[u][:], twice[u][:], 0.5, back[u][:], ALU.mult, ALU.subtract)
-            elif u < units:
-                h = order[u][1]
-                total = temp.tile([P, HALF], F32, name="total")
-                nc.gpsimd.tensor_tensor(total[:], twice[u][:], twice_at[u][:], ALU.add)
-                mixed[u] = work.tile([P, HALF], F32, name="mixed")
-                nc.gpsimd.tensor_tensor(mixed[u][:], total[:], half_weight[:, h * HALF : (h + 1) * HALF], ALU.mult)
-
-        def place(u):
-            t, h = order[u]
-            window = pages[t % PAGES][:].indirect(list1[:, h * HALF // 16 : (h + 1) * HALF // 16])
-            if u < LEAD - 1:
-                nc.vector.tensor_tensor(window, mixed[u][:], weight[:, h * HALF : (h + 1) * HALF], ALU.mult)
-            elif u == LEAD - 1:
-                weighed = held([P, HALF], F32, "weighed", "th%d%d" % order[LEAD])
-                nc.vector.tensor_tensor(weighed[:], mixed[u][:], weight[:, h * HALF : (h + 1) * HALF], ALU.mult)
-                nc.vector.tensor_copy(window, weighed[:])
-            else:
-                nc.vector.tensor_copy(window, mixed[u][:])
-            if h == HALVES - 1:
-                finish(t)
-
-        half_weight = held([P, J], F32, "half_weight")
-        nc.gpsimd.tensor_scalar(half_weight[:], weight[:], 0.5, 0.0, ALU.mult, ALU.add)
-        for k in range(blocks):
-            text(0, k)
-        for k in range(blocks):
-            picture(0, k)
-        for u in range(2):
-            gate_sum(*order[u])
-            turn_diff(u)
-            turn_back(u)
-        for k in range(blocks):
-            picture(1, k)
-        for k in range(blocks):
-            text(1, k)
-        gate(0)
-        gate(1)
-        mix(0)
-        mix(1)
-        place(0)
-        place(1)
-        for u in range(2, units):
-            gate_sum(*order[u])
-            if u < LEAD:
-                turn_diff(u)
-            turn_back(u)
-        woven = [held([P, CHUNK, PACK], BF16, "woven%d" % c, tag) for c, tag in enumerate(("z_codes", "v_codes1", "tab2_s", "z_planes"))]
-        gate(2)
-        gate(3)
-        mix(2)
-        place(2)
-        turn_diff(4)
-        gate(4)
-        mix(3)
-        mix(4)
-        for u in range(3, units):
-            turn_diff(u + 2)
-            gate(u + 2)
-            place(u)
-            mix(u + 2)
-
-        for c in range(CHUNKS):
+        def quantize(c):
             nc.vector.quantize_mx(
                 out=y_codes[c][:].bitcast(FP8X4), scales=y_scales[:, c * CHUNK : (c + 1) * CHUNK],
                 in_=woven[c][:].rearrange("p c t -> p (c t)"),
             )
             nc.sync.dma_start(out_words[:, c * CHUNK : (c + 1) * CHUNK], y_codes[c][:].bitcast(I32))
+
+        weave(0)
+        for c in range(CHUNKS):
+            if c + 1 < CHUNKS:
+                weave(c + 1)
+            quantize(c)
         for q in range(4):
             nc.scalar.dma_start(out_2[0, 4 * q : 4 * q + 4, :].bitcast(I32), y_scales[32 * q : 32 * q + 4, :].bitcast(I32))

@@ -35,7 +35,7 @@ def tile_list_gmu_silu_scatP_kernel(
     with ExitStack() as ctx:
         keep = ctx.enter_context(tc.tile_pool(name="keep", bufs=1))
         reuse = ctx.enter_context(tc.tile_pool(name="reuse", bufs=1))
-        acts = ctx.enter_context(tc.tile_pool(name="acts", bufs=4))
+        acts = ctx.enter_context(tc.tile_pool(name="acts", bufs=6))
         temp = ctx.enter_context(tc.tile_pool(name="temp", bufs=2))
         psum = ctx.enter_context(tc.psum_pool(name="psum", bufs=2))
 
@@ -56,43 +56,46 @@ def tile_list_gmu_silu_scatP_kernel(
         w_planes = held([P, 5 * N], U8, "w_planes")
         shifted_all = held([P, J], U8, "shifted")
         shifted = [shifted_all[:, h * HALF : (h + 1) * HALF] for h in range(HALVES)]
-        for tile in [tab_s[:], z_scales_raw[:], w_planes[:, 3 * N :], tab2_s[:], shifted_all[:]]:
+        for tile in (tab_s, tab2_s):
+            nc.gpsimd.memset(tile[:].bitcast(I32), 0)
+        for tile in [z_scales_raw[:], w_planes[:, 3 * N :], shifted_all[:]]:
             nc.vector.memset(tile.bitcast(I32), 0)
-        pages = [held([P, T], F32, "page%d" % t) for t in range(2)]
         w_rows = held([P, P], F32, "w_rows")
-        nc.gpsimd.memset(w_rows[:], 0.0)
+        nc.vector.memset(w_rows[:], 0.0)
         ident = held([P, P], F32, "ident")
         make_identity(nc, ident[:])
+        pages = [held([P, T], F32, "page%d" % t) for t in range(2)]
         for page in pages:
             nc.gpsimd.memset(page[:], 0.0)
 
         nc.sync.dma_start(list1[:], offs)
-        wt_raw = held([P, PACK, N], F32, "wt_raw")
-        nc.sync.dma_start(wt_raw[:], wt.rearrange("(p i) n -> p i n", i=PACK))
+        nc.sync.dma_start(list2[:], offs2)
         for q in range(4):
             nc.sync.dma_start(tab_s[32 * q : 32 * q + 8, :].bitcast(I32), tab_scales[:, 4 * q : 4 * q + 4, :].bitcast(I32))
+        nc.sync.dma_start(tab2_s[0:4, :].bitcast(I32), tab2_scales[0, 0:4, :].bitcast(I32))
+        wt_raw = held([P, PACK, N], F32, "wt_raw")
+        nc.sync.dma_start(wt_raw[:], wt.rearrange("(p i) n -> p i n", i=PACK))
+        for q in range(1, 4):
+            nc.sync.dma_start(tab2_s[32 * q : 32 * q + 4, :].bitcast(I32), tab2_scales[0, 4 * q : 4 * q + 4, :].bitcast(I32))
         for first, scales in ((0, zv_scales), (2, zt_scales)):
             passes = scales.shape[0]
             nc.sync.dma_start(
                 z_scales_raw[0:P:8, first * N : (first + passes) * N].bitcast(I32).rearrange("q (a n) -> q a n", a=passes),
                 scales.rearrange("a q n -> q a n").bitcast(I32),
             )
-        nc.sync.dma_start(list2[:], offs2)
-        tab2_w = held([P, T], I32, "tab2_w")
-        nc.sync.dma_start(tab2_w[:], tab2_words[0].rearrange("p t b -> p (t b)").bitcast(I32))
         nc.sync.dma_start(
             w_planes[0:P:8, 3 * N :].bitcast(I32).rearrange("q (a n) -> q a n", a=2),
             wv_scales.rearrange("a q n -> q a n").bitcast(I32),
         )
-        for q in range(4):
-            nc.sync.dma_start(tab2_s[32 * q : 32 * q + 4, :].bitcast(I32), tab2_scales[0, 4 * q : 4 * q + 4, :].bitcast(I32))
+        tab2_w = held([P, T], I32, "tab2_w")
+        nc.sync.dma_start(tab2_w[:], tab2_words[0].rearrange("p t b -> p (t b)").bitcast(I32))
+        nc.sync.dma_start(w_rows[0 : J // P, :], wgo[0].rearrange("(k p) -> k p", p=P))
         tab_w = held([P, T], I32, "tab_w")
         nc.sync.dma_start(tab_w[:], tab_words[0].rearrange("p t b -> p (t b)").bitcast(I32))
-        nc.sync.dma_start(w_rows[0 : J // P, :], wgo[0].rearrange("(k p) -> k p", p=P))
 
         wt_bf = held([P, N, PACK], BF16, "wt_bf")
         nc.scalar.copy(wt_bf[:], wt_raw[:].rearrange("p i n -> p n i"))
-        w_turned = psum.tile([P, P], F32, name="sums", bufs=6)
+        w_turned = psum.tile([P, P], F32, name="sums", bufs=5)
         nc.tensor.transpose(w_turned[:], w_rows[:], ident[:])
         half_w = held([P, J // P], F32, "half_w")
         nc.scalar.mul(half_w[:], w_turned[:, 0 : J // P], 0.5)
@@ -139,9 +142,10 @@ def tile_list_gmu_silu_scatP_kernel(
         v2_scales.append(gather(placed([P, HALF], U8, "v2_scales1", HALF), tab2_s[:], list2, 1))
         v_codes.append(part_v(1, pairs1))
         v2_codes.append(gather(placed([P, HALF], U32, "v2_codes1", 2 * HALF), tab2_w[:].bitcast(U32), list2, 1))
-        pages.append(held([P, T], F32, "page2", "tab_w"))
-        for c in range(CHUNKS):
-            nc.gpsimd.memset(pages[2][:, c * CHUNK : (c + 1) * CHUNK], 0.0)
+        for t, tag in ((2, "tab_w"), (3, "tab2_w")):
+            pages.append(held([P, T], F32, "page%d" % t, tag))
+            for c in range(CHUNKS):
+                nc.gpsimd.memset(pages[t][:, c * CHUNK : (c + 1) * CHUNK], 0.0)
 
         out_rows = out_0.rearrange("(p t) c -> p t c", t=PACK)
         out_words = out_1[0].rearrange("p t b -> p (t b)").bitcast(I32)
@@ -155,7 +159,7 @@ def tile_list_gmu_silu_scatP_kernel(
             h, k = divmod(block, blocks)
             cols = slice(k * P, (k + 1) * P)
             planes = (v_scales[h][:, cols], shifted[h][:, cols])
-            hv = psum.tile([P, N], F32, name="sums", bufs=6)
+            hv = psum.tile([P, N], F32, name="sums", bufs=5)
             for a in range(2):
                 nc.tensor.matmul_mx(
                     out=hv[:], lhsT=v_codes[h][:, a, 2 * k * P : 2 * (k + 1) * P].bitcast(FP4X4), lhsT_scale=planes[a],
@@ -169,7 +173,7 @@ def tile_list_gmu_silu_scatP_kernel(
         def text(block):
             h, k = divmod(block, blocks)
             cols = slice(k * P, (k + 1) * P)
-            ht = psum.tile([P, N], F32, name="sums", bufs=6)
+            ht = psum.tile([P, N], F32, name="sums", bufs=5)
             nc.tensor.matmul_mx(
                 out=ht[:], lhsT=v2_codes[h][:, cols].bitcast(FP8X4), lhsT_scale=v2_scales[h][:, cols],
                 rhs=wt_codes[:].bitcast(FP8X4), rhs_scale=wt_scales[:], start=True, stop=True,
@@ -181,7 +185,7 @@ def tile_list_gmu_silu_scatP_kernel(
 
         def gate_sum(h, t):
             planes = (v_scales[h], shifted[h])
-            z = psum.tile([P, HALF], F32, name="sums", bufs=6)
+            z = psum.tile([P, HALF], F32, name="sums", bufs=5)
             for a in range(2):
                 nc.tensor.matmul_mx(
                     out=z[:], lhsT=z_codes[:, t, a, :].bitcast(FP4X4), lhsT_scale=z_planes[:, t, a * P : (a + 1) * P],
@@ -195,8 +199,8 @@ def tile_list_gmu_silu_scatP_kernel(
 
         def combine(q, pair):
             h, cols = q // 2, slice(q % 2 * QUARTER, (q % 2 + 1) * QUARTER)
-            back = psum.tile([P, 2, QUARTER], F32, name="sums", bufs=6)
-            diff = psum.tile([P, 2, QUARTER], F32, name="diff")
+            back = psum.tile([P, 2, QUARTER], F32, name="sums", bufs=5)
+            diff = psum.tile([P, 2, QUARTER], F32, name="diff", bufs=3)
             spots = [(i, k, 2 * q + k, 2 * pair + i) for i in range(2) for k in range(2)]
             for i, k, block, t in spots:
                 nc.tensor.transpose(back[:, i, k * P : (k + 1) * P], said[block][:, t, :], ident[:])
@@ -215,17 +219,19 @@ def tile_list_gmu_silu_scatP_kernel(
             for branch in (text, picture) if q < 2 else (picture, text):
                 branch(2 * q)
                 branch(2 * q + 1)
-            for pair in range(2):
+            for pair in range(2 if q < 2 else 1):
                 if q % 2 == 0:
                     gate_sum(q // 2, 2 * pair)
                     gate_sum(q // 2, 2 * pair + 1)
                 combine(q, pair)
-            for t in range(PACK - 1):
+            for t in range(PACK if q < 2 else 2):
                 place(t, q * QUARTER, QUARTER)
-        pages.append(held([P, T], F32, "page3", "th10"))
-        nc.gpsimd.memset(pages[3][:], 0.0)
-        for h in range(HALVES):
-            place(PACK - 1, h * HALF, HALF)
+        gate_sum(1, 2)
+        gate_sum(1, 3)
+        combine(2, 1)
+        combine(3, 1)
+        for t in range(2, PACK):
+            place(t, HALF, HALF)
 
         paired = [held([P, 2, CHUNK, 2], BF16, "paired%d" % c) for c in range(CHUNKS)]
         woven = [held([P, CHUNK, PACK], BF16, "woven%d" % c) for c in range(CHUNKS)]

@@ -66,7 +66,7 @@ def tile_list_gmu_silu_scatP_kernel(
         make_identity(nc, ident[:])
         pages = [held([P, T], F32, "page%d" % t) for t in range(2)]
         for page in pages:
-            nc.gpsimd.memset(page[:], 0.0)
+            nc.vector.memset(page[:].bitcast(I32), 0)
 
         nc.sync.dma_start(list1[:], offs)
         nc.sync.dma_start(list2[:], offs2)
@@ -139,10 +139,10 @@ def tile_list_gmu_silu_scatP_kernel(
         z_codes = held([P, PACK, 3, 2 * P], U8, "z_codes")
         nc.vector.tensor_copy(z_codes[:].bitcast(U16), z_words[:].bitcast(U16).rearrange("p a (m t) -> p t a m", t=PACK))
         pairs1 = gather(placed([P, HALF], U32, "pairs1", 2 * HALF), tab_w[:].bitcast(U32), list1, 1)
-        v2_scales.append(gather(placed([P, HALF], U8, "v2_scales1", HALF), tab2_s[:], list2, 1))
         v_codes.append(part_v(1, pairs1))
-        v2_codes.append(gather(placed([P, HALF], U32, "v2_codes1", 2 * HALF), tab2_w[:].bitcast(U32), list2, 1))
-        for t, tag in ((2, "tab_w"), (3, "tab2_w")):
+        v2_codes.append(gather(placed([P, HALF], U32, "v2_codes1", 3 * HALF), tab2_w[:].bitcast(U32), list2, 1))
+        v2_scales.append(gather(placed([P, HALF], U8, "v2_scales1", 2 * HALF), tab2_s[:], list2, 1))
+        for t, tag in ((2, "tab2_w"), (3, "tab2_s")):
             pages.append(held([P, T], F32, "page%d" % t, tag))
             for c in range(CHUNKS):
                 nc.gpsimd.memset(pages[t][:, c * CHUNK : (c + 1) * CHUNK], 0.0)
@@ -241,9 +241,9 @@ def tile_list_gmu_silu_scatP_kernel(
             nc.sync.dma_start(out_rows[:, t, :], pages[t][:])
             for c in range(CHUNKS):
                 src = pages[t][:, c * CHUNK : (c + 1) * CHUNK]
-                if t == PACK - 1 and c == 0:
+                if t == PACK - 1 and c < 2:
                     nc.vector.tensor_copy(paired[c][:, t // 2, :, t % 2], src)
-                elif t == PACK - 2 and c == 0:
+                elif t == PACK - 2 and c < 2:
                     nc.scalar.copy(paired[c][:, t // 2, :, :], src.unsqueeze(2).to_broadcast([P, CHUNK, 2]))
                 else:
                     nc.scalar.copy(paired[c][:, t // 2, :, t % 2], src)

@@ -64,14 +64,13 @@ def tile_list_gmu_silu_scatP_kernel(
         nc.vector.memset(w_rows[:], 0.0)
         ident = held([P, P], F32, "ident")
         make_identity(nc, ident[:])
-        pages = [held([P, T], F32, "page%d" % t) for t in range(2)]
-        for page in pages:
-            nc.vector.memset(page[:].bitcast(I32), 0)
+        pages = [held([P, T], F32, "page0")]
+        nc.vector.memset(pages[0][:].bitcast(I32), 0)
 
         nc.sync.dma_start(list1[:], offs)
         nc.sync.dma_start(list2[:], offs2)
-        for q in range(4):
-            nc.sync.dma_start(tab_s[32 * q : 32 * q + 8, :].bitcast(I32), tab_scales[:, 4 * q : 4 * q + 4, :].bitcast(I32))
+        for r in range(4):
+            nc.sync.dma_start(tab_s[r:P:16, :].bitcast(I32), tab_scales[:, r:16:4, :].rearrange("a q n -> q a n").bitcast(I32))
         nc.sync.dma_start(tab2_s[0:4, :].bitcast(I32), tab2_scales[0, 0:4, :].bitcast(I32))
         wt_raw = held([P, PACK, N], F32, "wt_raw")
         nc.sync.dma_start(wt_raw[:], wt.rearrange("(p i) n -> p i n", i=PACK))
@@ -116,17 +115,17 @@ def tile_list_gmu_silu_scatP_kernel(
         picked = held([P, J], U8, "v_scales")
         nc.vector.tensor_copy(picked[:], tab_s[:].indirect(list1[:]))
         v_scales = [picked[:, h * HALF : (h + 1) * HALF] for h in range(HALVES)]
-        nc.sync.dma_start(shifted_all[0:100, :].bitcast(I32), picked[4:104, :].bitcast(I32))
+        nc.sync.dma_start(shifted_all[0:100, :].bitcast(I32), picked[16:116, :].bitcast(I32))
         z_planes = w_planes[:, 0 : 3 * N].rearrange("p (t m) -> p t m", t=PACK)
         nc.vector.tensor_copy(z_planes, z_scales_raw[:].rearrange("p (m t) -> p t m", t=PACK))
         flat_scales = w_planes[:].bitcast(I32)
         for r in range(1, 4):
             nc.sync.dma_start(flat_scales[r:P:32, :], flat_scales[8 * r : P : 32, :])
-        wv_codes = held([P, 2, 2 * N], U8, "wv_codes")
-        nc.sync.dma_start(wv_codes[:].bitcast(I32), wv_words.rearrange("a p c -> p a c").bitcast(I32))
         z_words = placed([P, 3, 2 * N], U8, "z_words", 0)
         for first, words in ((0, zv_words), (2, zt_words)):
             nc.sync.dma_start(z_words[:, first : first + words.shape[0], :].bitcast(I32), words.rearrange("a p c -> p a c").bitcast(I32))
+        wv_codes = held([P, 2, 2 * N], U8, "wv_codes")
+        nc.sync.dma_start(wv_codes[:].bitcast(I32), wv_words.rearrange("a p c -> p a c").bitcast(I32))
         bias = held([P, PACK], F32, "bias")
         nc.sync.dma_start(bias[:], b.rearrange("(p t) -> p t", t=PACK))
         half_bias = held([P, PACK], F32, "half_bias")
@@ -140,12 +139,13 @@ def tile_list_gmu_silu_scatP_kernel(
         nc.vector.tensor_copy(z_codes[:].bitcast(U16), z_words[:].bitcast(U16).rearrange("p a (m t) -> p t a m", t=PACK))
         pairs1 = gather(placed([P, HALF], U32, "pairs1", 2 * HALF), tab_w[:].bitcast(U32), list1, 1)
         v_codes.append(part_v(1, pairs1))
-        v2_codes.append(gather(placed([P, HALF], U32, "v2_codes1", 3 * HALF), tab2_w[:].bitcast(U32), list2, 1))
-        v2_scales.append(gather(placed([P, HALF], U8, "v2_scales1", 2 * HALF), tab2_s[:], list2, 1))
-        for t, tag in ((2, "tab2_w"), (3, "tab2_s")):
-            pages.append(held([P, T], F32, "page%d" % t, tag))
-            for c in range(CHUNKS):
-                nc.gpsimd.memset(pages[t][:, c * CHUNK : (c + 1) * CHUNK], 0.0)
+        v2_codes.append(gather(placed([P, HALF], U32, "v2_codes1", 0), tab2_w[:].bitcast(U32), list2, 1))
+        v2_scales.append(gather(placed([P, HALF], U8, "v2_scales1", 4 * HALF), tab2_s[:], list2, 1))
+        pages.append(placed([P, T], F32, "page1", 5 * HALF))
+        pages.append(held([P, T], F32, "page2", "tab2_w"))
+        pages.append(held([P, T], F32, "page3", "tab2_s"))
+        for page in pages[1:]:
+            nc.gpsimd.memset(page[:], 0.0)
 
         out_rows = out_0.rearrange("(p t) c -> p t c", t=PACK)
         out_words = out_1[0].rearrange("p t b -> p (t b)").bitcast(I32)

@@ -24,6 +24,7 @@ HALVES = J // HALF
 CHUNK = 512
 CHUNKS = T // CHUNK
 QUARTER = 256
+PAIRS_AT = 5 * HALF + 4 * T - 2 * HALF
 QUARTERS = J // QUARTER
 
 
@@ -121,9 +122,10 @@ def tile_list_gmu_silu_scatP_kernel(
         flat_scales = w_planes[:].bitcast(I32)
         for r in range(1, 4):
             nc.sync.dma_start(flat_scales[r:P:32, :], flat_scales[8 * r : P : 32, :])
-        z_words = placed([P, 3, 2 * N], U8, "z_words", 0)
-        for first, words in ((0, zv_words), (2, zt_words)):
-            nc.sync.dma_start(z_words[:, first : first + words.shape[0], :].bitcast(I32), words.rearrange("a p c -> p a c").bitcast(I32))
+        zv_raw = placed([P, 2, 2 * N], U8, "zv_raw", PAIRS_AT)
+        zt_raw = placed([P, 1, 2 * N], U8, "zt_raw", 0)
+        for raw, words in ((zv_raw, zv_words), (zt_raw, zt_words)):
+            nc.sync.dma_start(raw[:].bitcast(I32), words.rearrange("a p c -> p a c").bitcast(I32))
         wv_codes = held([P, 2, 2 * N], U8, "wv_codes")
         nc.sync.dma_start(wv_codes[:].bitcast(I32), wv_words.rearrange("a p c -> p a c").bitcast(I32))
         bias = held([P, PACK], F32, "bias")
@@ -136,16 +138,15 @@ def tile_list_gmu_silu_scatP_kernel(
         pairs0 = gather(held([P, HALF], U32, "pairs0"), tab_w[:].bitcast(U32), list1, 0)
         v_codes = [part_v(0, pairs0)]
         z_codes = held([P, PACK, 3, 2 * P], U8, "z_codes")
-        nc.vector.tensor_copy(z_codes[:].bitcast(U16), z_words[:].bitcast(U16).rearrange("p a (m t) -> p t a m", t=PACK))
-        pairs1 = gather(placed([P, HALF], U32, "pairs1", 2 * HALF), tab_w[:].bitcast(U32), list1, 1)
+        for raw, passes in ((zv_raw, slice(0, 2)), (zt_raw, slice(2, 3))):
+            nc.vector.tensor_copy(z_codes[:, :, passes, :].bitcast(U16), raw[:].bitcast(U16).rearrange("p a (m t) -> p t a m", t=PACK))
+        v2_codes.append(gather(placed([P, HALF], U32, "v2_codes1", HALF), tab2_w[:].bitcast(U32), list2, 1))
+        v2_scales.append(gather(placed([P, HALF], U8, "v2_scales1", 0), tab2_s[:], list2, 1))
+        pairs1 = gather(placed([P, HALF], U32, "pairs1", PAIRS_AT), tab_w[:].bitcast(U32), list1, 1)
         v_codes.append(part_v(1, pairs1))
-        v2_codes.append(gather(placed([P, HALF], U32, "v2_codes1", 0), tab2_w[:].bitcast(U32), list2, 1))
-        v2_scales.append(gather(placed([P, HALF], U8, "v2_scales1", 4 * HALF), tab2_s[:], list2, 1))
-        pages.append(placed([P, T], F32, "page1", 5 * HALF))
-        pages.append(held([P, T], F32, "page2", "tab2_w"))
-        pages.append(held([P, T], F32, "page3", "tab2_s"))
-        for page in pages[1:]:
-            nc.gpsimd.memset(page[:], 0.0)
+        for t, offset in ((1, PAIRS_AT + 2 * HALF - 4 * T), (2, PAIRS_AT + 2 * HALF)):
+            pages.append(placed([P, T], F32, "page%d" % t, offset))
+            nc.gpsimd.memset(pages[t][:], 0.0)
 
         out_rows = out_0.rearrange("(p t) c -> p t c", t=PACK)
         out_words = out_1[0].rearrange("p t b -> p (t b)").bitcast(I32)
@@ -167,8 +168,12 @@ def tile_list_gmu_silu_scatP_kernel(
                 )
             av = temp.tile([P, PACK, P], F32, name="av")
             nc.scalar.activation(av[:], hv[:].rearrange("p (m t) -> p t m", t=PACK), ACT.Silu)
-            seen[block] = acts.tile([P, PACK, P], F32, name="seen")
-            nc.scalar.mul(seen[block][:], av[:], half_w[:, block : block + 1])
+            if block < 2:
+                seen[block] = held([P, PACK, P], F32, "seen%d" % block, ("seen0", "page3")[block])
+                nc.scalar.mul(seen[block][:], av[:], half_w[:, block : block + 1])
+            else:
+                seen[block] = acts.tile([P, PACK, P], F32, name="seen")
+                nc.scalar.mul(seen[block][:], av[:], half_w[:, block : block + 1])
 
         def text(block):
             h, k = divmod(block, blocks)
@@ -216,7 +221,7 @@ def tile_list_gmu_silu_scatP_kernel(
             nc.vector.tensor_tensor(window, gated[h, t // 2][:, t % 2, cols], base[h, t // 2][:, t % 2, cols], ALU.add)
 
         for q in range(QUARTERS):
-            for branch in (text, picture) if q < 2 else (picture, text):
+            for branch in (text, picture):
                 branch(2 * q)
                 branch(2 * q + 1)
             for pair in range(2 if q < 2 else 1):
@@ -224,6 +229,9 @@ def tile_list_gmu_silu_scatP_kernel(
                     gate_sum(q // 2, 2 * pair)
                     gate_sum(q // 2, 2 * pair + 1)
                 combine(q, pair)
+            if q == 0:
+                pages.append(held([P, T], F32, "page3"))
+                nc.gpsimd.memset(pages[3][:], 0.0)
             for t in range(PACK if q < 2 else 2):
                 place(t, q * QUARTER, QUARTER)
         gate_sum(1, 2)

@@ -117,8 +117,11 @@ def tile_list_gmu_silu_scatP_kernel(
         nc.vector.tensor_copy(picked[:], tab_s[:].indirect(list1[:]))
         v_scales = [picked[:, h * HALF : (h + 1) * HALF] for h in range(HALVES)]
         nc.sync.dma_start(shifted_all[0:100, :].bitcast(I32), picked[16:116, :].bitcast(I32))
+        picked2 = held([P, J], U8, "v2_scales")
+        nc.vector.tensor_copy(picked2[:], tab2_s[:].indirect(list2[:]))
+        v2_scales = [picked2[:, h * HALF : (h + 1) * HALF] for h in range(HALVES)]
         z_planes = w_planes[:, 0 : 3 * N].rearrange("p (t m) -> p t m", t=PACK)
-        nc.vector.tensor_copy(z_planes, z_scales_raw[:].rearrange("p (m t) -> p t m", t=PACK))
+        nc.gpsimd.tensor_copy(z_planes, z_scales_raw[:].rearrange("p (m t) -> p t m", t=PACK))
         flat_scales = w_planes[:].bitcast(I32)
         for r in range(1, 4):
             nc.sync.dma_start(flat_scales[r:P:32, :], flat_scales[8 * r : P : 32, :])
@@ -133,7 +136,6 @@ def tile_list_gmu_silu_scatP_kernel(
         half_bias = held([P, PACK], F32, "half_bias")
         nc.scalar.mul(half_bias[:], bias[:], 0.5)
         nc.vector.quantize_mx(out=wt_codes[:].bitcast(FP8X4), scales=wt_scales[:], in_=wt_bf[:].rearrange("p n i -> p (n i)"))
-        v2_scales = [gather(held([P, HALF], U8, "v2_scales0"), tab2_s[:], list2, 0)]
         v2_codes = [gather(held([P, HALF], U32, "v2_codes0"), tab2_w[:].bitcast(U32), list2, 0)]
         pairs0 = gather(held([P, HALF], U32, "pairs0"), tab_w[:].bitcast(U32), list1, 0)
         v_codes = [part_v(0, pairs0)]
@@ -141,7 +143,6 @@ def tile_list_gmu_silu_scatP_kernel(
         for raw, passes in ((zv_raw, slice(0, 2)), (zt_raw, slice(2, 3))):
             nc.vector.tensor_copy(z_codes[:, :, passes, :].bitcast(U16), raw[:].bitcast(U16).rearrange("p a (m t) -> p t a m", t=PACK))
         v2_codes.append(gather(placed([P, HALF], U32, "v2_codes1", HALF), tab2_w[:].bitcast(U32), list2, 1))
-        v2_scales.append(gather(placed([P, HALF], U8, "v2_scales1", 0), tab2_s[:], list2, 1))
         pairs1 = gather(placed([P, HALF], U32, "pairs1", PAIRS_AT), tab_w[:].bitcast(U32), list1, 1)
         v_codes.append(part_v(1, pairs1))
         for t, offset in ((1, PAIRS_AT + 2 * HALF - 4 * T), (2, PAIRS_AT + 2 * HALF)):
@@ -198,7 +199,7 @@ def tile_list_gmu_silu_scatP_kernel(
                 )
             nc.tensor.matmul_mx(
                 out=z[:], lhsT=z_codes[:, t, 2, :].bitcast(FP4X4), lhsT_scale=z_planes[:, t, 2 * P : 3 * P],
-                rhs=v2_codes[h][:].bitcast(FP8X4), rhs_scale=v2_scales[h][:], start=False, stop=True,
+                rhs=v2_codes[h][:].bitcast(FP8X4), rhs_scale=v2_scales[h], start=False, stop=True,
             )
             nc.scalar.activation(th[h, t // 2][:, t % 2, :], z[:], ACT.Tanh, bias=half_bias[:, t : t + 1], scale=0.5)
 

@@ -184,10 +184,18 @@ def tile_list_gmu_silu_scatP_kernel(
                 out=ht[:], lhsT=v2_codes[h][:, cols].bitcast(FP8X4), lhsT_scale=v2_scales[h][:, cols],
                 rhs=wt_codes[:].bitcast(FP8X4), rhs_scale=wt_scales[:], start=True, stop=True,
             )
-            at = temp.tile([P, PACK, P], F32, name="at")
+            at = temp.tile([P, PACK, P], F32, name="at", bufs=4)
             nc.scalar.activation(at[:], ht[:].rearrange("p (m t) -> p t m", t=PACK), ACT.Silu)
             said[block] = acts.tile([P, PACK, P], F32, name="said")
-            nc.scalar.mul(said[block][:], at[:], neg_half_w[:, block : block + 1])
+            if block < blocks:
+                nc.gpsimd.tensor_scalar(said[block][:], at[:], neg_half_w[:, block : block + 1], 0.0, ALU.mult, ALU.add)
+            else:
+                nc.scalar.mul(said[block][:], at[:], neg_half_w[:, block : block + 1])
+
+        first_sums = {}
+
+        def gate_tanh(z, h, t, cols):
+            nc.scalar.activation(th[h, t // 2][:, t % 2, cols], z[:, cols], ACT.Tanh, bias=half_bias[:, t : t + 1], scale=0.5)
 
         def gate_sum(h, t):
             planes = (v_scales[h], shifted[h])
@@ -201,7 +209,11 @@ def tile_list_gmu_silu_scatP_kernel(
                 out=z[:], lhsT=z_codes[:, t, 2, :].bitcast(FP4X4), lhsT_scale=z_planes[:, t, 2 * P : 3 * P],
                 rhs=v2_codes[h][:].bitcast(FP8X4), rhs_scale=v2_scales[h], start=False, stop=True,
             )
-            nc.scalar.activation(th[h, t // 2][:, t % 2, :], z[:], ACT.Tanh, bias=half_bias[:, t : t + 1], scale=0.5)
+            if (h, t // 2) == (0, 0):
+                first_sums[t] = z
+                gate_tanh(z, h, t, slice(0, QUARTER))
+            else:
+                gate_tanh(z, h, t, slice(0, HALF))
 
         def combine(q, pair):
             h, cols = q // 2, slice(q % 2 * QUARTER, (q % 2 + 1) * QUARTER)
@@ -221,8 +233,10 @@ def tile_list_gmu_silu_scatP_kernel(
             window = pages[t][:].indirect(entries(list1, first, count))
             nc.vector.tensor_tensor(window, gated[h, t // 2][:, t % 2, cols], base[h, t // 2][:, t % 2, cols], ALU.add)
 
+        for block in range(blocks):
+            text(block)
         for q in range(QUARTERS):
-            for branch in (text, picture):
+            for branch in (text, picture) if q >= 2 else (picture,):
                 branch(2 * q)
                 branch(2 * q + 1)
             for pair in range(2 if q < 2 else 1):
@@ -230,6 +244,9 @@ def tile_list_gmu_silu_scatP_kernel(
                     gate_sum(q // 2, 2 * pair)
                     gate_sum(q // 2, 2 * pair + 1)
                 combine(q, pair)
+                if (q, pair) == (0, 0):
+                    for t in range(2):
+                        gate_tanh(first_sums[t], 0, t, slice(QUARTER, HALF))
             if q == 0:
                 pages.append(held([P, T], F32, "page3"))
                 nc.gpsimd.memset(pages[3][:], 0.0)

@@ -125,20 +125,25 @@ def tile_list_gmu_silu_scatP_kernel(
         flat_scales = w_planes[:].bitcast(I32)
         for r in range(1, 4):
             nc.sync.dma_start(flat_scales[r:P:32, :], flat_scales[8 * r : P : 32, :])
+        wv_codes = held([P, 2, 2 * N], U8, "wv_codes")
+        nc.sync.dma_start(wv_codes[:].bitcast(I32), wv_words.rearrange("a p c -> p a c").bitcast(I32))
         zv_raw = placed([P, 2, 2 * N], U8, "zv_raw", PAIRS_AT)
         zt_raw = placed([P, 1, 2 * N], U8, "zt_raw", 0)
         for raw, words in ((zv_raw, zv_words), (zt_raw, zt_words)):
             nc.sync.dma_start(raw[:].bitcast(I32), words.rearrange("a p c -> p a c").bitcast(I32))
-        wv_codes = held([P, 2, 2 * N], U8, "wv_codes")
-        nc.sync.dma_start(wv_codes[:].bitcast(I32), wv_words.rearrange("a p c -> p a c").bitcast(I32))
         bias = held([P, PACK], F32, "bias")
         nc.sync.dma_start(bias[:], b.rearrange("(p t) -> p t", t=PACK))
         half_bias = held([P, PACK], F32, "half_bias")
         nc.scalar.mul(half_bias[:], bias[:], 0.5)
         nc.vector.quantize_mx(out=wt_codes[:].bitcast(FP8X4), scales=wt_scales[:], in_=wt_bf[:].rearrange("p n i -> p (n i)"))
         v2_codes = [gather(held([P, HALF], U32, "v2_codes0"), tab2_w[:].bitcast(U32), list2, 0)]
-        pairs0 = gather(held([P, HALF], U32, "pairs0"), tab_w[:].bitcast(U32), list1, 0)
-        v_codes = [part_v(0, pairs0)]
+        v_codes = [held([P, 2, 2 * HALF], U8, "v_codes0")]
+        for q in range(2):
+            pairs = held([P, QUARTER], U32, "pairs0%d" % q)
+            nc.vector.tensor_copy(pairs[:], tab_w[:].bitcast(U32).indirect(entries(list1, q * QUARTER, QUARTER)))
+            nc.vector.tensor_copy(
+                v_codes[0][:].bitcast(U16)[:, :, q * QUARTER : (q + 1) * QUARTER], pairs[:].bitcast(U16).rearrange("p (j a) -> p a j", a=2)
+            )
         z_codes = held([P, PACK, 3, 2 * P], U8, "z_codes")
         for raw, passes in ((zv_raw, slice(0, 2)), (zt_raw, slice(2, 3))):
             nc.vector.tensor_copy(z_codes[:, :, passes, :].bitcast(U16), raw[:].bitcast(U16).rearrange("p a (m t) -> p t a m", t=PACK))

@@ -124,7 +124,7 @@ def tile_list_gmu_silu_scatP_kernel(
         nc.gpsimd.tensor_copy(z_planes, z_scales_raw[:].rearrange("p (m t) -> p t m", t=PACK))
         flat_scales = w_planes[:].bitcast(I32)
         for r in range(1, 4):
-            nc.sync.dma_start(flat_scales[r:P:32, :], flat_scales[8 * r : P : 32, :])
+            nc.scalar.dma_start(flat_scales[r:P:32, :], flat_scales[8 * r : P : 32, :])
         wv_codes = held([P, 2, 2 * N], U8, "wv_codes")
         nc.sync.dma_start(wv_codes[:].bitcast(I32), wv_words.rearrange("a p c -> p a c").bitcast(I32))
         zv_raw = placed([P, 2, 2 * N], U8, "zv_raw", PAIRS_AT)

@@ -94,7 +94,7 @@ def tile_list_gmu_silu_scatP_kernel(
         nc.sync.dma_start(tab_w[:], tab_words[0].rearrange("p t b -> p (t b)").bitcast(I32))
 
         wt_bf = held([P, N, PACK], BF16, "wt_bf")
-        nc.scalar.copy(wt_bf[:], wt_raw[:].rearrange("p i n -> p n i"))
+        nc.scalar.copy(wt_bf[:].rearrange("p (c j) i -> p c i j", j=4), wt_raw[:].rearrange("p i (c j) -> p c i j", j=4))
         w_turned = psum.tile([P, P], F32, name="sums", bufs=5)
         nc.tensor.transpose(w_turned[:], w_rows[:], ident[:])
         half_w = held([P, J // P], F32, "half_w")
@@ -145,8 +145,10 @@ def tile_list_gmu_silu_scatP_kernel(
                 v_codes[0][:].bitcast(U16)[:, :, q * QUARTER : (q + 1) * QUARTER], pairs[:].bitcast(U16).rearrange("p (j a) -> p a j", a=2)
             )
         z_codes = held([P, PACK, 3, 2 * P], U8, "z_codes")
-        for raw, passes in ((zv_raw, slice(0, 2)), (zt_raw, slice(2, 3))):
-            nc.vector.tensor_copy(z_codes[:, :, passes, :].bitcast(U16), raw[:].bitcast(U16).rearrange("p a (m t) -> p t a m", t=PACK))
+        for pages_of_pair in (slice(0, 2), slice(2, 4)):
+            for raw, passes in ((zv_raw, slice(0, 2)), (zt_raw, slice(2, 3))):
+                dealt = raw[:].bitcast(U16).rearrange("p a (m t) -> p t a m", t=PACK)
+                nc.vector.tensor_copy(z_codes[:, pages_of_pair, passes, :].bitcast(U16), dealt[:, pages_of_pair, :, :])
         v2_codes.append(gather(placed([P, HALF], U32, "v2_codes1", HALF), tab2_w[:].bitcast(U32), list2, 1))
         pairs1 = gather(placed([P, HALF], U32, "pairs1", PAIRS_AT), tab_w[:].bitcast(U32), list1, 1)
         v_codes.append(part_v(1, pairs1))

@@ -159,7 +159,7 @@ def tile_list_gmu_silu_scatP_kernel(
         out_rows = out_0.rearrange("(p t) c -> p t c", t=PACK)
         out_words = out_1[0].rearrange("p t b -> p (t b)").bitcast(I32)
         blocks = HALF // P
-        seen, said = {}, {}
+        seen, said, pictures = {}, {}, {}
         th = {(h, pair): held([P, 2, HALF], F32, "th%d%d" % (h, pair)) for h in range(HALVES) for pair in range(2)}
         gated = {(h, pair): held([P, 2, HALF], F32, "gated%d%d" % (h, pair)) for h in range(HALVES) for pair in range(2)}
         base = {(h, pair): held([P, 2, HALF], F32, "base%d%d" % (h, pair)) for h in range(HALVES) for pair in range(2)}
@@ -178,7 +178,7 @@ def tile_list_gmu_silu_scatP_kernel(
             nc.scalar.activation(av[:], hv[:].rearrange("p (m t) -> p t m", t=PACK), ACT.Silu)
             if block < 2:
                 seen[block] = held([P, PACK, P], F32, "seen%d" % block, ("seen0", "page3")[block])
-                nc.scalar.mul(seen[block][:], av[:], half_w[:, block : block + 1])
+                pictures[block] = av
             else:
                 seen[block] = acts.tile([P, PACK, P], F32, name="seen")
                 nc.scalar.mul(seen[block][:], av[:], half_w[:, block : block + 1])
@@ -240,25 +240,34 @@ def tile_list_gmu_silu_scatP_kernel(
             window = pages[t][:].indirect(entries(list1, first, count))
             nc.vector.tensor_tensor(window, gated[h, t // 2][:, t % 2, cols], base[h, t // 2][:, t % 2, cols], ALU.add)
 
+        def scale_first(pair):
+            for block in range(2):
+                of_pair = slice(2 * pair, 2 * pair + 2)
+                nc.scalar.mul(seen[block][:, of_pair, :], pictures[block][:, of_pair, :], half_w[:, block : block + 1])
+
         for block in range(blocks):
             text(block)
         for q in range(QUARTERS):
             for branch in (text, picture) if q >= 2 else (picture,):
                 branch(2 * q)
                 branch(2 * q + 1)
+            if q == 0:
+                scale_first(0)
             for pair in range(2 if q < 2 else 1):
                 if q % 2 == 0:
                     gate_sum(q // 2, 2 * pair)
                     gate_sum(q // 2, 2 * pair + 1)
                 combine(q, pair)
                 if (q, pair) == (0, 0):
+                    scale_first(1)
                     for t in range(2):
                         gate_tanh(first_sums[t], 0, t, slice(QUARTER, HALF))
             if q == 0:
                 pages.append(held([P, T], F32, "page3"))
                 nc.gpsimd.memset(pages[3][:], 0.0)
-            for t in range(PACK if q < 2 else 2):
+            for t in range(PACK if q < 2 else 1):
                 place(t, q * QUARTER, QUARTER)
+        place(1, HALF, HALF)
         gate_sum(1, 2)
         gate_sum(1, 3)
         combine(2, 1)
@@ -274,9 +283,9 @@ def tile_list_gmu_silu_scatP_kernel(
             nc.sync.dma_start(out_rows[:, t, :], pages[t][:])
             for c in range(CHUNKS):
                 src = pages[t][:, c * CHUNK : (c + 1) * CHUNK]
-                if t == PACK - 1 and c < 2:
+                if t == PACK - 1 and c < 1:
                     nc.vector.tensor_copy(paired[c][:, t // 2, :, t % 2], src)
-                elif t == PACK - 2 and c < 2:
+                elif t == PACK - 2 and c < 1:
                     nc.scalar.copy(paired[c][:, t // 2, :, :], src.unsqueeze(2).to_broadcast([P, CHUNK, 2]))
                 else:
                     nc.scalar.copy(paired[c][:, t // 2, :, t % 2], src)

@@ -235,6 +235,15 @@ def tile_list_gmu_silu_scatP_kernel(
             nc.scalar.mul(base[h, pair][:, :, cols], back[:], -2.0)
             nc.vector.scalar_tensor_tensor(gated[h, pair][:, :, cols], th[h, pair][:, :, cols], 1.0, diff[:], ALU.add, ALU.mult)
 
+        def first_page(t):
+            both = psum.tile([P, 2, QUARTER], F32, name=("sums", "diff")[t], bufs=(5, 3)[t])
+            for i, blocks_of in enumerate((seen, said)):
+                for k in range(2):
+                    nc.tensor.transpose(both[:, i, k * P : (k + 1) * P], blocks_of[k][:, t, :], ident[:])
+            tanh = th[0, 0][:, t, 0:QUARTER]
+            nc.vector.scalar_tensor_tensor(gated[0, 0][:, t, 0:QUARTER], tanh, 1.0, both[:, 0, :], ALU.add, ALU.mult)
+            nc.vector.scalar_tensor_tensor(base[0, 0][:, t, 0:QUARTER], tanh, -1.0, both[:, 1, :], ALU.add, ALU.mult)
+
         def place(t, first, count):
             h, cols = first // HALF, slice(first % HALF, first % HALF + count)
             window = pages[t][:].indirect(entries(list1, first, count))
@@ -257,8 +266,11 @@ def tile_list_gmu_silu_scatP_kernel(
                 if q % 2 == 0:
                     gate_sum(q // 2, 2 * pair)
                     gate_sum(q // 2, 2 * pair + 1)
-                combine(q, pair)
-                if (q, pair) == (0, 0):
+                if (q, pair) != (0, 0):
+                    combine(q, pair)
+                else:
+                    first_page(0)
+                    first_page(1)
                     scale_first(1)
                     for t in range(2):
                         gate_tanh(first_sums[t], 0, t, slice(QUARTER, HALF))
@@ -283,9 +295,9 @@ def tile_list_gmu_silu_scatP_kernel(
             nc.sync.dma_start(out_rows[:, t, :], pages[t][:])
             for c in range(CHUNKS):
                 src = pages[t][:, c * CHUNK : (c + 1) * CHUNK]
-                if t == PACK - 1 and c < 1:
+                if t == PACK - 1 and c < 2:
                     nc.vector.tensor_copy(paired[c][:, t // 2, :, t % 2], src)
-                elif t == PACK - 2 and c < 1:
+                elif t == PACK - 2 and c < 2:
                     nc.scalar.copy(paired[c][:, t // 2, :, :], src.unsqueeze(2).to_broadcast([P, CHUNK, 2]))
                 else:
                     nc.scalar.copy(paired[c][:, t // 2, :, t % 2], src)

@@ -290,7 +290,7 @@ def tile_list_gmu_silu_scatP_kernel(
         paired = [held([P, 2, CHUNK, 2], BF16, "paired%d" % c) for c in range(CHUNKS)]
         woven = [held([P, CHUNK, PACK], BF16, "woven%d" % c) for c in range(CHUNKS)]
         y_codes = [held([P, CHUNK], U32, "y_codes%d" % c) for c in range(CHUNKS)]
-        y_scales = held([P, T], U8, "y_scales")
+        y_scales = held([P, CHUNK], U8, "y_scales")
         for t in range(PACK):
             nc.sync.dma_start(out_rows[:, t, :], pages[t][:])
             for c in range(CHUNKS):
@@ -309,7 +309,7 @@ def tile_list_gmu_silu_scatP_kernel(
 
         def quantize(c):
             nc.vector.quantize_mx(
-                out=y_codes[c][:].bitcast(FP8X4), scales=y_scales[:, c * CHUNK : (c + 1) * CHUNK],
+                out=y_codes[c][:].bitcast(FP8X4), scales=y_scales[4 * c : P, :],
                 in_=woven[c][:].rearrange("p c t -> p (c t)"),
             )
             nc.sync.dma_start(out_words[:, c * CHUNK : (c + 1) * CHUNK], y_codes[c][:].bitcast(I32))
@@ -320,4 +320,5 @@ def tile_list_gmu_silu_scatP_kernel(
                 weave(c + 1)
             quantize(c)
         for q in range(4):
-            nc.scalar.dma_start(out_2[0, 4 * q : 4 * q + 4, :].bitcast(I32), y_scales[32 * q : 32 * q + 4, :].bitcast(I32))
+            rows = out_2[0, 4 * q : 4 * q + 4, :].bitcast(I32).rearrange("r (c x) -> c r x", c=CHUNKS)
+            nc.scalar.dma_start(rows, y_scales[32 * q : 32 * q + 16, :].bitcast(I32))

@@ -36,8 +36,6 @@ def tile_list_gmu_silu_scatP_kernel(
     with ExitStack() as ctx:
         keep = ctx.enter_context(tc.tile_pool(name="keep", bufs=1))
         reuse = ctx.enter_context(tc.tile_pool(name="reuse", bufs=1))
-        acts = ctx.enter_context(tc.tile_pool(name="acts", bufs=6))
-        temp = ctx.enter_context(tc.tile_pool(name="temp", bufs=2))
         psum = ctx.enter_context(tc.psum_pool(name="psum", bufs=2))
 
         def held(shape, dtype, name, tag=""):
@@ -159,10 +157,11 @@ def tile_list_gmu_silu_scatP_kernel(
         out_rows = out_0.rearrange("(p t) c -> p t c", t=PACK)
         out_words = out_1[0].rearrange("p t b -> p (t b)").bitcast(I32)
         blocks = HALF // P
-        seen, said, pictures = {}, {}, {}
+        raw_silu, scaled = {}, {}
         th = {(h, pair): held([P, 2, HALF], F32, "th%d%d" % (h, pair)) for h in range(HALVES) for pair in range(2)}
         gated = {(h, pair): held([P, 2, HALF], F32, "gated%d%d" % (h, pair)) for h in range(HALVES) for pair in range(2)}
         base = {(h, pair): held([P, 2, HALF], F32, "base%d%d" % (h, pair)) for h in range(HALVES) for pair in range(2)}
+        late_tags = {("seen", 1, 0): "page3", ("said", 6, 1): "paired0", ("said", 7, 1): "paired1", ("seen", 6, 1): "paired2", ("seen", 7, 1): "paired3"}
 
         def picture(block):
             h, k = divmod(block, blocks)
@@ -174,14 +173,9 @@ def tile_list_gmu_silu_scatP_kernel(
                     out=hv[:], lhsT=v_codes[h][:, a, 2 * k * P : 2 * (k + 1) * P].bitcast(FP4X4), lhsT_scale=planes[a],
                     rhs=wv_codes[:, a, :].bitcast(FP4X4), rhs_scale=w_planes[:, (3 + a) * N : (4 + a) * N], start=(a == 0), stop=(a == 1),
                 )
-            av = temp.tile([P, PACK, P], F32, name="av")
+            av = held([P, PACK, P], F32, "av%d" % block)
             nc.scalar.activation(av[:], hv[:].rearrange("p (m t) -> p t m", t=PACK), ACT.Silu)
-            if block < 2:
-                seen[block] = held([P, PACK, P], F32, "seen%d" % block, ("seen0", "page3")[block])
-                pictures[block] = av
-            else:
-                seen[block] = acts.tile([P, PACK, P], F32, name="seen")
-                nc.scalar.mul(seen[block][:], av[:], half_w[:, block : block + 1])
+            raw_silu["seen", block] = av
 
         def text(block):
             h, k = divmod(block, blocks)
@@ -191,13 +185,22 @@ def tile_list_gmu_silu_scatP_kernel(
                 out=ht[:], lhsT=v2_codes[h][:, cols].bitcast(FP8X4), lhsT_scale=v2_scales[h][:, cols],
                 rhs=wt_codes[:].bitcast(FP8X4), rhs_scale=wt_scales[:], start=True, stop=True,
             )
-            at = temp.tile([P, PACK, P], F32, name="at", bufs=4)
+            at = held([P, PACK, P], F32, "at%d" % block, "at%d" % k)
             nc.scalar.activation(at[:], ht[:].rearrange("p (m t) -> p t m", t=PACK), ACT.Silu)
-            said[block] = acts.tile([P, PACK, P], F32, name="said")
+            raw_silu["said", block] = at
             if block < blocks:
-                nc.gpsimd.tensor_scalar(said[block][:], at[:], neg_half_w[:, block : block + 1], 0.0, ALU.mult, ALU.add)
-            else:
-                nc.scalar.mul(said[block][:], at[:], neg_half_w[:, block : block + 1])
+                said = held([P, PACK, P], F32, "said%d" % block)
+                nc.gpsimd.tensor_scalar(said[:], at[:], neg_half_w[:, block : block + 1], 0.0, ALU.mult, ALU.add)
+                for pair in range(2):
+                    scaled["said", block, pair] = said[:, 2 * pair : 2 * pair + 2, :]
+
+        def scale(q, pair):
+            for kind, factor in (("said", neg_half_w), ("seen", half_w)):
+                for block in (2 * q, 2 * q + 1):
+                    key = (kind, block, pair)
+                    if key not in scaled:
+                        scaled[key] = held([P, 2, P], F32, "%s%d%d" % key, late_tags.get(key, ""))[:]
+                        nc.scalar.mul(scaled[key], raw_silu[kind, block][:, 2 * pair : 2 * pair + 2, :], factor[:, block : block + 1])
 
         first_sums = {}
 
@@ -226,20 +229,21 @@ def tile_list_gmu_silu_scatP_kernel(
             h, cols = q // 2, slice(q % 2 * QUARTER, (q % 2 + 1) * QUARTER)
             back = psum.tile([P, 2, QUARTER], F32, name="sums", bufs=5)
             diff = psum.tile([P, 2, QUARTER], F32, name="diff", bufs=3)
-            spots = [(i, k, 2 * q + k, 2 * pair + i) for i in range(2) for k in range(2)]
-            for i, k, block, t in spots:
-                nc.tensor.transpose(back[:, i, k * P : (k + 1) * P], said[block][:, t, :], ident[:])
-            for i, k, block, t in spots:
-                nc.tensor.matmul(diff[:, i, k * P : (k + 1) * P], seen[block][:, t, :], ident[:], start=True, stop=False, is_transpose=True)
-                nc.tensor.matmul(diff[:, i, k * P : (k + 1) * P], said[block][:, t, :], ident[:], start=False, stop=True, is_transpose=True)
+            spots = [(i, k, 2 * q + k) for i in range(2) for k in range(2)]
+            for i, k, block in spots:
+                nc.tensor.transpose(back[:, i, k * P : (k + 1) * P], scaled["said", block, pair][:, i, :], ident[:])
+            for i, k, block in spots:
+                nc.tensor.matmul(diff[:, i, k * P : (k + 1) * P], scaled["seen", block, pair][:, i, :], ident[:], start=True, stop=False, is_transpose=True)
+                nc.tensor.matmul(diff[:, i, k * P : (k + 1) * P], scaled["said", block, pair][:, i, :], ident[:], start=False, stop=True, is_transpose=True)
             nc.scalar.mul(base[h, pair][:, :, cols], back[:], -2.0)
-            nc.vector.scalar_tensor_tensor(gated[h, pair][:, :, cols], th[h, pair][:, :, cols], 1.0, diff[:], ALU.add, ALU.mult)
+            for i in range(2):
+                nc.vector.scalar_tensor_tensor(gated[h, pair][:, i, cols], th[h, pair][:, i, cols], 1.0, diff[:, i, :], ALU.add, ALU.mult)
 
         def first_page(t):
             both = psum.tile([P, 2, QUARTER], F32, name=("sums", "diff")[t], bufs=(5, 3)[t])
-            for i, blocks_of in enumerate((seen, said)):
+            for i, kind in enumerate(("seen", "said")):
                 for k in range(2):
-                    nc.tensor.transpose(both[:, i, k * P : (k + 1) * P], blocks_of[k][:, t, :], ident[:])
+                    nc.tensor.transpose(both[:, i, k * P : (k + 1) * P], scaled[kind, k, 0][:, t, :], ident[:])
             tanh = th[0, 0][:, t, 0:QUARTER]
             nc.vector.scalar_tensor_tensor(gated[0, 0][:, t, 0:QUARTER], tanh, 1.0, both[:, 0, :], ALU.add, ALU.mult)
             nc.vector.scalar_tensor_tensor(base[0, 0][:, t, 0:QUARTER], tanh, -1.0, both[:, 1, :], ALU.add, ALU.mult)
@@ -249,41 +253,49 @@ def tile_list_gmu_silu_scatP_kernel(
             window = pages[t][:].indirect(entries(list1, first, count))
             nc.vector.tensor_tensor(window, gated[h, t // 2][:, t % 2, cols], base[h, t // 2][:, t % 2, cols], ALU.add)
 
-        def scale_first(pair):
-            for block in range(2):
-                of_pair = slice(2 * pair, 2 * pair + 2)
-                nc.scalar.mul(seen[block][:, of_pair, :], pictures[block][:, of_pair, :], half_w[:, block : block + 1])
+        def unit(q, pair):
+            scale(q, pair)
+            combine(q, pair)
+            for t in (2 * pair, 2 * pair + 1):
+                place(t, q * QUARTER, QUARTER)
 
         for block in range(blocks):
             text(block)
-        for q in range(QUARTERS):
-            for branch in (text, picture) if q >= 2 else (picture,):
+        picture(0)
+        picture(1)
+        scale(0, 0)
+        gate_sum(0, 0)
+        gate_sum(0, 1)
+        first_page(0)
+        first_page(1)
+        pages.append(held([P, T], F32, "page3"))
+        nc.gpsimd.memset(pages[3][:], 0.0)
+        place(0, 0, QUARTER)
+        place(1, 0, QUARTER)
+        scale(0, 1)
+        for t in range(2):
+            gate_tanh(first_sums[t], 0, t, slice(QUARTER, HALF))
+        gate_sum(0, 2)
+        gate_sum(0, 3)
+        unit(0, 1)
+        picture(2)
+        picture(3)
+        unit(1, 0)
+        unit(1, 1)
+        for q in range(2, QUARTERS):
+            for branch in (text, picture):
                 branch(2 * q)
                 branch(2 * q + 1)
-            if q == 0:
-                scale_first(0)
-            for pair in range(2 if q < 2 else 1):
-                if q % 2 == 0:
-                    gate_sum(q // 2, 2 * pair)
-                    gate_sum(q // 2, 2 * pair + 1)
-                if (q, pair) != (0, 0):
-                    combine(q, pair)
-                else:
-                    first_page(0)
-                    first_page(1)
-                    scale_first(1)
-                    for t in range(2):
-                        gate_tanh(first_sums[t], 0, t, slice(QUARTER, HALF))
-            if q == 0:
-                pages.append(held([P, T], F32, "page3"))
-                nc.gpsimd.memset(pages[3][:], 0.0)
-            for t in range(PACK if q < 2 else 1):
-                place(t, q * QUARTER, QUARTER)
-        place(1, HALF, HALF)
+            scale(q, 0)
+            if q == 2:
+                gate_sum(1, 0)
+                gate_sum(1, 1)
+            unit(q, 0)
         gate_sum(1, 2)
         gate_sum(1, 3)
-        combine(2, 1)
-        combine(3, 1)
+        for q in range(2, QUARTERS):
+            scale(q, 1)
+            combine(q, 1)
         for t in range(2, PACK):
             place(t, HALF, HALF)
 

@@ -147,8 +147,8 @@ def tile_list_gmu_silu_scatP_kernel(
             for raw, passes in ((zv_raw, slice(0, 2)), (zt_raw, slice(2, 3))):
                 dealt = raw[:].bitcast(U16).rearrange("p a (m t) -> p t a m", t=PACK)
                 nc.vector.tensor_copy(z_codes[:, pages_of_pair, passes, :].bitcast(U16), dealt[:, pages_of_pair, :, :])
-        v2_codes.append(gather(placed([P, HALF], U32, "v2_codes1", HALF), tab2_w[:].bitcast(U32), list2, 1))
         pairs1 = gather(placed([P, HALF], U32, "pairs1", PAIRS_AT), tab_w[:].bitcast(U32), list1, 1)
+        v2_codes.append(gather(placed([P, HALF], U32, "v2_codes1", HALF), tab2_w[:].bitcast(U32), list2, 1))
         v_codes.append(part_v(1, pairs1))
         for t, offset in ((1, PAIRS_AT + 2 * HALF - 4 * T), (2, PAIRS_AT + 2 * HALF)):
             pages.append(placed([P, T], F32, "page%d" % t, offset))
@@ -161,7 +161,7 @@ def tile_list_gmu_silu_scatP_kernel(
         th = {(h, pair): held([P, 2, HALF], F32, "th%d%d" % (h, pair)) for h in range(HALVES) for pair in range(2)}
         gated = {(h, pair): held([P, 2, HALF], F32, "gated%d%d" % (h, pair)) for h in range(HALVES) for pair in range(2)}
         base = {(h, pair): held([P, 2, HALF], F32, "base%d%d" % (h, pair)) for h in range(HALVES) for pair in range(2)}
-        late_tags = {("seen", 1, 0): "page3", ("said", 6, 1): "paired0", ("said", 7, 1): "paired1", ("seen", 6, 1): "paired2", ("seen", 7, 1): "paired3"}
+        late_tags = {("seen", 1, 0): "page3", ("said", 6, 0): "paired0", ("said", 7, 0): "paired1", ("seen", 6, 0): "paired2", ("seen", 7, 0): "paired3"}
 
         def picture(block):
             h, k = divmod(block, blocks)
@@ -198,9 +198,16 @@ def tile_list_gmu_silu_scatP_kernel(
             for kind, factor in (("said", neg_half_w), ("seen", half_w)):
                 for block in (2 * q, 2 * q + 1):
                     key = (kind, block, pair)
-                    if key not in scaled:
+                    if key in scaled:
+                        continue
+                    if q == 0:
                         scaled[key] = held([P, 2, P], F32, "%s%d%d" % key, late_tags.get(key, ""))[:]
                         nc.scalar.mul(scaled[key], raw_silu[kind, block][:, 2 * pair : 2 * pair + 2, :], factor[:, block : block + 1])
+                    else:
+                        whole = held([P, PACK, P], F32, "%s%d" % (kind, block), late_tags.get(key, ""))
+                        nc.scalar.mul(whole[:], raw_silu[kind, block][:], factor[:, block : block + 1])
+                        for both in range(2):
+                            scaled[kind, block, both] = whole[:, 2 * both : 2 * both + 2, :]
 
         first_sums = {}
 
@@ -307,12 +314,8 @@ def tile_list_gmu_silu_scatP_kernel(
             nc.sync.dma_start(out_rows[:, t, :], pages[t][:])
             for c in range(CHUNKS):
                 src = pages[t][:, c * CHUNK : (c + 1) * CHUNK]
-                if t == PACK - 1 and c < 2:
-                    nc.vector.tensor_copy(paired[c][:, t // 2, :, t % 2], src)
-                elif t == PACK - 2 and c < 2:
-                    nc.scalar.copy(paired[c][:, t // 2, :, :], src.unsqueeze(2).to_broadcast([P, CHUNK, 2]))
-                else:
-                    nc.scalar.copy(paired[c][:, t // 2, :, t % 2], src)
+                engine_copy = nc.vector.tensor_copy if t >= 2 and c == 0 else nc.scalar.copy
+                engine_copy(paired[c][:, t // 2, :, t % 2], src)
 
         def weave(c):
             engine_copy, word = (nc.scalar.copy, U32) if c == CHUNKS - 1 else (nc.vector.tensor_copy, I32)

@@ -163,7 +163,7 @@ def tile_list_gmu_silu_scatP_kernel(
         base = {(h, pair): held([P, 2, HALF], F32, "base%d%d" % (h, pair)) for h in range(HALVES) for pair in range(2)}
         late_tags = {("seen", 1, 0): "page3", ("said", 6, 0): "paired0", ("said", 7, 0): "paired1", ("seen", 6, 0): "paired2", ("seen", 7, 0): "paired3"}
 
-        def picture(block):
+        def picture_sum(block):
             h, k = divmod(block, blocks)
             cols = slice(k * P, (k + 1) * P)
             planes = (v_scales[h][:, cols], shifted[h][:, cols])
@@ -173,11 +173,14 @@ def tile_list_gmu_silu_scatP_kernel(
                     out=hv[:], lhsT=v_codes[h][:, a, 2 * k * P : 2 * (k + 1) * P].bitcast(FP4X4), lhsT_scale=planes[a],
                     rhs=wv_codes[:, a, :].bitcast(FP4X4), rhs_scale=w_planes[:, (3 + a) * N : (4 + a) * N], start=(a == 0), stop=(a == 1),
                 )
+            return hv
+
+        def picture_silu(block, hv):
             av = held([P, PACK, P], F32, "av%d" % block)
             nc.scalar.activation(av[:], hv[:].rearrange("p (m t) -> p t m", t=PACK), ACT.Silu)
             raw_silu["seen", block] = av
 
-        def text(block):
+        def text_sum(block):
             h, k = divmod(block, blocks)
             cols = slice(k * P, (k + 1) * P)
             ht = psum.tile([P, N], F32, name="sums", bufs=5)
@@ -185,7 +188,10 @@ def tile_list_gmu_silu_scatP_kernel(
                 out=ht[:], lhsT=v2_codes[h][:, cols].bitcast(FP8X4), lhsT_scale=v2_scales[h][:, cols],
                 rhs=wt_codes[:].bitcast(FP8X4), rhs_scale=wt_scales[:], start=True, stop=True,
             )
-            at = held([P, PACK, P], F32, "at%d" % block, "at%d" % k)
+            return ht
+
+        def text_silu(block, ht):
+            at = held([P, PACK, P], F32, "at%d" % block, "at%d" % (block % blocks))
             nc.scalar.activation(at[:], ht[:].rearrange("p (m t) -> p t m", t=PACK), ACT.Silu)
             raw_silu["said", block] = at
             if block < blocks:
@@ -194,8 +200,9 @@ def tile_list_gmu_silu_scatP_kernel(
                 for pair in range(2):
                     scaled["said", block, pair] = said[:, 2 * pair : 2 * pair + 2, :]
 
-        def scale(q, pair):
-            for kind, factor in (("said", neg_half_w), ("seen", half_w)):
+        def scale(q, pair, kinds=("said", "seen")):
+            for kind in kinds:
+                factor = neg_half_w if kind == "said" else half_w
                 for block in (2 * q, 2 * q + 1):
                     key = (kind, block, pair)
                     if key in scaled:
@@ -208,8 +215,6 @@ def tile_list_gmu_silu_scatP_kernel(
                         nc.scalar.mul(whole[:], raw_silu[kind, block][:], factor[:, block : block + 1])
                         for both in range(2):
                             scaled[kind, block, both] = whole[:, 2 * both : 2 * both + 2, :]
-
-        first_sums = {}
 
         def gate_tanh(z, h, t, cols):
             nc.scalar.activation(th[h, t // 2][:, t % 2, cols], z[:, cols], ACT.Tanh, bias=half_bias[:, t : t + 1], scale=0.5)
@@ -226,11 +231,21 @@ def tile_list_gmu_silu_scatP_kernel(
                 out=z[:], lhsT=z_codes[:, t, 2, :].bitcast(FP4X4), lhsT_scale=z_planes[:, t, 2 * P : 3 * P],
                 rhs=v2_codes[h][:].bitcast(FP8X4), rhs_scale=v2_scales[h], start=False, stop=True,
             )
-            if (h, t // 2) == (0, 0):
-                first_sums[t] = z
-                gate_tanh(z, h, t, slice(0, QUARTER))
-            else:
-                gate_tanh(z, h, t, slice(0, HALF))
+            return z
+
+        def gate_sums(h, pair):
+            return {t: gate_sum(h, t) for t in (2 * pair, 2 * pair + 1)}
+
+        def gate_tanhs(h, sums, cols=slice(0, HALF)):
+            for t in sums:
+                gate_tanh(sums[t], h, t, cols)
+
+        def sums_of(branch_sum, q):
+            return {block: branch_sum(block) for block in (2 * q, 2 * q + 1)}
+
+        def silu_of(branch_silu, sums):
+            for block in sums:
+                branch_silu(block, sums[block])
 
         def combine(q, pair):
             h, cols = q // 2, slice(q % 2 * QUARTER, (q % 2 + 1) * QUARTER)
@@ -267,12 +282,14 @@ def tile_list_gmu_silu_scatP_kernel(
                 place(t, q * QUARTER, QUARTER)
 
         for block in range(blocks):
-            text(block)
-        picture(0)
-        picture(1)
+            text_silu(block, text_sum(block))
+        for block in range(2):
+            picture_silu(block, picture_sum(block))
         scale(0, 0)
-        gate_sum(0, 0)
-        gate_sum(0, 1)
+        first_sums = {}
+        for t in range(2):
+            first_sums[t] = gate_sum(0, t)
+            gate_tanh(first_sums[t], 0, t, slice(0, QUARTER))
         first_page(0)
         first_page(1)
         pages.append(held([P, T], F32, "page3"))
@@ -280,26 +297,34 @@ def tile_list_gmu_silu_scatP_kernel(
         place(0, 0, QUARTER)
         place(1, 0, QUARTER)
         scale(0, 1)
-        for t in range(2):
-            gate_tanh(first_sums[t], 0, t, slice(QUARTER, HALF))
-        gate_sum(0, 2)
-        gate_sum(0, 3)
+        gate_tanhs(0, first_sums, slice(QUARTER, HALF))
+        gate_tanhs(0, gate_sums(0, 1))
+        next_sums = sums_of(picture_sum, 1)
         unit(0, 1)
-        picture(2)
-        picture(3)
+        silu_of(picture_silu, next_sums)
+        scale(1, 0)
+        next_sums = sums_of(text_sum, 2)
         unit(1, 0)
+        silu_of(text_silu, next_sums)
+        next_sums = sums_of(picture_sum, 2)
+        scale(2, 0, ("said",))
         unit(1, 1)
-        for q in range(2, QUARTERS):
-            for branch in (text, picture):
-                branch(2 * q)
-                branch(2 * q + 1)
-            scale(q, 0)
-            if q == 2:
-                gate_sum(1, 0)
-                gate_sum(1, 1)
-            unit(q, 0)
-        gate_sum(1, 2)
-        gate_sum(1, 3)
+        silu_of(picture_silu, next_sums)
+        scale(2, 0)
+        gate_tanhs(1, gate_sums(1, 0))
+        next_sums = sums_of(text_sum, 3)
+        combine(2, 0)
+        place(0, HALF, QUARTER)
+        silu_of(text_silu, next_sums)
+        next_sums = sums_of(picture_sum, 3)
+        scale(3, 0, ("said",))
+        silu_of(picture_silu, next_sums)
+        scale(3, 0)
+        last_sums = gate_sums(1, 1)
+        combine(3, 0)
+        place(0, HALF + QUARTER, QUARTER)
+        place(1, HALF, HALF)
+        gate_tanhs(1, last_sums)
         for q in range(2, QUARTERS):
             scale(q, 1)
             combine(q, 1)

@@ -296,15 +296,15 @@ def tile_list_gmu_silu_scatP_kernel(
         nc.gpsimd.memset(pages[3][:], 0.0)
         place(0, 0, QUARTER)
         place(1, 0, QUARTER)
-        scale(0, 1)
-        gate_tanhs(0, first_sums, slice(QUARTER, HALF))
-        gate_tanhs(0, gate_sums(0, 1))
-        next_sums = sums_of(picture_sum, 1)
-        unit(0, 1)
-        silu_of(picture_silu, next_sums)
+        silu_of(picture_silu, sums_of(picture_sum, 1))
         scale(1, 0)
-        next_sums = sums_of(text_sum, 2)
+        gate_tanhs(0, first_sums, slice(QUARTER, HALF))
+        next_sums = gate_sums(0, 1)
         unit(1, 0)
+        scale(0, 1)
+        gate_tanhs(0, next_sums)
+        next_sums = sums_of(text_sum, 2)
+        unit(0, 1)
         silu_of(text_silu, next_sums)
         next_sums = sums_of(picture_sum, 2)
         scale(2, 0, ("said",))

@@ -57,14 +57,15 @@ def tile_list_gmu_silu_scatP_kernel(
         shifted = [shifted_all[:, h * HALF : (h + 1) * HALF] for h in range(HALVES)]
         for tile in (tab_s, tab2_s):
             nc.gpsimd.memset(tile[:].bitcast(I32), 0)
-        for tile in [z_scales_raw[:], w_planes[:, 3 * N :], shifted_all[:]]:
-            nc.vector.memset(tile.bitcast(I32), 0)
         w_rows = held([P, P], F32, "w_rows")
-        nc.vector.memset(w_rows[:], 0.0)
+        pages = [held([P, T], F32, "page%d" % t) for t in range(2)]
+        for tile in [z_scales_raw[:], w_planes[:, 3 * N :], shifted_all[:], w_rows[:], pages[0][:]]:
+            words = tile.bitcast(I32)
+            nc.vector.memset(words[:, 1:], 0)
+            nc.vector.memset(words[:, 0:1], 0)
         ident = held([P, P], F32, "ident")
         make_identity(nc, ident[:])
-        pages = [held([P, T], F32, "page0")]
-        nc.vector.memset(pages[0][:].bitcast(I32), 0)
+        nc.gpsimd.memset(pages[1][:], 0.0)
 
         nc.sync.dma_start(list1[:], offs)
         nc.sync.dma_start(list2[:], offs2)
@@ -150,9 +151,8 @@ def tile_list_gmu_silu_scatP_kernel(
         pairs1 = gather(placed([P, HALF], U32, "pairs1", PAIRS_AT), tab_w[:].bitcast(U32), list1, 1)
         v2_codes.append(gather(placed([P, HALF], U32, "v2_codes1", HALF), tab2_w[:].bitcast(U32), list2, 1))
         v_codes.append(part_v(1, pairs1))
-        for t, offset in ((1, PAIRS_AT + 2 * HALF - 4 * T), (2, PAIRS_AT + 2 * HALF)):
-            pages.append(placed([P, T], F32, "page%d" % t, offset))
-            nc.gpsimd.memset(pages[t][:], 0.0)
+        pages.append(placed([P, T], F32, "page2", PAIRS_AT + 2 * HALF))
+        nc.gpsimd.memset(pages[2][:], 0.0)
 
         out_rows = out_0.rearrange("(p t) c -> p t c", t=PACK)
         out_words = out_1[0].rearrange("p t b -> p (t b)").bitcast(I32)

@@ -135,7 +135,11 @@ def tile_list_gmu_silu_scatP_kernel(
         half_bias = held([P, PACK], F32, "half_bias")
         nc.scalar.mul(half_bias[:], bias[:], 0.5)
         nc.vector.quantize_mx(out=wt_codes[:].bitcast(FP8X4), scales=wt_scales[:], in_=wt_bf[:].rearrange("p n i -> p (n i)"))
-        v2_codes = [gather(held([P, HALF], U32, "v2_codes0"), tab2_w[:].bitcast(U32), list2, 0)]
+        v2_codes = [held([P, HALF], U32, "v2_codes0")]
+        for q in range(2):
+            nc.vector.tensor_copy(
+                v2_codes[0][:, q * QUARTER : (q + 1) * QUARTER], tab2_w[:].bitcast(U32).indirect(entries(list2, q * QUARTER, QUARTER))
+            )
         v_codes = [held([P, 2, 2 * HALF], U8, "v_codes0")]
         for q in range(2):
             pairs = held([P, QUARTER], U32, "pairs0%d" % q)
@@ -348,11 +352,14 @@ def tile_list_gmu_silu_scatP_kernel(
             engine_copy(woven[c][:].bitcast(word), words.rearrange("p u c -> p c u"))
 
         def quantize(c):
-            nc.vector.quantize_mx(
-                out=y_codes[c][:].bitcast(FP8X4), scales=y_scales[4 * c : P, :],
-                in_=woven[c][:].rearrange("p c t -> p (c t)"),
-            )
-            nc.sync.dma_start(out_words[:, c * CHUNK : (c + 1) * CHUNK], y_codes[c][:].bitcast(I32))
+            width = CHUNK // 2 if c == CHUNKS - 1 else CHUNK
+            for first in range(0, CHUNK, width):
+                cols = slice(first, first + width)
+                nc.vector.quantize_mx(
+                    out=y_codes[c][:, cols].bitcast(FP8X4), scales=y_scales[4 * c : P, cols],
+                    in_=woven[c][:, cols, :].rearrange("p c t -> p (c t)"),
+                )
+                nc.sync.dma_start(out_words[:, c * CHUNK + first : c * CHUNK + first + width], y_codes[c][:, cols].bitcast(I32))
 
         weave(0)
         for c in range(CHUNKS):
@@ -361,4 +368,4 @@ def tile_list_gmu_silu_scatP_kernel(
             quantize(c)
         for q in range(4):
             rows = out_2[0, 4 * q : 4 * q + 4, :].bitcast(I32).rearrange("r (c x) -> c r x", c=CHUNKS)
-            nc.scalar.dma_start(rows, y_scales[32 * q : 32 * q + 16, :].bitcast(I32))
+            (nc.scalar, nc.sync)[q % 2].dma_start(rows, y_scales[32 * q : 32 * q + 16, :].bitcast(I32))

@@ -59,12 +59,13 @@ def tile_list_gmu_silu_scatP_kernel(
             nc.gpsimd.memset(tile[:].bitcast(I32), 0)
         w_rows = held([P, P], F32, "w_rows")
         pages = [held([P, T], F32, "page%d" % t) for t in range(2)]
-        for tile in [z_scales_raw[:], w_planes[:, 3 * N :], shifted_all[:], w_rows[:], pages[0][:]]:
+        for tile in [z_scales_raw[:], w_planes[:, 3 * N :], shifted_all[:], w_rows[:], pages[0][:, 0 : T // 2]]:
             words = tile.bitcast(I32)
             nc.vector.memset(words[:, 1:], 0)
             nc.vector.memset(words[:, 0:1], 0)
         ident = held([P, P], F32, "ident")
         make_identity(nc, ident[:])
+        nc.gpsimd.memset(pages[0][:, T // 2 :], 0.0)
         nc.gpsimd.memset(pages[1][:], 0.0)
 
         nc.sync.dma_start(list1[:], offs)
@@ -335,21 +336,29 @@ def tile_list_gmu_silu_scatP_kernel(
         for t in range(2, PACK):
             place(t, HALF, HALF)
 
-        paired = [held([P, 2, CHUNK, 2], BF16, "paired%d" % c) for c in range(CHUNKS)]
+        paired = [held([P, 2, 2, CHUNK // 2, 2], BF16, "paired%d" % c) for c in range(CHUNKS)]
         woven = [held([P, CHUNK, PACK], BF16, "woven%d" % c) for c in range(CHUNKS)]
         y_codes = [held([P, CHUNK], U32, "y_codes%d" % c) for c in range(CHUNKS)]
         y_scales = held([P, CHUNK], U8, "y_scales")
         for t in range(PACK):
             nc.sync.dma_start(out_rows[:, t, :], pages[t][:])
             for c in range(CHUNKS):
-                src = pages[t][:, c * CHUNK : (c + 1) * CHUNK]
-                engine_copy = nc.vector.tensor_copy if t >= 2 and c == 0 else nc.scalar.copy
-                engine_copy(paired[c][:, t // 2, :, t % 2], src)
+                src = pages[t][:, c * CHUNK : (c + 1) * CHUNK].rearrange("p (h c) -> p h c", h=2)
+                if t >= 2 and c == 0:
+                    nc.vector.tensor_copy(paired[c][:, 0, 1, :, t % 2], src[:, 0, :])
+                    nc.scalar.copy(paired[c][:, 1, 1, :, t % 2], src[:, 1, :])
+                else:
+                    nc.scalar.copy(paired[c][:, :, t // 2, :, t % 2], src)
 
         def weave(c):
             engine_copy, word = (nc.scalar.copy, U32) if c == CHUNKS - 1 else (nc.vector.tensor_copy, I32)
-            words = paired[c][:].rearrange("p u c e -> p u (c e)").bitcast(word)
-            engine_copy(woven[c][:].bitcast(word), words.rearrange("p u c -> p c u"))
+            words = paired[c][:].rearrange("p h u c e -> p h u (c e)").bitcast(word).rearrange("p h u c -> p h c u")
+            lines = woven[c][:].bitcast(word).rearrange("p (h c) u -> p h c u", h=2)
+            if c in (0, CHUNKS - 1):
+                for h in range(2):
+                    engine_copy(lines[:, h, :, :], words[:, h, :, :])
+            else:
+                engine_copy(lines, words)
 
         def quantize(c):
             width = CHUNK // 2 if c == CHUNKS - 1 else CHUNK

from contextlib import ExitStack

import concourse.mybir as mybir
from concourse.masks import make_identity

K, L, N, T, J = 1024, 512, 512, 2048, 1024
FLOPS = 2 * J * N * (2 * K + 2 * L)

F32 = mybir.dt.float32
BF16 = mybir.dt.bfloat16
I32 = mybir.dt.int32
U32 = mybir.dt.uint32
U16 = mybir.dt.uint16
U8 = mybir.dt.uint8
FP8X4 = mybir.dt.float8_e4m3fn_x4
FP4X4 = mybir.dt.float4_e2m1fn_x4
ACT = mybir.ActivationFunctionType
ALU = mybir.AluOpType

P = 128
PACK = 4
HALF = 512
HALVES = J // HALF
CHUNK = 512
CHUNKS = T // CHUNK
QUARTER = 256
PAIRS_AT = 5 * HALF + 4 * T - 2 * HALF
QUARTERS = J // QUARTER


def tile_list_gmu_silu_scatP_kernel(
    tc, tab_words, tab_scales, tab2_words, tab2_scales, zv_words, zv_scales, zt_words, zt_scales,
    b, wv_words, wv_scales, wt, wgo, offs, offs2, out_0, out_1, out_2,
):
    nc = tc.nc
    with ExitStack() as ctx:
        keep = ctx.enter_context(tc.tile_pool(name="keep", bufs=1))
        reuse = ctx.enter_context(tc.tile_pool(name="reuse", bufs=1))
        psum = ctx.enter_context(tc.psum_pool(name="psum", bufs=2))

        def held(shape, dtype, name, tag=""):
            return keep.tile(shape, dtype, name=name, tag=tag or name, align_bytes=64)

        def placed(shape, dtype, name, offset):
            return reuse.tile(shape, dtype, name=name, align_bytes=64, offset=offset)

        def entries(offsets, first, count):
            return offsets[:, first // 16 : (first + count) // 16]

        list1 = held([P, J // 16], U16, "list1")
        list2 = held([P, J // 16], U16, "list2")
        tab_s = held([P, T], U8, "tab_s")
        tab2_s = held([P, T], U8, "tab2_s")
        z_scales_raw = held([P, 3 * N], U8, "z_scales_raw")
        w_planes = held([P, 5 * N], U8, "w_planes")
        shifted_all = held([P, J], U8, "shifted")
        shifted = [shifted_all[:, h * HALF : (h + 1) * HALF] for h in range(HALVES)]
        for tile in (tab_s, tab2_s):
            nc.gpsimd.memset(tile[:].bitcast(I32), 0)
        w_rows = held([P, P], F32, "w_rows")
        pages = [held([P, T], F32, "page%d" % t) for t in range(2)]
        for tile in [z_scales_raw[:], w_planes[:, 3 * N :], shifted_all[:], w_rows[:], pages[0][:, 0 : T // 2]]:
            words = tile.bitcast(I32)
            nc.vector.memset(words[:, 1:], 0)
            nc.vector.memset(words[:, 0:1], 0)
        ident = held([P, P], F32, "ident")
        make_identity(nc, ident[:])
        nc.gpsimd.memset(pages[0][:, T // 2 :], 0.0)
        nc.gpsimd.memset(pages[1][:], 0.0)

        nc.sync.dma_start(list1[:], offs)
        nc.sync.dma_start(list2[:], offs2)
        for r in range(4):
            nc.sync.dma_start(tab_s[r:P:16, :].bitcast(I32), tab_scales[:, r:16:4, :].rearrange("a q n -> q a n").bitcast(I32))
        nc.sync.dma_start(tab2_s[0:4, :].bitcast(I32), tab2_scales[0, 0:4, :].bitcast(I32))
        wt_raw = held([P, PACK, N], F32, "wt_raw")
        nc.sync.dma_start(wt_raw[:], wt.rearrange("(p i) n -> p i n", i=PACK))
        for q in range(1, 4):
            nc.sync.dma_start(tab2_s[32 * q : 32 * q + 4, :].bitcast(I32), tab2_scales[0, 4 * q : 4 * q + 4, :].bitcast(I32))
        for first, scales in ((0, zv_scales), (2, zt_scales)):
            passes = scales.shape[0]
            nc.sync.dma_start(
                z_scales_raw[0:P:8, first * N : (first + passes) * N].bitcast(I32).rearrange("q (a n) -> q a n", a=passes),
                scales.rearrange("a q n -> q a n").bitcast(I32),
            )
        nc.sync.dma_start(
            w_planes[0:P:8, 3 * N :].bitcast(I32).rearrange("q (a n) -> q a n", a=2),
            wv_scales.rearrange("a q n -> q a n").bitcast(I32),
        )
        tab2_w = held([P, T], I32, "tab2_w")
        nc.sync.dma_start(tab2_w[:], tab2_words[0].rearrange("p t b -> p (t b)").bitcast(I32))
        nc.sync.dma_start(w_rows[0 : J // P, :], wgo[0].rearrange("(k p) -> k p", p=P))
        tab_w = held([P, T], I32, "tab_w")
        nc.sync.dma_start(tab_w[:], tab_words[0].rearrange("p t b -> p (t b)").bitcast(I32))

        wt_bf = held([P, N, PACK], BF16, "wt_bf")
        nc.scalar.copy(wt_bf[:].rearrange("p (c j) i -> p c i j", j=4), wt_raw[:].rearrange("p i (c j) -> p c i j", j=4))
        w_turned = psum.tile([P, P], F32, name="sums", bufs=5)
        nc.tensor.transpose(w_turned[:], w_rows[:], ident[:])
        half_w = held([P, J // P], F32, "half_w")
        nc.scalar.mul(half_w[:], w_turned[:, 0 : J // P], 0.5)
        neg_half_w = held([P, J // P], F32, "neg_half_w")
        nc.scalar.mul(neg_half_w[:], w_turned[:, 0 : J // P], -0.5)
        wt_codes = held([P, N], U32, "wt_codes")
        wt_scales = held([P, N], U8, "wt_scales")

        def gather(out, window, offsets, h):
            nc.vector.tensor_copy(out[:], window.indirect(entries(offsets, h * HALF, HALF)))
            return out

        def part_v(h, pairs):
            codes = held([P, 2, 2 * HALF], U8, "v_codes%d" % h)
            nc.vector.tensor_copy(codes[:].bitcast(U16), pairs[:].bitcast(U16).rearrange("p (j a) -> p a j", a=2))
            return codes

        picked = held([P, J], U8, "v_scales")
        nc.vector.tensor_copy(picked[:], tab_s[:].indirect(list1[:]))
        v_scales = [picked[:, h * HALF : (h + 1) * HALF] for h in range(HALVES)]
        nc.sync.dma_start(shifted_all[0:100, :].bitcast(I32), picked[16:116, :].bitcast(I32))
        picked2 = held([P, J], U8, "v2_scales")
        nc.vector.tensor_copy(picked2[:], tab2_s[:].indirect(list2[:]))
        v2_scales = [picked2[:, h * HALF : (h + 1) * HALF] for h in range(HALVES)]
        z_planes = w_planes[:, 0 : 3 * N].rearrange("p (t m) -> p t m", t=PACK)
        nc.gpsimd.tensor_copy(z_planes, z_scales_raw[:].rearrange("p (m t) -> p t m", t=PACK))
        flat_scales = w_planes[:].bitcast(I32)
        for r in range(1, 4):
            nc.scalar.dma_start(flat_scales[r:P:32, :], flat_scales[8 * r : P : 32, :])
        wv_codes = held([P, 2, 2 * N], U8, "wv_codes")
        nc.sync.dma_start(wv_codes[:].bitcast(I32), wv_words.rearrange("a p c -> p a c").bitcast(I32))
        zv_raw = placed([P, 2, 2 * N], U8, "zv_raw", PAIRS_AT)
        zt_raw = placed([P, 1, 2 * N], U8, "zt_raw", 0)
        for raw, words in ((zv_raw, zv_words), (zt_raw, zt_words)):
            nc.sync.dma_start(raw[:].bitcast(I32), words.rearrange("a p c -> p a c").bitcast(I32))
        bias = held([P, PACK], F32, "bias")
        nc.sync.dma_start(bias[:], b.rearrange("(p t) -> p t", t=PACK))
        half_bias = held([P, PACK], F32, "half_bias")
        nc.scalar.mul(half_bias[:], bias[:], 0.5)
        nc.vector.quantize_mx(out=wt_codes[:].bitcast(FP8X4), scales=wt_scales[:], in_=wt_bf[:].rearrange("p n i -> p (n i)"))
        v2_codes = [held([P, HALF], U32, "v2_codes0")]
        for q in range(2):
            nc.vector.tensor_copy(
                v2_codes[0][:, q * QUARTER : (q + 1) * QUARTER], tab2_w[:].bitcast(U32).indirect(entries(list2, q * QUARTER, QUARTER))
            )
        v_codes = [held([P, 2, 2 * HALF], U8, "v_codes0")]
        for q in range(2):
            pairs = held([P, QUARTER], U32, "pairs0%d" % q)
            nc.vector.tensor_copy(pairs[:], tab_w[:].bitcast(U32).indirect(entries(list1, q * QUARTER, QUARTER)))
            nc.vector.tensor_copy(
                v_codes[0][:].bitcast(U16)[:, :, q * QUARTER : (q + 1) * QUARTER], pairs[:].bitcast(U16).rearrange("p (j a) -> p a j", a=2)
            )
        z_codes = held([P, PACK, 3, 2 * P], U8, "z_codes")
        for pages_of_pair in (slice(0, 2), slice(2, 4)):
            for raw, passes in ((zv_raw, slice(0, 2)), (zt_raw, slice(2, 3))):
                dealt = raw[:].bitcast(U16).rearrange("p a (m t) -> p t a m", t=PACK)
                nc.vector.tensor_copy(z_codes[:, pages_of_pair, passes, :].bitcast(U16), dealt[:, pages_of_pair, :, :])
        pairs1 = gather(placed([P, HALF], U32, "pairs1", PAIRS_AT), tab_w[:].bitcast(U32), list1, 1)
        v2_codes.append(gather(placed([P, HALF], U32, "v2_codes1", HALF), tab2_w[:].bitcast(U32), list2, 1))
        v_codes.append(part_v(1, pairs1))
        pages.append(placed([P, T], F32, "page2", PAIRS_AT + 2 * HALF))
        nc.gpsimd.memset(pages[2][:], 0.0)

        out_rows = out_0.rearrange("(p t) c -> p t c", t=PACK)
        out_words = out_1[0].rearrange("p t b -> p (t b)").bitcast(I32)
        blocks = HALF // P
        raw_silu, scaled = {}, {}
        th = {(h, pair): held([P, 2, HALF], F32, "th%d%d" % (h, pair)) for h in range(HALVES) for pair in range(2)}
        gated = {(h, pair): held([P, 2, HALF], F32, "gated%d%d" % (h, pair)) for h in range(HALVES) for pair in range(2)}
        base = {(h, pair): held([P, 2, HALF], F32, "base%d%d" % (h, pair)) for h in range(HALVES) for pair in range(2)}
        late_tags = {("seen", 1, 0): "page3", ("said", 6, 0): "paired0", ("said", 7, 0): "paired1", ("seen", 6, 0): "paired2", ("seen", 7, 0): "paired3"}

        def picture_sum(block):
            h, k = divmod(block, blocks)
            cols = slice(k * P, (k + 1) * P)
            planes = (v_scales[h][:, cols], shifted[h][:, cols])
            hv = psum.tile([P, N], F32, name="sums", bufs=5)
            for a in range(2):
                nc.tensor.matmul_mx(
                    out=hv[:], lhsT=v_codes[h][:, a, 2 * k * P : 2 * (k + 1) * P].bitcast(FP4X4), lhsT_scale=planes[a],
                    rhs=wv_codes[:, a, :].bitcast(FP4X4), rhs_scale=w_planes[:, (3 + a) * N : (4 + a) * N], start=(a == 0), stop=(a == 1),
                )
            return hv

        def picture_silu(block, hv):
            av = held([P, PACK, P], F32, "av%d" % block)
            nc.scalar.activation(av[:], hv[:].rearrange("p (m t) -> p t m", t=PACK), ACT.Silu)
            raw_silu["seen", block] = av

        def text_sum(block):
            h, k = divmod(block, blocks)
            cols = slice(k * P, (k + 1) * P)
            ht = psum.tile([P, N], F32, name="sums", bufs=5)
            nc.tensor.matmul_mx(
                out=ht[:], lhsT=v2_codes[h][:, cols].bitcast(FP8X4), lhsT_scale=v2_scales[h][:, cols],
                rhs=wt_codes[:].bitcast(FP8X4), rhs_scale=wt_scales[:], start=True, stop=True,
            )
            return ht

        def text_silu(block, ht):
            at = held([P, PACK, P], F32, "at%d" % block, "at%d" % (block % blocks))
            nc.scalar.activation(at[:], ht[:].rearrange("p (m t) -> p t m", t=PACK), ACT.Silu)
            raw_silu["said", block] = at
            if block < blocks:
                said = held([P, PACK, P], F32, "said%d" % block)
                nc.gpsimd.tensor_scalar(said[:], at[:], neg_half_w[:, block : block + 1], 0.0, ALU.mult, ALU.add)
                for pair in range(2):
                    scaled["said", block, pair] = said[:, 2 * pair : 2 * pair + 2, :]

        def scale(q, pair, kinds=("said", "seen")):
            for kind in kinds:
                factor = neg_half_w if kind == "said" else half_w
                for block in (2 * q, 2 * q + 1):
                    key = (kind, block, pair)
                    if key in scaled:
                        continue
                    if q == 0:
                        scaled[key] = held([P, 2, P], F32, "%s%d%d" % key, late_tags.get(key, ""))[:]
                        nc.scalar.mul(scaled[key], raw_silu[kind, block][:, 2 * pair : 2 * pair + 2, :], factor[:, block : block + 1])
                    else:
                        whole = held([P, PACK, P], F32, "%s%d" % (kind, block), late_tags.get(key, ""))
                        nc.scalar.mul(whole[:], raw_silu[kind, block][:], factor[:, block : block + 1])
                        for both in range(2):
                            scaled[kind, block, both] = whole[:, 2 * both : 2 * both + 2, :]

        def gate_tanh(z, h, t, cols):
            nc.scalar.activation(th[h, t // 2][:, t % 2, cols], z[:, cols], ACT.Tanh, bias=half_bias[:, t : t + 1], scale=0.5)

        def gate_sum(h, t):
            planes = (v_scales[h], shifted[h])
            z = psum.tile([P, HALF], F32, name="sums", bufs=5)
            for a in range(2):
                nc.tensor.matmul_mx(
                    out=z[:], lhsT=z_codes[:, t, a, :].bitcast(FP4X4), lhsT_scale=z_planes[:, t, a * P : (a + 1) * P],
                    rhs=v_codes[h][:, a, :].bitcast(FP4X4), rhs_scale=planes[a], start=(a == 0), stop=False,
                )
            nc.tensor.matmul_mx(
                out=z[:], lhsT=z_codes[:, t, 2, :].bitcast(FP4X4), lhsT_scale=z_planes[:, t, 2 * P : 3 * P],
                rhs=v2_codes[h][:].bitcast(FP8X4), rhs_scale=v2_scales[h], start=False, stop=True,
            )
            return z

        def gate_sums(h, pair):
            return {t: gate_sum(h, t) for t in (2 * pair, 2 * pair + 1)}

        def gate_tanhs(h, sums, cols=slice(0, HALF)):
            for t in sums:
                gate_tanh(sums[t], h, t, cols)

        def sums_of(branch_sum, q):
            return {block: branch_sum(block) for block in (2 * q, 2 * q + 1)}

        def silu_of(branch_silu, sums):
            for block in sums:
                branch_silu(block, sums[block])

        def combine(q, pair):
            h, cols = q // 2, slice(q % 2 * QUARTER, (q % 2 + 1) * QUARTER)
            back = psum.tile([P, 2, QUARTER], F32, name="sums", bufs=5)
            diff = psum.tile([P, 2, QUARTER], F32, name="diff", bufs=3)
            spots = [(i, k, 2 * q + k) for i in range(2) for k in range(2)]
            for i, k, block in spots:
                nc.tensor.transpose(back[:, i, k * P : (k + 1) * P], scaled["said", block, pair][:, i, :], ident[:])
            for i, k, block in spots:
                nc.tensor.matmul(diff[:, i, k * P : (k + 1) * P], scaled["seen", block, pair][:, i, :], ident[:], start=True, stop=False, is_transpose=True)
                nc.tensor.matmul(diff[:, i, k * P : (k + 1) * P], scaled["said", block, pair][:, i, :], ident[:], start=False, stop=True, is_transpose=True)
            nc.scalar.mul(base[h, pair][:, :, cols], back[:], -2.0)
            for i in range(2):
                nc.vector.scalar_tensor_tensor(gated[h, pair][:, i, cols], th[h, pair][:, i, cols], 1.0, diff[:, i, :], ALU.add, ALU.mult)

        def first_page(t):
            both = psum.tile([P, 2, QUARTER], F32, name=("sums", "diff")[t], bufs=(5, 3)[t])
            for i, kind in enumerate(("seen", "said")):
                for k in range(2):
                    nc.tensor.transpose(both[:, i, k * P : (k + 1) * P], scaled[kind, k, 0][:, t, :], ident[:])
            tanh = th[0, 0][:, t, 0:QUARTER]
            nc.vector.scalar_tensor_tensor(gated[0, 0][:, t, 0:QUARTER], tanh, 1.0, both[:, 0, :], ALU.add, ALU.mult)
            nc.vector.scalar_tensor_tensor(base[0, 0][:, t, 0:QUARTER], tanh, -1.0, both[:, 1, :], ALU.add, ALU.mult)

        def place(t, first, count):
            h, cols = first // HALF, slice(first % HALF, first % HALF + count)
            window = pages[t][:].indirect(entries(list1, first, count))
            nc.vector.tensor_tensor(window, gated[h, t // 2][:, t % 2, cols], base[h, t // 2][:, t % 2, cols], ALU.add)

        def unit(q, pair):
            scale(q, pair)
            combine(q, pair)
            for t in (2 * pair, 2 * pair + 1):
                place(t, q * QUARTER, QUARTER)

        for block in range(blocks):
            text_silu(block, text_sum(block))
        for block in range(2):
            picture_silu(block, picture_sum(block))
        scale(0, 0)
        first_sums = {}
        for t in range(2):
            first_sums[t] = gate_sum(0, t)
            gate_tanh(first_sums[t], 0, t, slice(0, QUARTER))
        first_page(0)
        first_page(1)
        pages.append(held([P, T], F32, "page3"))
        nc.gpsimd.memset(pages[3][:], 0.0)
        place(0, 0, QUARTER)
        place(1, 0, QUARTER)
        silu_of(picture_silu, sums_of(picture_sum, 1))
        scale(1, 0)
        gate_tanhs(0, first_sums, slice(QUARTER, HALF))
        next_sums = gate_sums(0, 1)
        unit(1, 0)
        scale(0, 1)
        gate_tanhs(0, next_sums)
        next_sums = sums_of(text_sum, 2)
        unit(0, 1)
        silu_of(text_silu, next_sums)
        next_sums = sums_of(picture_sum, 2)
        scale(2, 0, ("said",))
        unit(1, 1)
        silu_of(picture_silu, next_sums)
        scale(2, 0)
        gate_tanhs(1, gate_sums(1, 0))
        next_sums = sums_of(text_sum, 3)
        combine(2, 0)
        place(0, HALF, QUARTER)
        silu_of(text_silu, next_sums)
        next_sums = sums_of(picture_sum, 3)
        scale(3, 0, ("said",))
        silu_of(picture_silu, next_sums)
        scale(3, 0)
        last_sums = gate_sums(1, 1)
        combine(3, 0)
        place(0, HALF + QUARTER, QUARTER)
        place(1, HALF, HALF)
        gate_tanhs(1, last_sums)
        for q in range(2, QUARTERS):
            scale(q, 1)
            combine(q, 1)
        for t in range(2, PACK):
            place(t, HALF, HALF)

        paired = [held([P, 2, 2, CHUNK // 2, 2], BF16, "paired%d" % c) for c in range(CHUNKS)]
        woven = [held([P, CHUNK, PACK], BF16, "woven%d" % c) for c in range(CHUNKS)]
        y_codes = [held([P, CHUNK], U32, "y_codes%d" % c) for c in range(CHUNKS)]
        y_scales = held([P, CHUNK], U8, "y_scales")
        for t in range(PACK):
            nc.sync.dma_start(out_rows[:, t, :], pages[t][:])
            for c in range(CHUNKS):
                src = pages[t][:, c * CHUNK : (c + 1) * CHUNK].rearrange("p (h c) -> p h c", h=2)
                if t >= 2 and c == 0:
                    nc.vector.tensor_copy(paired[c][:, 0, 1, :, t % 2], src[:, 0, :])
                    nc.scalar.copy(paired[c][:, 1, 1, :, t % 2], src[:, 1, :])
                else:
                    nc.scalar.copy(paired[c][:, :, t // 2, :, t % 2], src)

        def weave(c):
            engine_copy, word = (nc.scalar.copy, U32) if c == CHUNKS - 1 else (nc.vector.tensor_copy, I32)
            words = paired[c][:].rearrange("p h u c e -> p h u (c e)").bitcast(word).rearrange("p h u c -> p h c u")
            lines = woven[c][:].bitcast(word).rearrange("p (h c) u -> p h c u", h=2)
            if c in (0, CHUNKS - 1):
                for h in range(2):
                    engine_copy(lines[:, h, :, :], words[:, h, :, :])
            else:
                engine_copy(lines, words)

        def quantize(c):
            width = CHUNK // 2 if c == CHUNKS - 1 else CHUNK
            for first in range(0, CHUNK, width):
                cols = slice(first, first + width)
                nc.vector.quantize_mx(
                    out=y_codes[c][:, cols].bitcast(FP8X4), scales=y_scales[4 * c : P, cols],
                    in_=woven[c][:, cols, :].rearrange("p c t -> p (c t)"),
                )
                nc.sync.dma_start(out_words[:, c * CHUNK + first : c * CHUNK + first + width], y_codes[c][:, cols].bitcast(I32))

        weave(0)
        for c in range(CHUNKS):
            if c + 1 < CHUNKS:
                weave(c + 1)
            quantize(c)
        for q in range(4):
            rows = out_2[0, 4 * q : 4 * q + 4, :].bitcast(I32).rearrange("r (c x) -> c r x", c=CHUNKS)
            (nc.scalar, nc.sync)[q % 2].dma_start(rows, y_scales[32 * q : 32 * q + 16, :].bitcast(I32))
